import numpy as np
import ml_dtypes


def mxq(x, axis, fmt="e4m3"):
    dtype, down = {"e4m3": (ml_dtypes.float8_e4m3fn, 7), "e5m2": (ml_dtypes.float8_e5m2, 14)}[fmt]
    v = np.moveaxis(np.asarray(x, np.float32).astype(ml_dtypes.bfloat16).astype(np.float64), axis, -1)
    blocks = v.reshape(v.shape[:-1] + (-1, 32))
    amax = np.abs(blocks).max(-1, keepdims=True)
    byte = np.maximum(np.where(amax > 0, np.frexp(amax)[1] - 1 + 127, 0) - down, 1)
    scale = np.exp2(byte - 127.0)
    codes = (blocks / scale).astype(np.float32).astype(dtype).astype(np.float64)
    return np.moveaxis((codes * scale).reshape(v.shape), -1, axis)


WIDE = False


def mx_kscale(k):
    if not WIDE:
        return np.ones(k)
    levels = np.array([10, -10, 5, -5, 0])
    if k % 512:
        return np.exp2(np.random.permutation(np.resize(levels, k // 32))).repeat(32)
    a = np.empty((k // 512, 16))
    for p in range(k // 512):
        a[p, :8] = np.random.permutation(np.resize(levels, 8))
        for g in range(8):
            far = levels[np.abs(levels - a[p, g]) >= 10]
            a[p, g + 8] = far[np.random.randint(len(far))]
    return np.exp2(a.ravel()).repeat(32)


def f64(x):
    return np.asarray(x).astype(np.float64)


def striped(idx):
    return np.tile(idx.reshape(-1, 16).T, (8, 1)).astype(np.uint16)


def unstriped(offs):
    return offs[:16].T.reshape(-1).astype(np.int64)


E2M1 = np.array([0.0, 0.5, 1.0, 1.5, 2.0, 3.0, 4.0, 6.0, -0.0, -0.5, -1.0, -1.5, -2.0, -3.0, -4.0, -6.0])


def pack_weight(w, fmt):
    k, n = w.shape
    w = f64(np.asarray(w, np.float32).astype(ml_dtypes.bfloat16)).reshape(k // 32, 32, n)
    amax = np.abs(w).max(1)
    if fmt == "e4m3":
        byte = np.frexp(amax)[1] - 1 + 127 - 7
    else:
        mant, ex = np.frexp(amax / 6.0)
        byte = np.where(mant > 0.5, ex, ex - 1) + 127
    byte = np.clip(np.where(amax > 0, byte, 1), 1, 254)
    scaled = (w * np.exp2(127.0 - byte)[:, None, :]).reshape(k, n).astype(np.float32)
    by_word = np.ascontiguousarray(scaled.reshape(k // 512, 128, 4, n).transpose(0, 1, 3, 2))
    if fmt == "e4m3":
        words = by_word.astype(ml_dtypes.float8_e4m3fn).view(np.uint8)
    else:
        c = by_word.astype(ml_dtypes.float4_e2m1fn).view(np.uint8) & 0xF
        words = (c[..., 0::2] | (c[..., 1::2] << 4)).reshape(k // 512, 128, 2 * n)
    return np.ascontiguousarray(words), np.ascontiguousarray(byte.astype(np.uint8).reshape(k // 512, 16, n))


def unpack_weight(words, scales, fmt):
    g, _, n = scales.shape
    words = np.ascontiguousarray(words).reshape(g, 128, n, -1)
    if fmt == "e4m3":
        vals = words.view(ml_dtypes.float8_e4m3fn).astype(np.float64)
    else:
        nib = np.empty((g, 128, n, 4), np.uint8)
        nib[..., 0::2] = words & 0xF
        nib[..., 1::2] = words >> 4
        vals = E2M1[nib]
    vals = vals * np.repeat(np.exp2(scales.astype(np.float64) - 127.0), 8, axis=1)[..., None]
    return vals.transpose(0, 1, 3, 2).reshape(g * 512, n)


def gelu(v):
    return 0.5 * v * (1.0 + np.tanh(np.sqrt(2.0 / np.pi) * (v + 0.044715 * v**3)))


K, H, N, T, S, T2, S2 = 1024, 512, 384, 4096, 1024, 2048, 1024

def setup_inputs():
    n = np.random.standard_normal
    s = mx_kscale(K)[:, None]
    u = mx_kscale(H)[:, None]
    w = mx_kscale(S2)[:, None]
    tab_words, tab_scales = pack_weight(n((K, T)) * s, "e4m3")
    tab2_words, tab2_scales = pack_weight(n((H, T2)) / np.sqrt(H) / u, "e4m3")
    wd_words, wd_scales = pack_weight(0.6 * n((K, N)) / np.sqrt(K) / s, "e2m1")
    return {
        "tab_words": tab_words, "tab_scales": tab_scales,
        "offs": striped(np.random.permutation(T)[:S]),
        "tab2_words": tab2_words, "tab2_scales": tab2_scales,
        "offs2": striped(np.random.permutation(T2)[:S2]),
        "wq": (n((K, H)) / np.sqrt(K) / s * u.T).astype(np.float32),
        "bq": (0.5 * n(H) * u[:, 0]).astype(np.float32),
        "gain": (np.exp(0.4 * n(S2)) * w[:, 0]).astype(np.float32),
        "mix": (0.6 * n((S2, N)) / np.sqrt(S2) / w).astype(np.float32),
        "wd_words": wd_words, "wd_scales": wd_scales,
    }

def reference(tab_words, tab_scales, offs, tab2_words, tab2_scales, offs2, wq, bq, gain, mix, wd_words, wd_scales):
    v = unpack_weight(tab_words, tab_scales, "e4m3")[:, unstriped(offs)]
    v2 = unpack_weight(tab2_words, tab2_scales, "e4m3")[:, unstriped(offs2)]
    wd = unpack_weight(wd_words, wd_scales, "e2m1")
    h = (mxq(f64(wq), 0, "e4m3").T @ v) + f64(bq)[:, None]
    e = v2.T @ mxq(h, 0, "e4m3")
    z = np.abs(e) * f64(gain)[:, None]
    y = mxq(f64(mix), 0, "e4m3").T @ mxq(z, 0, "e4m3") + wd.T @ v
    return np.tanh(y)

@@ -1,0 +1,290 @@
+from contextlib import ExitStack
+
+import concourse.mybir as mybir
+
+K, H, N, T, S, T2, S2 = 1024, 512, 384, 4096, 1024, 2048, 1024
+FLOPS = 2 * S * (K * H + H * S2 + S2 * N + K * N)
+
+F32 = mybir.dt.float32
+BF16 = mybir.dt.bfloat16
+I32 = mybir.dt.int32
+U32 = mybir.dt.uint32
+U16 = mybir.dt.uint16
+U8 = mybir.dt.uint8
+FP8X4 = mybir.dt.float8_e4m3fn_x4
+FP4X4 = mybir.dt.float4_e2m1fn_x4
+ALU = mybir.AluOpType
+ACT = mybir.ActivationFunctionType
+
+P = 128
+PACK = 4
+PASSES = 2
+CHUNK = 512
+CHUNKS = S // CHUNK
+BLOCK = 128
+N_TILES = N // P
+
+
+def tile_list_tutor_progress_matching_kernel(
+    tc, tab_words, tab_scales, offs, tab2_words, tab2_scales, offs2, wq, bq, gain, mix, wd_words, wd_scales, out
+):
+    nc = tc.nc
+    with ExitStack() as ctx:
+        held = ctx.enter_context(tc.tile_pool(name="held", bufs=1))
+        ring = ctx.enter_context(tc.tile_pool(name="ring", bufs=2))
+        psum = ctx.enter_context(tc.psum_pool(name="psum", bufs=1))
+
+        def sb(shape, dtype, name, tag=None, pool=held):
+            return pool.tile(shape, dtype, name=name, tag=tag or name, align_bytes=64)
+
+        idx = held.tile([P, S // 16], U16, name="idx")
+        idx2 = held.tile([P, S2 // 16], U16, name="idx2")
+        v_scale_win = sb([P, T], U8, "v_scale_win", tag="share_a")
+        v2_word_win = sb([P, T2], I32, "v2_word_win", tag="share_b")
+        v2_scale_win = sb([P, T2], U8, "v2_scale_win", tag="share_c")
+        v_word_win = [sb([P, T], I32, "v_word_win%d" % a) for a in range(PASSES)]
+        wq_raw0 = sb([P, PACK, H], F32, "wq_raw0")
+        wq_raw1a = sb([P, PACK, H // 2], F32, "wq_raw1a")
+        v_planes = sb([P, PASSES, S], U8, "v_planes")
+        wd_planes = sb([P, PASSES, N], U8, "wd_planes")
+        bq_sb = sb([P, PACK], F32, "bq_sb")
+        gain_sb = sb([P, PASSES, PACK], F32, "gain_sb")
+        warm = sb([P, 1], F32, "warm")
+
+        nc.gpsimd.memset(v2_scale_win[:].bitcast(I32), 0)
+        nc.gpsimd.memset(wd_planes[:].bitcast(I32), 0)
+        nc.vector.memset(v_scale_win[32:64, :].bitcast(I32), 0)
+        nc.vector.memset(v_scale_win[64:128, :].bitcast(I32), 0)
+        nc.vector.memset(v_planes[:].bitcast(I32), 0)
+        nc.vector.memset(warm[:], 0.0)
+        nc.scalar.activation(out=warm[:], in_=warm[:], func=ACT.Tanh)
+
+        def words_of(table, a):
+            return table[a].rearrange("p t i -> p (t i)").bitcast(I32)
+
+        wq_view = wq.rearrange("(a p i) r -> a p i r", a=PASSES, i=PACK)
+        mix_view = mix.rearrange("(a p i) n -> a p i n", a=PASSES, i=PACK)
+
+        nc.sync.dma_start(idx[:], offs)
+        nc.sync.dma_start(v_scale_win[0:32, :].bitcast(I32), tab_scales.rearrange("a q x -> q a x").bitcast(I32))
+        nc.sync.dma_start(idx2[:], offs2)
+        nc.sync.dma_start(v2_word_win[:], words_of(tab2_words, 0))
+        for q in range(4):
+            nc.sync.dma_start(
+                v2_scale_win[32 * q : 32 * q + 4, :].bitcast(I32), tab2_scales[0, 4 * q : 4 * q + 4, :].bitcast(I32)
+            )
+        nc.sync.dma_start(v_word_win[0][:], words_of(tab_words, 0))
+        nc.sync.dma_start(wq_raw0[:], wq_view[0])
+        nc.sync.dma_start(v_word_win[1][:], words_of(tab_words, 1))
+        nc.sync.dma_start(wq_raw1a[:], wq_view[1][:, :, 0 : H // 2])
+
+        nc.gpsimd.dma_start(bq_sb[:], bq.rearrange("(p i) -> p i", i=PACK))
+        nc.gpsimd.dma_start(gain_sb[:], gain.rearrange("(a p i) -> p a i", a=PASSES, i=PACK))
+        for q in range(4):
+            nc.gpsimd.dma_start(
+                wd_planes[32 * q : 32 * q + 4, :, :].bitcast(I32),
+                wd_scales[:, 4 * q : 4 * q + 4, :].rearrange("a r c -> r a c").bitcast(I32),
+            )
+        gain_ge = sb([P, PASSES * PACK], F32, "gain_ge")
+        gain_sign = sb([P, PASSES * PACK], F32, "gain_sign")
+        gain_flat = gain_sb[:].rearrange("p a i -> p (a i)")
+        nc.gpsimd.tensor_scalar(gain_ge[:], gain_flat, 0.0, None, ALU.is_ge)
+        nc.gpsimd.tensor_scalar(gain_sign[:], gain_ge[:], 2.0, -1.0, ALU.mult, ALU.add)
+
+        v_scale_rows = sb([P, S], U8, "v_scale_rows")
+        nc.vector.tensor_copy(v_scale_rows[:], v_scale_win[:].indirect(idx[:]))
+        for q in range(4):
+            nc.sync.dma_start(
+                v_planes[32 * q : 32 * q + 4, :, :].bitcast(I32), v_scale_rows[8 * q : 8 * q + 8, :].bitcast(I32)
+            )
+        wq_raw1b = sb([P, PACK, H // 2], F32, "wq_raw1b", tag="share_a")
+        nc.sync.dma_start(wq_raw1b[:], wq_view[1][:, :, H // 2 : H])
+
+        v2_words = sb([P, S2], U32, "v2_words")
+        nc.vector.tensor_copy(
+            v2_words[:].rearrange("p (a i s) -> p a s i", a=PASSES, i=PACK),
+            v2_word_win[:].bitcast(U32).indirect(idx2[:]),
+        )
+        v2_scale_list = sb([P, S2], U8, "v2_scale_list", tag="share_d")
+        nc.vector.tensor_copy(v2_scale_list[:], v2_scale_win[:].indirect(idx2[:]))
+        v2_plane = sb([P, S2], U8, "v2_plane")
+        nc.vector.tensor_copy(
+            v2_plane[:].rearrange("p (a i s) -> p a i s", a=PASSES, i=PACK),
+            v2_scale_list[:].rearrange("p (a s i) -> p a i s", a=PASSES, i=PACK),
+        )
+        mix_raw = [sb([P, PACK, N], F32, "mix_raw0", tag="share_b"), sb([P, PACK, N], F32, "mix_raw1", tag="share_c")]
+        wd_codes = sb([P, PASSES, 2 * N], U8, "wd_codes", tag="share_d")
+        nc.sync.dma_start(wd_codes[:].bitcast(I32), wd_words.rearrange("a p c -> p a c").bitcast(I32))
+        for a in range(PASSES):
+            nc.sync.dma_start(mix_raw[a][:], mix_view[a])
+
+        v_words = [sb([P, S], U32, "v_words%d" % a) for a in range(PASSES)]
+        nc.vector.tensor_copy(v_words[0][:], v_word_win[0][:].bitcast(U32).indirect(idx[:]))
+
+        wq_bf = [sb([P, PACK, P, PACK], BF16, "wq_bf%d" % a) for a in range(PASSES)]
+        wq_codes = sb([P, PASSES, H], U32, "wq_codes")
+        wq_planes = sb([P, PASSES, H], U8, "wq_planes")
+
+        def wq_views(a, raw, m0):
+            count = raw.shape[2] // PACK
+            return (
+                wq_bf[a][:, :, m0 : m0 + count, :].rearrange("p t m i -> p m t i"),
+                raw[:].rearrange("p i (m t) -> p m t i", t=PACK),
+            )
+
+        nc.scalar.copy(*wq_views(0, wq_raw0, 0))
+        nc.vector.quantize_mx(
+            wq_codes[:, 0, :].bitcast(FP8X4), wq_planes[:, 0, :], wq_bf[0][:].rearrange("p t m i -> p (t m i)")
+        )
+        cols = CHUNK // 16
+        for c in range(CHUNKS):
+            nc.vector.tensor_copy(
+                v_words[1][:, c * CHUNK : (c + 1) * CHUNK],
+                v_word_win[1][:].bitcast(U32).indirect(idx[:, c * cols : (c + 1) * cols]),
+            )
+        nc.scalar.copy(*wq_views(1, wq_raw1a, 0))
+        nc.vector.tensor_copy(*wq_views(1, wq_raw1b, P // 2))
+        for t in range(PACK):
+            nc.vector.quantize_mx(
+                wq_codes[:, 1, t * P : (t + 1) * P].bitcast(FP8X4),
+                wq_planes[:, 1, t * P : (t + 1) * P],
+                wq_bf[1][:, t, :, :].rearrange("p m i -> p (m i)"),
+            )
+
+        def bank(name, shape, tag, bufs):
+            return psum.tile(shape, F32, name=name, tag=tag, bufs=bufs)
+
+        h_bf = [sb([P, CHUNK, PACK], BF16, "h_bf%d" % c) for c in range(CHUNKS)]
+        h_codes = [sb([P, CHUNK], U32, "h_codes%d" % c) for c in range(CHUNKS)]
+        h_planes = [sb([P, CHUNK], U8, "h_planes%d" % c) for c in range(CHUNKS)]
+
+        def h_pass(acc, a, t, j0):
+            nc.tensor.matmul_mx(
+                acc[:, t, :],
+                lhsT=wq_codes[:, a, t * P : (t + 1) * P].bitcast(FP8X4),
+                lhsT_scale=wq_planes[:, a, t * P : (t + 1) * P],
+                rhs=v_words[a][:, j0 : j0 + BLOCK].bitcast(FP8X4),
+                rhs_scale=v_planes[:, a, j0 : j0 + BLOCK],
+                start=(a == 0 and t == 0),
+                stop=(a == PASSES - 1 and t == PACK - 1),
+            )
+
+        def h_out(acc, c, b):
+            nc.vector.tensor_tensor(
+                h_bf[c][:, b * BLOCK : (b + 1) * BLOCK, :],
+                acc[:].rearrange("p t j -> p j t"),
+                bq_sb[:].unsqueeze(1).to_broadcast([P, BLOCK, PACK]),
+                ALU.add,
+            )
+
+        def h_stage(c):
+            blocks = range(CHUNK // BLOCK)
+            accs = [bank("h_acc", [P, PACK, BLOCK], "acc", 5) for b in blocks]
+            for a in range(PASSES):
+                for b in blocks:
+                    for t in range(PACK):
+                        h_pass(accs[b], a, t, c * CHUNK + b * BLOCK)
+            for b in blocks:
+                h_out(accs[b], c, b)
+            nc.vector.quantize_mx(
+                h_codes[c][:].bitcast(FP8X4), h_planes[c][:], h_bf[c][:].rearrange("p j t -> p (j t)")
+            )
+
+        def interleave(dst, src):
+            nc.vector.tensor_copy(
+                dst.rearrange("p (c i) t -> p c t i", i=4), src.rearrange("p t (c i) -> p c t i", i=4)
+            )
+
+        mix_rows = [sb([P, PACK, N], BF16, "mix_rows%d" % a) for a in range(PASSES)]
+        mix_bf = sb([P, PASSES * N, PACK], BF16, "mix_bf")
+        mix_codes = sb([P, PASSES * N], U32, "mix_codes")
+        mix_planes = sb([P, PASSES * N], U8, "mix_planes")
+
+        def mix_stage():
+            for a in range(PASSES):
+                for t in range(PACK):
+                    col = a * PACK + t
+                    nc.scalar.activation(
+                        out=mix_rows[a][:, t, :], in_=mix_raw[a][:, t, :], func=ACT.Copy,
+                        scale=gain_sign[:, col : col + 1],
+                    )
+                interleave(mix_bf[:, a * N : (a + 1) * N, :], mix_rows[a][:])
+            for lo, hi in ((0, 512), (512, PASSES * N)):
+                nc.vector.quantize_mx(
+                    mix_codes[:, lo:hi].bitcast(FP8X4),
+                    mix_planes[:, lo:hi],
+                    mix_bf[:, lo:hi, :].rearrange("p n t -> p (n t)"),
+                )
+
+        def z_stage(c, a):
+            rows = sb([P, PACK, CHUNK], BF16, "z_rows", pool=ring)
+            for t in range(PACK):
+                col = a * PACK + t
+                acc = bank("e_acc", [P, CHUNK], "acc", 5)
+                nc.tensor.matmul_mx(
+                    acc[:],
+                    lhsT=v2_words[:, col * P : (col + 1) * P].bitcast(FP8X4),
+                    lhsT_scale=v2_plane[:, col * P : (col + 1) * P],
+                    rhs=h_codes[c][:].bitcast(FP8X4),
+                    rhs_scale=h_planes[c][:],
+                    start=True,
+                    stop=True,
+                )
+                nc.scalar.activation(out=rows[:, t, :], in_=acc[:], func=ACT.Abs, scale=gain_sb[:, a, t : t + 1])
+            woven = sb([P, CHUNK, PACK], BF16, "z_bf", pool=ring)
+            interleave(woven[:], rows[:])
+            codes = sb([P, CHUNK], U32, "z_codes%d%d" % (c, a))
+            plane = sb([P, CHUNK], U8, "z_plane%d%d" % (c, a))
+            nc.vector.quantize_mx(codes[:].bitcast(FP8X4), plane[:], woven[:].rearrange("p j t -> p (j t)"))
+            return codes, plane
+
+        def y_open(c):
+            accs = [bank("y_acc", [P, CHUNK], "y", N_TILES) for n in range(N_TILES)]
+            js = slice(c * CHUNK, (c + 1) * CHUNK)
+            for n in range(N_TILES):
+                for a in range(PASSES):
+                    nc.tensor.matmul_mx(
+                        accs[n][:],
+                        lhsT=wd_codes[:, a, 2 * n * P : 2 * (n + 1) * P].bitcast(FP4X4),
+                        lhsT_scale=wd_planes[:, a, n * P : (n + 1) * P],
+                        rhs=v_words[a][:, js].bitcast(FP8X4),
+                        rhs_scale=v_planes[:, a, js],
+                        start=(a == 0),
+                        stop=False,
+                    )
+            return accs
+
+        def y_mix(accs, a, z):
+            for n in range(N_TILES):
+                cs = slice(a * N + n * P, a * N + (n + 1) * P)
+                nc.tensor.matmul_mx(
+                    accs[n][:],
+                    lhsT=mix_codes[:, cs].bitcast(FP8X4),
+                    lhsT_scale=mix_planes[:, cs],
+                    rhs=z[0][:].bitcast(FP8X4),
+                    rhs_scale=z[1][:],
+                    start=False,
+                    stop=(a == PASSES - 1),
+                )
+
+        def y_out(accs, c):
+            for n in range(N_TILES):
+                res = sb([P, CHUNK], F32, "res%d%d" % (c, n))
+                nc.scalar.activation(out=res[:], in_=accs[n][:], func=ACT.Tanh)
+                nc.sync.dma_start(out[n * P : (n + 1) * P, c * CHUNK : (c + 1) * CHUNK], res[:])
+
+        h_stage(0)
+        y0 = y_open(0)
+        mix_stage()
+        h_stage(1)
+        z00 = z_stage(0, 0)
+        z01 = z_stage(0, 1)
+        y_mix(y0, 0, z00)
+        z10 = z_stage(1, 0)
+        y_mix(y0, 1, z01)
+        z11 = z_stage(1, 1)
+        y_out(y0, 0)
+        y1 = y_open(1)
+        y_mix(y1, 0, z10)
+        y_mix(y1, 1, z11)
+        y_out(y1, 1)

@@ -31,20 +31,18 @@ def tile_list_tutor_progress_matching_kernel(
     nc = tc.nc
     with ExitStack() as ctx:
         held = ctx.enter_context(tc.tile_pool(name="held", bufs=1))
-        ring = ctx.enter_context(tc.tile_pool(name="ring", bufs=2))
         psum = ctx.enter_context(tc.psum_pool(name="psum", bufs=1))
 
-        def sb(shape, dtype, name, tag=None, pool=held):
-            return pool.tile(shape, dtype, name=name, tag=tag or name, align_bytes=64)
+        def sb(shape, dtype, name, tag=None):
+            return held.tile(shape, dtype, name=name, tag=tag or name, align_bytes=64)
 
         idx = held.tile([P, S // 16], U16, name="idx")
         idx2 = held.tile([P, S2 // 16], U16, name="idx2")
         v_scale_win = sb([P, T], U8, "v_scale_win", tag="share_a")
         v2_word_win = sb([P, T2], I32, "v2_word_win", tag="share_b")
         v2_scale_win = sb([P, T2], U8, "v2_scale_win", tag="share_c")
-        v_word_win = [sb([P, T], I32, "v_word_win%d" % a) for a in range(PASSES)]
+        v_word_win0 = sb([P, T], I32, "v_word_win0", tag="share_f")
         wq_raw0 = sb([P, PACK, H], F32, "wq_raw0")
-        wq_raw1a = sb([P, PACK, H // 2], F32, "wq_raw1a")
         v_planes = sb([P, PASSES, S], U8, "v_planes")
         wd_planes = sb([P, PASSES, N], U8, "wd_planes")
         bq_sb = sb([P, PACK], F32, "bq_sb")
@@ -73,10 +71,8 @@ def tile_list_tutor_progress_matching_kernel(
             nc.sync.dma_start(
                 v2_scale_win[32 * q : 32 * q + 4, :].bitcast(I32), tab2_scales[0, 4 * q : 4 * q + 4, :].bitcast(I32)
             )
-        nc.sync.dma_start(v_word_win[0][:], words_of(tab_words, 0))
+        nc.sync.dma_start(v_word_win0[:], words_of(tab_words, 0))
         nc.sync.dma_start(wq_raw0[:], wq_view[0])
-        nc.sync.dma_start(v_word_win[1][:], words_of(tab_words, 1))
-        nc.sync.dma_start(wq_raw1a[:], wq_view[1][:, :, 0 : H // 2])
 
         nc.gpsimd.dma_start(bq_sb[:], bq.rearrange("(p i) -> p i", i=PACK))
         nc.gpsimd.dma_start(gain_sb[:], gain.rearrange("(a p i) -> p a i", a=PASSES, i=PACK))
@@ -91,35 +87,39 @@ def tile_list_tutor_progress_matching_kernel(
         nc.gpsimd.tensor_scalar(gain_ge[:], gain_flat, 0.0, None, ALU.is_ge)
         nc.gpsimd.tensor_scalar(gain_sign[:], gain_ge[:], 2.0, -1.0, ALU.mult, ALU.add)
 
-        v_scale_rows = sb([P, S], U8, "v_scale_rows")
+        v_scale_rows = sb([P, S], U8, "v_scale_rows", tag="share_e")
         nc.vector.tensor_copy(v_scale_rows[:], v_scale_win[:].indirect(idx[:]))
         for q in range(4):
             nc.sync.dma_start(
                 v_planes[32 * q : 32 * q + 4, :, :].bitcast(I32), v_scale_rows[8 * q : 8 * q + 8, :].bitcast(I32)
             )
-        wq_raw1b = sb([P, PACK, H // 2], F32, "wq_raw1b", tag="share_a")
-        nc.sync.dma_start(wq_raw1b[:], wq_view[1][:, :, H // 2 : H])
+        v_word_win1 = sb([P, T], I32, "v_word_win1", tag="share_a")
+        nc.sync.dma_start(v_word_win1[:], words_of(tab_words, 1))
 
         v2_words = sb([P, S2], U32, "v2_words")
         nc.vector.tensor_copy(
             v2_words[:].rearrange("p (a i s) -> p a s i", a=PASSES, i=PACK),
             v2_word_win[:].bitcast(U32).indirect(idx2[:]),
         )
+        wq_raw1a = sb([P, PACK, H // 2], F32, "wq_raw1a", tag="share_b")
+        nc.sync.dma_start(wq_raw1a[:], wq_view[1][:, :, 0 : H // 2])
         v2_scale_list = sb([P, S2], U8, "v2_scale_list", tag="share_d")
         nc.vector.tensor_copy(v2_scale_list[:], v2_scale_win[:].indirect(idx2[:]))
+        wq_raw1b = sb([P, PACK, H // 2], F32, "wq_raw1b", tag="share_c")
+        nc.sync.dma_start(wq_raw1b[:], wq_view[1][:, :, H // 2 : H])
         v2_plane = sb([P, S2], U8, "v2_plane")
         nc.vector.tensor_copy(
             v2_plane[:].rearrange("p (a i s) -> p a i s", a=PASSES, i=PACK),
             v2_scale_list[:].rearrange("p (a s i) -> p a i s", a=PASSES, i=PACK),
         )
-        mix_raw = [sb([P, PACK, N], F32, "mix_raw0", tag="share_b"), sb([P, PACK, N], F32, "mix_raw1", tag="share_c")]
         wd_codes = sb([P, PASSES, 2 * N], U8, "wd_codes", tag="share_d")
         nc.sync.dma_start(wd_codes[:].bitcast(I32), wd_words.rearrange("a p c -> p a c").bitcast(I32))
-        for a in range(PASSES):
-            nc.sync.dma_start(mix_raw[a][:], mix_view[a])
 
         v_words = [sb([P, S], U32, "v_words%d" % a) for a in range(PASSES)]
-        nc.vector.tensor_copy(v_words[0][:], v_word_win[0][:].bitcast(U32).indirect(idx[:]))
+        nc.vector.tensor_copy(v_words[0][:], v_word_win0[:].bitcast(U32).indirect(idx[:]))
+        mix_raw = [sb([P, PACK, N], F32, "mix_raw0", tag="share_e"), sb([P, PACK, N], F32, "mix_raw1", tag="share_f")]
+        for a in range(PASSES):
+            nc.sync.dma_start(mix_raw[a][:], mix_view[a])
 
         wq_bf = [sb([P, PACK, P, PACK], BF16, "wq_bf%d" % a) for a in range(PASSES)]
         wq_codes = sb([P, PASSES, H], U32, "wq_codes")
@@ -140,19 +140,18 @@ def tile_list_tutor_progress_matching_kernel(
         for c in range(CHUNKS):
             nc.vector.tensor_copy(
                 v_words[1][:, c * CHUNK : (c + 1) * CHUNK],
-                v_word_win[1][:].bitcast(U32).indirect(idx[:, c * cols : (c + 1) * cols]),
+                v_word_win1[:].bitcast(U32).indirect(idx[:, c * cols : (c + 1) * cols]),
             )
         nc.scalar.copy(*wq_views(1, wq_raw1a, 0))
         nc.vector.tensor_copy(*wq_views(1, wq_raw1b, P // 2))
-        for t in range(PACK):
-            nc.vector.quantize_mx(
-                wq_codes[:, 1, t * P : (t + 1) * P].bitcast(FP8X4),
-                wq_planes[:, 1, t * P : (t + 1) * P],
-                wq_bf[1][:, t, :, :].rearrange("p m i -> p (m i)"),
-            )
+        nc.vector.quantize_mx(
+            wq_codes[:, 1, :].bitcast(FP8X4), wq_planes[:, 1, :], wq_bf[1][:].rearrange("p t m i -> p (t m i)")
+        )
 
-        def bank(name, shape, tag, bufs):
-            return psum.tile(shape, F32, name=name, tag=tag, bufs=bufs)
+        def bank(number, shape):
+            return psum.tile(shape, F32, name="bank%d" % number, tag="bank%d" % number)
+
+        E_BANKS = (0, 1, 2)
 
         h_bf = [sb([P, CHUNK, PACK], BF16, "h_bf%d" % c) for c in range(CHUNKS)]
         h_codes = [sb([P, CHUNK], U32, "h_codes%d" % c) for c in range(CHUNKS)]
@@ -177,17 +176,22 @@ def tile_list_tutor_progress_matching_kernel(
                 ALU.add,
             )
 
-        def h_stage(c):
-            blocks = range(CHUNK // BLOCK)
-            accs = [bank("h_acc", [P, PACK, BLOCK], "acc", 5) for b in blocks]
-            for a in range(PASSES):
-                for b in blocks:
-                    for t in range(PACK):
-                        h_pass(accs[b], a, t, c * CHUNK + b * BLOCK)
-            for b in blocks:
-                h_out(accs[b], c, b)
+        def h_quant(c):
             nc.vector.quantize_mx(
                 h_codes[c][:].bitcast(FP8X4), h_planes[c][:], h_bf[c][:].rearrange("p j t -> p (j t)")
+            )
+
+        h_rows = sb([P, PACK, CHUNK], BF16, "h_rows")
+
+        def h_wide_pass(acc, a, t):
+            nc.tensor.matmul_mx(
+                acc[:],
+                lhsT=wq_codes[:, a, t * P : (t + 1) * P].bitcast(FP8X4),
+                lhsT_scale=wq_planes[:, a, t * P : (t + 1) * P],
+                rhs=v_words[a][:, CHUNK:S].bitcast(FP8X4),
+                rhs_scale=v_planes[:, a, CHUNK:S],
+                start=(a == 0),
+                stop=(a == PASSES - 1),
             )
 
         def interleave(dst, src):
@@ -200,27 +204,32 @@ def tile_list_tutor_progress_matching_kernel(
         mix_codes = sb([P, PASSES * N], U32, "mix_codes")
         mix_planes = sb([P, PASSES * N], U8, "mix_planes")
 
-        def mix_stage():
-            for a in range(PASSES):
-                for t in range(PACK):
-                    col = a * PACK + t
-                    nc.scalar.activation(
-                        out=mix_rows[a][:, t, :], in_=mix_raw[a][:, t, :], func=ACT.Copy,
-                        scale=gain_sign[:, col : col + 1],
-                    )
-                interleave(mix_bf[:, a * N : (a + 1) * N, :], mix_rows[a][:])
-            for lo, hi in ((0, 512), (512, PASSES * N)):
-                nc.vector.quantize_mx(
-                    mix_codes[:, lo:hi].bitcast(FP8X4),
-                    mix_planes[:, lo:hi],
-                    mix_bf[:, lo:hi, :].rearrange("p n t -> p (n t)"),
-                )
-
-        def z_stage(c, a):
-            rows = sb([P, PACK, CHUNK], BF16, "z_rows", pool=ring)
+        def mix_sign(a):
             for t in range(PACK):
                 col = a * PACK + t
-                acc = bank("e_acc", [P, CHUNK], "acc", 5)
+                nc.gpsimd.tensor_scalar(
+                    mix_rows[a][:, t, :], mix_raw[a][:, t, :], gain_sign[:, col : col + 1], 0.0, ALU.mult, ALU.add
+                )
+
+        def mix_weave(a):
+            interleave(mix_bf[:, a * N : (a + 1) * N, :], mix_rows[a][:])
+
+        def mix_quant(lo, hi):
+            nc.vector.quantize_mx(
+                mix_codes[:, lo:hi].bitcast(FP8X4),
+                mix_planes[:, lo:hi],
+                mix_bf[:, lo:hi, :].rearrange("p n t -> p (n t)"),
+            )
+
+        z_rows = [[sb([P, PACK, CHUNK], BF16, "z_rows%d%d" % (c, a)) for a in range(PASSES)] for c in range(CHUNKS)]
+        z_bf = [[sb([P, CHUNK, PACK], BF16, "z_bf%d%d" % (c, a)) for a in range(PASSES)] for c in range(CHUNKS)]
+        z_codes = [[sb([P, CHUNK], U32, "z_codes%d%d" % (c, a)) for a in range(PASSES)] for c in range(CHUNKS)]
+        z_planes = [[sb([P, CHUNK], U8, "z_planes%d%d" % (c, a)) for a in range(PASSES)] for c in range(CHUNKS)]
+
+        def e_stage(c, a):
+            for t in range(PACK):
+                col = a * PACK + t
+                acc = bank(E_BANKS[(c * PASSES * PACK + col) % len(E_BANKS)], [P, CHUNK])
                 nc.tensor.matmul_mx(
                     acc[:],
                     lhsT=v2_words[:, col * P : (col + 1) * P].bitcast(FP8X4),
@@ -230,61 +239,127 @@ def tile_list_tutor_progress_matching_kernel(
                     start=True,
                     stop=True,
                 )
-                nc.scalar.activation(out=rows[:, t, :], in_=acc[:], func=ACT.Abs, scale=gain_sb[:, a, t : t + 1])
-            woven = sb([P, CHUNK, PACK], BF16, "z_bf", pool=ring)
-            interleave(woven[:], rows[:])
-            codes = sb([P, CHUNK], U32, "z_codes%d%d" % (c, a))
-            plane = sb([P, CHUNK], U8, "z_plane%d%d" % (c, a))
-            nc.vector.quantize_mx(codes[:].bitcast(FP8X4), plane[:], woven[:].rearrange("p j t -> p (j t)"))
-            return codes, plane
-
-        def y_open(c):
-            accs = [bank("y_acc", [P, CHUNK], "y", N_TILES) for n in range(N_TILES)]
-            js = slice(c * CHUNK, (c + 1) * CHUNK)
-            for n in range(N_TILES):
-                for a in range(PASSES):
-                    nc.tensor.matmul_mx(
-                        accs[n][:],
-                        lhsT=wd_codes[:, a, 2 * n * P : 2 * (n + 1) * P].bitcast(FP4X4),
-                        lhsT_scale=wd_planes[:, a, n * P : (n + 1) * P],
-                        rhs=v_words[a][:, js].bitcast(FP8X4),
-                        rhs_scale=v_planes[:, a, js],
-                        start=(a == 0),
-                        stop=False,
-                    )
-            return accs
-
-        def y_mix(accs, a, z):
-            for n in range(N_TILES):
-                cs = slice(a * N + n * P, a * N + (n + 1) * P)
-                nc.tensor.matmul_mx(
-                    accs[n][:],
-                    lhsT=mix_codes[:, cs].bitcast(FP8X4),
-                    lhsT_scale=mix_planes[:, cs],
-                    rhs=z[0][:].bitcast(FP8X4),
-                    rhs_scale=z[1][:],
-                    start=False,
-                    stop=(a == PASSES - 1),
+                nc.scalar.activation(
+                    out=z_rows[c][a][:, t, :], in_=acc[:], func=ACT.Abs, scale=gain_sb[:, a, t : t + 1]
                 )
 
-        def y_out(accs, c):
-            for n in range(N_TILES):
-                res = sb([P, CHUNK], F32, "res%d%d" % (c, n))
-                nc.scalar.activation(out=res[:], in_=accs[n][:], func=ACT.Tanh)
-                nc.sync.dma_start(out[n * P : (n + 1) * P, c * CHUNK : (c + 1) * CHUNK], res[:])
+        def z_weave(c, a, lo=0, hi=CHUNK):
+            interleave(z_bf[c][a][:, lo:hi, :], z_rows[c][a][:, :, lo:hi])
 
-        h_stage(0)
-        y0 = y_open(0)
-        mix_stage()
-        h_stage(1)
-        z00 = z_stage(0, 0)
-        z01 = z_stage(0, 1)
-        y_mix(y0, 0, z00)
-        z10 = z_stage(1, 0)
-        y_mix(y0, 1, z01)
-        z11 = z_stage(1, 1)
-        y_out(y0, 0)
-        y1 = y_open(1)
-        y_mix(y1, 0, z10)
-        y_mix(y1, 1, z11)
-        y_out(y1, 1)
+        def z_quant(c, a, lo=0, hi=CHUNK):
+            nc.vector.quantize_mx(
+                z_codes[c][a][:, lo:hi].bitcast(FP8X4),
+                z_planes[c][a][:, lo:hi],
+                z_bf[c][a][:, lo:hi, :].rearrange("p j t -> p (j t)"),
+            )
+
+        def y_open(c, lo, hi, groups):
+            width = hi - lo
+            step = CHUNK if width == CHUNK else BLOCK
+            piece = []
+            for number, tiles in groups:
+                acc = bank(number, [P, len(tiles), width])
+                first = True
+                for k, n in enumerate(tiles):
+                    for a in range(PASSES):
+                        for j in range(0, width, step):
+                            js = slice(c * CHUNK + lo + j, c * CHUNK + lo + j + step)
+                            nc.tensor.matmul_mx(
+                                acc[:, k, j : j + step],
+                                lhsT=wd_codes[:, a, 2 * n * P : 2 * (n + 1) * P].bitcast(FP4X4),
+                                lhsT_scale=wd_planes[:, a, n * P : (n + 1) * P],
+                                rhs=v_words[a][:, js].bitcast(FP8X4),
+                                rhs_scale=v_planes[:, a, js],
+                                start=first,
+                                stop=False,
+                            )
+                            first = False
+                piece.append((acc, tiles))
+            return c, lo, hi, piece
+
+        def y_mix(y, a):
+            c, lo, hi, piece = y
+            for acc, tiles in piece:
+                for k, n in enumerate(tiles):
+                    cs = slice(a * N + n * P, a * N + (n + 1) * P)
+                    nc.tensor.matmul_mx(
+                        acc[:, k, :],
+                        lhsT=mix_codes[:, cs].bitcast(FP8X4),
+                        lhsT_scale=mix_planes[:, cs],
+                        rhs=z_codes[c][a][:, lo:hi].bitcast(FP8X4),
+                        rhs_scale=z_planes[c][a][:, lo:hi],
+                        start=False,
+                        stop=(a == PASSES - 1 and k == len(tiles) - 1),
+                    )
+
+        out_view = out.rearrange("(n p) j -> p n j", p=P)
+
+        def y_out(y):
+            c, lo, hi, piece = y
+            for acc, tiles in piece:
+                res = sb([P, len(tiles), hi - lo], F32, "res%d_%d_%d" % (c, lo, tiles[0]))
+                nc.scalar.activation(out=res[:], in_=acc[:], func=ACT.Tanh)
+                nc.sync.dma_start(
+                    out_view[:, tiles[0] : tiles[-1] + 1, c * CHUNK + lo : c * CHUNK + hi], res[:]
+                )
+
+        blocks = range(CHUNK // BLOCK)
+        narrow = [bank(b, [P, PACK, BLOCK]) for b in blocks]
+        wide = [bank(4 + t, [P, CHUNK]) for t in range(PACK)]
+        for t in range(PACK):
+            h_wide_pass(wide[t], 0, t)
+        for b in blocks:
+            for t in range(PACK):
+                h_pass(narrow[b], 0, t, b * BLOCK)
+        for b in blocks:
+            for t in range(PACK):
+                h_pass(narrow[b], 1, t, b * BLOCK)
+            if b > 0:
+                h_wide_pass(wide[b - 1], 1, b - 1)
+        h_wide_pass(wide[PACK - 1], 1, PACK - 1)
+        for b in blocks:
+            h_out(narrow[b], 0, b)
+            nc.scalar.activation(out=h_rows[:, b, :], in_=wide[b][:], func=ACT.Identity, bias=bq_sb[:, b : b + 1])
+        h_quant(0)
+        mix_sign(0)
+        mix_sign(1)
+        e_stage(0, 0)
+        y0 = y_open(0, 0, CHUNK, ((3, (0,)), (4, (1,)), (5, (2,))))
+        interleave(h_bf[1][:], h_rows[:])
+        mix_weave(0)
+        h_quant(1)
+        e_stage(0, 1)
+        z_weave(0, 0)
+        mix_weave(1)
+        mix_quant(0, 512)
+        mix_quant(512, PASSES * N)
+        e_stage(1, 0)
+        z_weave(0, 1)
+        z_quant(0, 0)
+        y_mix(y0, 0)
+        y1a = y_open(1, 0, 256, ((6, (0, 1)), (7, (2,))))
+        e_stage(1, 1)
+        y1b = y_open(1, 256, 384, ((1, (0, 1, 2)),))
+        y1c = y_open(1, 384, 512, ((2, (0, 1, 2)),))
+        z_weave(1, 0, 0, 256)
+        z_quant(0, 1)
+        y_mix(y0, 1)
+        y_out(y0)
+        z_weave(1, 1, 0, 256)
+        z_quant(1, 0, 0, 256)
+        y_mix(y1a, 0)
+        z_weave(1, 0, 256, 512)
+        z_quant(1, 1, 0, 256)
+        y_mix(y1a, 1)
+        y_out(y1a)
+        z_weave(1, 1, 256, 384)
+        z_quant(1, 0, 256, 512)
+        y_mix(y1b, 0)
+        y_mix(y1c, 0)
+        z_weave(1, 1, 384, 512)
+        z_quant(1, 1, 256, 384)
+        y_mix(y1b, 1)
+        y_out(y1b)
+        z_quant(1, 1, 384, 512)
+        y_mix(y1c, 1)
+        y_out(y1c)

@@ -74,8 +74,8 @@ def tile_list_tutor_progress_matching_kernel(
         nc.sync.dma_start(v_word_win0[:], words_of(tab_words, 0))
         nc.sync.dma_start(wq_raw0[:], wq_view[0])
 
-        nc.gpsimd.dma_start(bq_sb[:], bq.rearrange("(p i) -> p i", i=PACK))
-        nc.gpsimd.dma_start(gain_sb[:], gain.rearrange("(a p i) -> p a i", a=PASSES, i=PACK))
+        nc.sync.dma_start(bq_sb[:], bq.rearrange("(p i) -> p i", i=PACK))
+        nc.sync.dma_start(gain_sb[:], gain.rearrange("(a p i) -> p a i", a=PASSES, i=PACK))
         for q in range(4):
             nc.gpsimd.dma_start(
                 wd_planes[32 * q : 32 * q + 4, :, :].bitcast(I32),
@@ -112,14 +112,14 @@ def tile_list_tutor_progress_matching_kernel(
             v2_plane[:].rearrange("p (a i s) -> p a i s", a=PASSES, i=PACK),
             v2_scale_list[:].rearrange("p (a s i) -> p a i s", a=PASSES, i=PACK),
         )
-        wd_codes = sb([P, PASSES, 2 * N], U8, "wd_codes", tag="share_d")
-        nc.sync.dma_start(wd_codes[:].bitcast(I32), wd_words.rearrange("a p c -> p a c").bitcast(I32))
+        mix_raw = [sb([P, PACK, N], F32, "mix_raw0", tag="share_d"), sb([P, PACK, N], F32, "mix_raw1", tag="share_e")]
+        for a in range(PASSES):
+            nc.sync.dma_start(mix_raw[a][:], mix_view[a])
 
         v_words = [sb([P, S], U32, "v_words%d" % a) for a in range(PASSES)]
         nc.vector.tensor_copy(v_words[0][:], v_word_win0[:].bitcast(U32).indirect(idx[:]))
-        mix_raw = [sb([P, PACK, N], F32, "mix_raw0", tag="share_e"), sb([P, PACK, N], F32, "mix_raw1", tag="share_f")]
-        for a in range(PASSES):
-            nc.sync.dma_start(mix_raw[a][:], mix_view[a])
+        wd_codes = sb([P, PASSES, 2 * N], U8, "wd_codes", tag="share_f")
+        nc.sync.dma_start(wd_codes[:].bitcast(I32), wd_words.rearrange("a p c -> p a c").bitcast(I32))
 
         wq_bf = [sb([P, PACK, P, PACK], BF16, "wq_bf%d" % a) for a in range(PASSES)]
         wq_codes = sb([P, PASSES, H], U32, "wq_codes")
@@ -181,19 +181,6 @@ def tile_list_tutor_progress_matching_kernel(
                 h_codes[c][:].bitcast(FP8X4), h_planes[c][:], h_bf[c][:].rearrange("p j t -> p (j t)")
             )
 
-        h_rows = sb([P, PACK, CHUNK], BF16, "h_rows")
-
-        def h_wide_pass(acc, a, t):
-            nc.tensor.matmul_mx(
-                acc[:],
-                lhsT=wq_codes[:, a, t * P : (t + 1) * P].bitcast(FP8X4),
-                lhsT_scale=wq_planes[:, a, t * P : (t + 1) * P],
-                rhs=v_words[a][:, CHUNK:S].bitcast(FP8X4),
-                rhs_scale=v_planes[:, a, CHUNK:S],
-                start=(a == 0),
-                stop=(a == PASSES - 1),
-            )
-
         def interleave(dst, src):
             nc.vector.tensor_copy(
                 dst.rearrange("p (c i) t -> p c t i", i=4), src.rearrange("p t (c i) -> p c t i", i=4)
@@ -207,8 +194,9 @@ def tile_list_tutor_progress_matching_kernel(
         def mix_sign(a):
             for t in range(PACK):
                 col = a * PACK + t
-                nc.gpsimd.tensor_scalar(
-                    mix_rows[a][:, t, :], mix_raw[a][:, t, :], gain_sign[:, col : col + 1], 0.0, ALU.mult, ALU.add
+                nc.scalar.activation(
+                    out=mix_rows[a][:, t, :], in_=mix_raw[a][:, t, :], func=ACT.Copy,
+                    scale=gain_sign[:, col : col + 1],
                 )
 
         def mix_weave(a):
@@ -303,31 +291,21 @@ def tile_list_tutor_progress_matching_kernel(
                     out_view[:, tiles[0] : tiles[-1] + 1, c * CHUNK + lo : c * CHUNK + hi], res[:]
                 )
 
-        blocks = range(CHUNK // BLOCK)
-        narrow = [bank(b, [P, PACK, BLOCK]) for b in blocks]
-        wide = [bank(4 + t, [P, CHUNK]) for t in range(PACK)]
-        for t in range(PACK):
-            h_wide_pass(wide[t], 0, t)
-        for b in blocks:
-            for t in range(PACK):
-                h_pass(narrow[b], 0, t, b * BLOCK)
-        for b in blocks:
-            for t in range(PACK):
-                h_pass(narrow[b], 1, t, b * BLOCK)
-            if b > 0:
-                h_wide_pass(wide[b - 1], 1, b - 1)
-        h_wide_pass(wide[PACK - 1], 1, PACK - 1)
-        for b in blocks:
-            h_out(narrow[b], 0, b)
-            nc.scalar.activation(out=h_rows[:, b, :], in_=wide[b][:], func=ACT.Identity, bias=bq_sb[:, b : b + 1])
-        h_quant(0)
+        per_chunk = CHUNK // BLOCK
+        h_accs = [bank(b, [P, PACK, BLOCK]) for b in range(S // BLOCK)]
+        for a in range(PASSES):
+            for b in range(S // BLOCK):
+                for t in range(PACK):
+                    h_pass(h_accs[b], a, t, b * BLOCK)
+        for c in range(CHUNKS):
+            for b in range(per_chunk):
+                h_out(h_accs[c * per_chunk + b], c, b)
+            h_quant(c)
         mix_sign(0)
         mix_sign(1)
         e_stage(0, 0)
         y0 = y_open(0, 0, CHUNK, ((3, (0,)), (4, (1,)), (5, (2,))))
-        interleave(h_bf[1][:], h_rows[:])
         mix_weave(0)
-        h_quant(1)
         e_stage(0, 1)
         z_weave(0, 0)
         mix_weave(1)

@@ -42,15 +42,11 @@ def tile_list_tutor_progress_matching_kernel(
         v2_word_win = sb([P, T2], I32, "v2_word_win", tag="share_b")
         v2_scale_win = sb([P, T2], U8, "v2_scale_win", tag="share_c")
         v_word_win0 = sb([P, T], I32, "v_word_win0", tag="share_f")
-        wq_raw0 = sb([P, PACK, H], F32, "wq_raw0")
+        wq_raw0 = sb([P, PACK, H], F32, "wq_raw0", tag="share_g")
         v_planes = sb([P, PASSES, S], U8, "v_planes")
-        wd_planes = sb([P, PASSES, N], U8, "wd_planes")
-        bq_sb = sb([P, PACK], F32, "bq_sb")
-        gain_sb = sb([P, PASSES, PACK], F32, "gain_sb")
         warm = sb([P, 1], F32, "warm")
 
         nc.gpsimd.memset(v2_scale_win[:].bitcast(I32), 0)
-        nc.gpsimd.memset(wd_planes[:].bitcast(I32), 0)
         nc.vector.memset(v_scale_win[32:64, :].bitcast(I32), 0)
         nc.vector.memset(v_scale_win[64:128, :].bitcast(I32), 0)
         nc.vector.memset(v_planes[:].bitcast(I32), 0)
@@ -74,18 +70,6 @@ def tile_list_tutor_progress_matching_kernel(
         nc.sync.dma_start(v_word_win0[:], words_of(tab_words, 0))
         nc.sync.dma_start(wq_raw0[:], wq_view[0])
 
-        nc.sync.dma_start(bq_sb[:], bq.rearrange("(p i) -> p i", i=PACK))
-        nc.sync.dma_start(gain_sb[:], gain.rearrange("(a p i) -> p a i", a=PASSES, i=PACK))
-        for q in range(4):
-            nc.gpsimd.dma_start(
-                wd_planes[32 * q : 32 * q + 4, :, :].bitcast(I32),
-                wd_scales[:, 4 * q : 4 * q + 4, :].rearrange("a r c -> r a c").bitcast(I32),
-            )
-        gain_ge = sb([P, PASSES * PACK], F32, "gain_ge")
-        gain_sign = sb([P, PASSES * PACK], F32, "gain_sign")
-        gain_flat = gain_sb[:].rearrange("p a i -> p (a i)")
-        nc.gpsimd.tensor_scalar(gain_ge[:], gain_flat, 0.0, None, ALU.is_ge)
-        nc.gpsimd.tensor_scalar(gain_sign[:], gain_ge[:], 2.0, -1.0, ALU.mult, ALU.add)
 
         v_scale_rows = sb([P, S], U8, "v_scale_rows", tag="share_e")
         nc.vector.tensor_copy(v_scale_rows[:], v_scale_win[:].indirect(idx[:]))
@@ -105,8 +89,15 @@ def tile_list_tutor_progress_matching_kernel(
         nc.sync.dma_start(wq_raw1a[:], wq_view[1][:, :, 0 : H // 2])
         v2_scale_list = sb([P, S2], U8, "v2_scale_list", tag="share_d")
         nc.vector.tensor_copy(v2_scale_list[:], v2_scale_win[:].indirect(idx2[:]))
-        wq_raw1b = sb([P, PACK, H // 2], F32, "wq_raw1b", tag="share_c")
-        nc.sync.dma_start(wq_raw1b[:], wq_view[1][:, :, H // 2 : H])
+        late = sb([P, 2 * H + 16], F32, "late", tag="share_c")
+        wq_raw1b = late[:, 0 : 2 * H].rearrange("p (i r) -> p i r", i=PACK)
+        bq_sb = late[:, 2 * H : 2 * H + PACK]
+        gain_sb = late[:, 2 * H + 8 : 2 * H + 16]
+        nc.sync.dma_start(wq_raw1b, wq_view[1][:, :, H // 2 : H])
+        nc.sync.dma_start(bq_sb, bq.rearrange("(p i) -> p i", i=PACK))
+        nc.sync.dma_start(
+            gain_sb.rearrange("p (a i) -> p a i", i=PACK), gain.rearrange("(a p i) -> p a i", a=PASSES, i=PACK)
+        )
         v2_plane = sb([P, S2], U8, "v2_plane")
         nc.vector.tensor_copy(
             v2_plane[:].rearrange("p (a i s) -> p a i s", a=PASSES, i=PACK),
@@ -129,24 +120,36 @@ def tile_list_tutor_progress_matching_kernel(
             count = raw.shape[2] // PACK
             return (
                 wq_bf[a][:, :, m0 : m0 + count, :].rearrange("p t m i -> p m t i"),
-                raw[:].rearrange("p i (m t) -> p m t i", t=PACK),
+                raw.rearrange("p i (m t) -> p m t i", t=PACK),
             )
 
-        nc.scalar.copy(*wq_views(0, wq_raw0, 0))
+        nc.scalar.copy(*wq_views(0, wq_raw0[:], 0))
         nc.vector.quantize_mx(
             wq_codes[:, 0, :].bitcast(FP8X4), wq_planes[:, 0, :], wq_bf[0][:].rearrange("p t m i -> p (t m i)")
         )
+        wd_planes = sb([P, PASSES, N], U8, "wd_planes", tag="share_g")
+        nc.vector.memset(wd_planes[:].bitcast(I32), 0)
+        for q in range(4):
+            nc.sync.dma_start(
+                wd_planes[32 * q : 32 * q + 4, :, :].bitcast(I32),
+                wd_scales[:, 4 * q : 4 * q + 4, :].rearrange("a r c -> r a c").bitcast(I32),
+            )
         cols = CHUNK // 16
         for c in range(CHUNKS):
             nc.vector.tensor_copy(
                 v_words[1][:, c * CHUNK : (c + 1) * CHUNK],
                 v_word_win1[:].bitcast(U32).indirect(idx[:, c * cols : (c + 1) * cols]),
             )
-        nc.scalar.copy(*wq_views(1, wq_raw1a, 0))
+        nc.scalar.copy(*wq_views(1, wq_raw1a[:], 0))
         nc.vector.tensor_copy(*wq_views(1, wq_raw1b, P // 2))
         nc.vector.quantize_mx(
             wq_codes[:, 1, :].bitcast(FP8X4), wq_planes[:, 1, :], wq_bf[1][:].rearrange("p t m i -> p (t m i)")
         )
+
+        gain_ge = sb([P, PASSES * PACK], F32, "gain_ge")
+        gain_sign = sb([P, PASSES * PACK], F32, "gain_sign")
+        nc.scalar.activation(out=gain_ge[:], in_=gain_sb, func=ACT.Sign)
+        nc.scalar.activation(out=gain_sign[:], in_=gain_ge[:], func=ACT.Sign, scale=2.0, bias=1.0)
 
         def bank(number, shape):
             return psum.tile(shape, F32, name="bank%d" % number, tag="bank%d" % number)
@@ -170,9 +173,9 @@ def tile_list_tutor_progress_matching_kernel(
 
         def h_out(acc, c, b):
             nc.vector.tensor_tensor(
-                h_bf[c][:, b * BLOCK : (b + 1) * BLOCK, :],
-                acc[:].rearrange("p t j -> p j t"),
-                bq_sb[:].unsqueeze(1).to_broadcast([P, BLOCK, PACK]),
+                h_bf[c][:, b * BLOCK : (b + 1) * BLOCK, :].rearrange("p (j i) t -> p j t i", i=2),
+                acc[:].rearrange("p t (j i) -> p j t i", i=2),
+                bq_sb.unsqueeze(1).unsqueeze(3).to_broadcast([P, BLOCK // 2, PACK, 2]),
                 ALU.add,
             )
 
@@ -228,7 +231,7 @@ def tile_list_tutor_progress_matching_kernel(
                     stop=True,
                 )
                 nc.scalar.activation(
-                    out=z_rows[c][a][:, t, :], in_=acc[:], func=ACT.Abs, scale=gain_sb[:, a, t : t + 1]
+                    out=z_rows[c][a][:, t, :], in_=acc[:], func=ACT.Abs, scale=gain_sb[:, col : col + 1]
                 )
 
         def z_weave(c, a, lo=0, hi=CHUNK):

@@ -19,10 +19,13 @@ ACT = mybir.ActivationFunctionType
 P = 128
 PACK = 4
 PASSES = 2
+QUADS = 4
+QUAD = P // QUADS
+LIST_ROWS = 16
 CHUNK = 512
 CHUNKS = S // CHUNK
 BLOCK = 128
-N_TILES = N // P
+E_BANKS = (0, 1, 2)
 
 
 def tile_list_tutor_progress_matching_kernel(
@@ -36,48 +39,56 @@ def tile_list_tutor_progress_matching_kernel(
         def sb(shape, dtype, name, tag=None):
             return held.tile(shape, dtype, name=name, tag=tag or name, align_bytes=64)
 
-        idx = held.tile([P, S // 16], U16, name="idx")
-        idx2 = held.tile([P, S2 // 16], U16, name="idx2")
-        v_scale_win = sb([P, T], U8, "v_scale_win", tag="share_a")
-        v2_word_win = sb([P, T2], I32, "v2_word_win", tag="share_b")
-        v2_scale_win = sb([P, T2], U8, "v2_scale_win", tag="share_c")
-        v_word_win0 = sb([P, T], I32, "v_word_win0", tag="share_f")
-        wq_raw0 = sb([P, PACK, H], F32, "wq_raw0", tag="share_g")
-        v_planes = sb([P, PASSES, S], U8, "v_planes")
-        warm = sb([P, 1], F32, "warm")
-
-        nc.gpsimd.memset(v2_scale_win[:].bitcast(I32), 0)
-        nc.vector.memset(v_scale_win[32:64, :].bitcast(I32), 0)
-        nc.vector.memset(v_scale_win[64:128, :].bitcast(I32), 0)
-        nc.vector.memset(v_planes[:].bitcast(I32), 0)
-        nc.vector.memset(warm[:], 0.0)
-        nc.scalar.activation(out=warm[:], in_=warm[:], func=ACT.Tanh)
+        def bank(number, shape):
+            return psum.tile(shape, F32, name="bank%d" % number, tag="bank%d" % number)
 
         def words_of(table, a):
             return table[a].rearrange("p t i -> p (t i)").bitcast(I32)
+
+        def quantise(codes, plane, woven):
+            nc.vector.quantize_mx(codes.bitcast(FP8X4), plane, woven.rearrange("p c t -> p (c t)"))
+
+        def weave(woven, slices):
+            nc.vector.tensor_copy(
+                woven.rearrange("p (c i) t -> p c t i", i=4), slices.rearrange("p t (c i) -> p c t i", i=4)
+            )
+
+        idx = held.tile([P, S // LIST_ROWS], U16, name="idx")
+        idx2 = held.tile([P, S2 // LIST_ROWS], U16, name="idx2")
+        v_scale_win = sb([P, T], U8, "v_scale_win", tag="reuse_a")
+        v2_word_win = sb([P, T2], I32, "v2_word_win", tag="reuse_b")
+        v2_scale_win = sb([P, T2], U8, "v2_scale_win", tag="reuse_c")
+        v_word_win0 = sb([P, T], I32, "v_word_win0", tag="reuse_f")
+        wq_raw0 = sb([P, PACK, H], F32, "wq_raw0", tag="reuse_g")
+        v_planes = sb([P, PASSES, S], U8, "v_planes")
+
+        nc.gpsimd.memset(v2_scale_win[:].bitcast(I32), 0)
+        nc.vector.memset(v_scale_win[QUAD : 2 * QUAD, :].bitcast(I32), 0)
+        nc.vector.memset(v_scale_win[2 * QUAD : P, :].bitcast(I32), 0)
+        nc.vector.memset(v_planes[:].bitcast(I32), 0)
 
         wq_view = wq.rearrange("(a p i) r -> a p i r", a=PASSES, i=PACK)
         mix_view = mix.rearrange("(a p i) n -> a p i n", a=PASSES, i=PACK)
 
         nc.sync.dma_start(idx[:], offs)
-        nc.sync.dma_start(v_scale_win[0:32, :].bitcast(I32), tab_scales.rearrange("a q x -> q a x").bitcast(I32))
+        nc.sync.dma_start(v_scale_win[0:QUAD, :].bitcast(I32), tab_scales.rearrange("a q x -> q a x").bitcast(I32))
         nc.sync.dma_start(idx2[:], offs2)
         nc.sync.dma_start(v2_word_win[:], words_of(tab2_words, 0))
-        for q in range(4):
+        for q in range(QUADS):
             nc.sync.dma_start(
-                v2_scale_win[32 * q : 32 * q + 4, :].bitcast(I32), tab2_scales[0, 4 * q : 4 * q + 4, :].bitcast(I32)
+                v2_scale_win[QUAD * q : QUAD * q + 4, :].bitcast(I32),
+                tab2_scales[0, 4 * q : 4 * q + 4, :].bitcast(I32),
             )
         nc.sync.dma_start(v_word_win0[:], words_of(tab_words, 0))
         nc.sync.dma_start(wq_raw0[:], wq_view[0])
 
-
-        v_scale_rows = sb([P, S], U8, "v_scale_rows", tag="share_e")
+        v_scale_rows = sb([P, S], U8, "v_scale_rows", tag="reuse_e")
         nc.vector.tensor_copy(v_scale_rows[:], v_scale_win[:].indirect(idx[:]))
-        for q in range(4):
+        for q in range(QUADS):
             nc.sync.dma_start(
-                v_planes[32 * q : 32 * q + 4, :, :].bitcast(I32), v_scale_rows[8 * q : 8 * q + 8, :].bitcast(I32)
+                v_planes[QUAD * q : QUAD * q + 4, :, :].bitcast(I32), v_scale_rows[8 * q : 8 * q + 8, :].bitcast(I32)
             )
-        v_word_win1 = sb([P, T], I32, "v_word_win1", tag="share_a")
+        v_word_win1 = sb([P, T], I32, "v_word_win1", tag="reuse_a")
         nc.sync.dma_start(v_word_win1[:], words_of(tab_words, 1))
 
         v2_words = sb([P, S2], U32, "v2_words")
@@ -85,15 +96,16 @@ def tile_list_tutor_progress_matching_kernel(
             v2_words[:].rearrange("p (a i s) -> p a s i", a=PASSES, i=PACK),
             v2_word_win[:].bitcast(U32).indirect(idx2[:]),
         )
-        wq_raw1a = sb([P, PACK, H // 2], F32, "wq_raw1a", tag="share_b")
-        nc.sync.dma_start(wq_raw1a[:], wq_view[1][:, :, 0 : H // 2])
-        v2_scale_list = sb([P, S2], U8, "v2_scale_list", tag="share_d")
+        wq_raw1_low = sb([P, PACK, H // 2], F32, "wq_raw1_low", tag="reuse_b")
+        nc.sync.dma_start(wq_raw1_low[:], wq_view[1][:, :, 0 : H // 2])
+        v2_scale_list = sb([P, S2], U8, "v2_scale_list", tag="reuse_d")
         nc.vector.tensor_copy(v2_scale_list[:], v2_scale_win[:].indirect(idx2[:]))
-        late = sb([P, 2 * H + 16], F32, "late", tag="share_c")
-        wq_raw1b = late[:, 0 : 2 * H].rearrange("p (i r) -> p i r", i=PACK)
+
+        late = sb([P, 2 * H + 16], F32, "late", tag="reuse_c")
+        wq_raw1_high = late[:, 0 : 2 * H].rearrange("p (i r) -> p i r", i=PACK)
         bq_sb = late[:, 2 * H : 2 * H + PACK]
         gain_sb = late[:, 2 * H + 8 : 2 * H + 16]
-        nc.sync.dma_start(wq_raw1b, wq_view[1][:, :, H // 2 : H])
+        nc.sync.dma_start(wq_raw1_high, wq_view[1][:, :, H // 2 : H])
         nc.sync.dma_start(bq_sb, bq.rearrange("(p i) -> p i", i=PACK))
         nc.sync.dma_start(
             gain_sb.rearrange("p (a i) -> p a i", i=PACK), gain.rearrange("(a p i) -> p a i", a=PASSES, i=PACK)
@@ -103,244 +115,200 @@ def tile_list_tutor_progress_matching_kernel(
             v2_plane[:].rearrange("p (a i s) -> p a i s", a=PASSES, i=PACK),
             v2_scale_list[:].rearrange("p (a s i) -> p a i s", a=PASSES, i=PACK),
         )
-        mix_raw = [sb([P, PACK, N], F32, "mix_raw0", tag="share_d"), sb([P, PACK, N], F32, "mix_raw1", tag="share_e")]
+        mix_raw = [sb([P, PACK, N], F32, "mix_raw0", tag="reuse_d"), sb([P, PACK, N], F32, "mix_raw1", tag="reuse_e")]
         for a in range(PASSES):
             nc.sync.dma_start(mix_raw[a][:], mix_view[a])
 
         v_words = [sb([P, S], U32, "v_words%d" % a) for a in range(PASSES)]
         nc.vector.tensor_copy(v_words[0][:], v_word_win0[:].bitcast(U32).indirect(idx[:]))
-        wd_codes = sb([P, PASSES, 2 * N], U8, "wd_codes", tag="share_f")
+        wd_codes = sb([P, PASSES, 2 * N], U8, "wd_codes", tag="reuse_f")
         nc.sync.dma_start(wd_codes[:].bitcast(I32), wd_words.rearrange("a p c -> p a c").bitcast(I32))
 
         wq_bf = [sb([P, PACK, P, PACK], BF16, "wq_bf%d" % a) for a in range(PASSES)]
         wq_codes = sb([P, PASSES, H], U32, "wq_codes")
         wq_planes = sb([P, PASSES, H], U8, "wq_planes")
 
-        def wq_views(a, raw, m0):
+        def wq_views(a, raw, s0):
             count = raw.shape[2] // PACK
             return (
-                wq_bf[a][:, :, m0 : m0 + count, :].rearrange("p t m i -> p m t i"),
-                raw.rearrange("p i (m t) -> p m t i", t=PACK),
+                wq_bf[a][:, :, s0 : s0 + count, :].rearrange("p t s i -> p s t i"),
+                raw.rearrange("p i (s t) -> p s t i", t=PACK),
             )
 
+        def wq_quantise(a):
+            quantise(wq_codes[:, a, :], wq_planes[:, a, :], wq_bf[a][:].rearrange("p t s i -> p (t s) i"))
+
         nc.scalar.copy(*wq_views(0, wq_raw0[:], 0))
-        nc.vector.quantize_mx(
-            wq_codes[:, 0, :].bitcast(FP8X4), wq_planes[:, 0, :], wq_bf[0][:].rearrange("p t m i -> p (t m i)")
-        )
-        wd_planes = sb([P, PASSES, N], U8, "wd_planes", tag="share_g")
+        wq_quantise(0)
+        wd_planes = sb([P, PASSES, N], U8, "wd_planes", tag="reuse_g")
         nc.vector.memset(wd_planes[:].bitcast(I32), 0)
-        for q in range(4):
+        for q in range(QUADS):
             nc.sync.dma_start(
-                wd_planes[32 * q : 32 * q + 4, :, :].bitcast(I32),
+                wd_planes[QUAD * q : QUAD * q + 4, :, :].bitcast(I32),
                 wd_scales[:, 4 * q : 4 * q + 4, :].rearrange("a r c -> r a c").bitcast(I32),
             )
-        cols = CHUNK // 16
+        list_cols = CHUNK // LIST_ROWS
         for c in range(CHUNKS):
             nc.vector.tensor_copy(
                 v_words[1][:, c * CHUNK : (c + 1) * CHUNK],
-                v_word_win1[:].bitcast(U32).indirect(idx[:, c * cols : (c + 1) * cols]),
+                v_word_win1[:].bitcast(U32).indirect(idx[:, c * list_cols : (c + 1) * list_cols]),
             )
-        nc.scalar.copy(*wq_views(1, wq_raw1a[:], 0))
-        nc.vector.tensor_copy(*wq_views(1, wq_raw1b, P // 2))
-        nc.vector.quantize_mx(
-            wq_codes[:, 1, :].bitcast(FP8X4), wq_planes[:, 1, :], wq_bf[1][:].rearrange("p t m i -> p (t m i)")
-        )
+        nc.scalar.copy(*wq_views(1, wq_raw1_low[:], 0))
+        nc.vector.tensor_copy(*wq_views(1, wq_raw1_high, P // 2))
+        wq_quantise(1)
 
-        gain_ge = sb([P, PASSES * PACK], F32, "gain_ge")
+        gain_sign0 = sb([P, PASSES * PACK], F32, "gain_sign0")
         gain_sign = sb([P, PASSES * PACK], F32, "gain_sign")
-        nc.scalar.activation(out=gain_ge[:], in_=gain_sb, func=ACT.Sign)
-        nc.scalar.activation(out=gain_sign[:], in_=gain_ge[:], func=ACT.Sign, scale=2.0, bias=1.0)
-
-        def bank(number, shape):
-            return psum.tile(shape, F32, name="bank%d" % number, tag="bank%d" % number)
-
-        E_BANKS = (0, 1, 2)
+        nc.scalar.activation(out=gain_sign0[:], in_=gain_sb, func=ACT.Sign)
+        nc.scalar.activation(out=gain_sign[:], in_=gain_sign0[:], func=ACT.Sign, scale=2.0, bias=1.0)
 
         h_bf = [sb([P, CHUNK, PACK], BF16, "h_bf%d" % c) for c in range(CHUNKS)]
         h_codes = [sb([P, CHUNK], U32, "h_codes%d" % c) for c in range(CHUNKS)]
         h_planes = [sb([P, CHUNK], U8, "h_planes%d" % c) for c in range(CHUNKS)]
-
-        def h_pass(acc, a, t, j0):
-            nc.tensor.matmul_mx(
-                acc[:, t, :],
-                lhsT=wq_codes[:, a, t * P : (t + 1) * P].bitcast(FP8X4),
-                lhsT_scale=wq_planes[:, a, t * P : (t + 1) * P],
-                rhs=v_words[a][:, j0 : j0 + BLOCK].bitcast(FP8X4),
-                rhs_scale=v_planes[:, a, j0 : j0 + BLOCK],
-                start=(a == 0 and t == 0),
-                stop=(a == PASSES - 1 and t == PACK - 1),
-            )
-
-        def h_out(acc, c, b):
-            nc.vector.tensor_tensor(
-                h_bf[c][:, b * BLOCK : (b + 1) * BLOCK, :].rearrange("p (j i) t -> p j t i", i=2),
-                acc[:].rearrange("p t (j i) -> p j t i", i=2),
-                bq_sb.unsqueeze(1).unsqueeze(3).to_broadcast([P, BLOCK // 2, PACK, 2]),
-                ALU.add,
-            )
-
-        def h_quant(c):
-            nc.vector.quantize_mx(
-                h_codes[c][:].bitcast(FP8X4), h_planes[c][:], h_bf[c][:].rearrange("p j t -> p (j t)")
-            )
-
-        def interleave(dst, src):
-            nc.vector.tensor_copy(
-                dst.rearrange("p (c i) t -> p c t i", i=4), src.rearrange("p t (c i) -> p c t i", i=4)
-            )
+        h_accs = [bank(b, [P, PACK, BLOCK]) for b in range(S // BLOCK)]
+        for a in range(PASSES):
+            for b in range(S // BLOCK):
+                for t in range(PACK):
+                    nc.tensor.matmul_mx(
+                        h_accs[b][:, t, :],
+                        lhsT=wq_codes[:, a, t * P : (t + 1) * P].bitcast(FP8X4),
+                        lhsT_scale=wq_planes[:, a, t * P : (t + 1) * P],
+                        rhs=v_words[a][:, b * BLOCK : (b + 1) * BLOCK].bitcast(FP8X4),
+                        rhs_scale=v_planes[:, a, b * BLOCK : (b + 1) * BLOCK],
+                        start=(a == 0 and t == 0),
+                        stop=(a == PASSES - 1 and t == PACK - 1),
+                    )
+        per_chunk = CHUNK // BLOCK
+        for c in range(CHUNKS):
+            for b in range(per_chunk):
+                nc.vector.tensor_tensor(
+                    h_bf[c][:, b * BLOCK : (b + 1) * BLOCK, :].rearrange("p (j i) t -> p j t i", i=2),
+                    h_accs[c * per_chunk + b][:].rearrange("p t (j i) -> p j t i", i=2),
+                    bq_sb.unsqueeze(1).unsqueeze(3).to_broadcast([P, BLOCK // 2, PACK, 2]),
+                    ALU.add,
+                )
+            quantise(h_codes[c][:], h_planes[c][:], h_bf[c][:])
 
         mix_rows = [sb([P, PACK, N], BF16, "mix_rows%d" % a) for a in range(PASSES)]
         mix_bf = sb([P, PASSES * N, PACK], BF16, "mix_bf")
         mix_codes = sb([P, PASSES * N], U32, "mix_codes")
         mix_planes = sb([P, PASSES * N], U8, "mix_planes")
-
-        def mix_sign(a):
+        for a in range(PASSES):
             for t in range(PACK):
                 col = a * PACK + t
                 nc.scalar.activation(
-                    out=mix_rows[a][:, t, :], in_=mix_raw[a][:, t, :], func=ACT.Copy,
-                    scale=gain_sign[:, col : col + 1],
+                    out=mix_rows[a][:, t, :], in_=mix_raw[a][:, t, :], func=ACT.Copy, scale=gain_sign[:, col : col + 1]
                 )
 
         def mix_weave(a):
-            interleave(mix_bf[:, a * N : (a + 1) * N, :], mix_rows[a][:])
-
-        def mix_quant(lo, hi):
-            nc.vector.quantize_mx(
-                mix_codes[:, lo:hi].bitcast(FP8X4),
-                mix_planes[:, lo:hi],
-                mix_bf[:, lo:hi, :].rearrange("p n t -> p (n t)"),
-            )
+            weave(mix_bf[:, a * N : (a + 1) * N, :], mix_rows[a][:])
 
         z_rows = [[sb([P, PACK, CHUNK], BF16, "z_rows%d%d" % (c, a)) for a in range(PASSES)] for c in range(CHUNKS)]
         z_bf = [[sb([P, CHUNK, PACK], BF16, "z_bf%d%d" % (c, a)) for a in range(PASSES)] for c in range(CHUNKS)]
         z_codes = [[sb([P, CHUNK], U32, "z_codes%d%d" % (c, a)) for a in range(PASSES)] for c in range(CHUNKS)]
         z_planes = [[sb([P, CHUNK], U8, "z_planes%d%d" % (c, a)) for a in range(PASSES)] for c in range(CHUNKS)]
+        for c in range(CHUNKS):
+            for a in range(PASSES):
+                for t in range(PACK):
+                    col = a * PACK + t
+                    acc = bank(E_BANKS[(c * PASSES * PACK + col) % len(E_BANKS)], [P, CHUNK])
+                    nc.tensor.matmul_mx(
+                        acc[:],
+                        lhsT=v2_words[:, col * P : (col + 1) * P].bitcast(FP8X4),
+                        lhsT_scale=v2_plane[:, col * P : (col + 1) * P],
+                        rhs=h_codes[c][:].bitcast(FP8X4),
+                        rhs_scale=h_planes[c][:],
+                        start=True,
+                        stop=True,
+                    )
+                    nc.scalar.activation(
+                        out=z_rows[c][a][:, t, :], in_=acc[:], func=ACT.Abs, scale=gain_sb[:, col : col + 1]
+                    )
 
-        def e_stage(c, a):
-            for t in range(PACK):
-                col = a * PACK + t
-                acc = bank(E_BANKS[(c * PASSES * PACK + col) % len(E_BANKS)], [P, CHUNK])
-                nc.tensor.matmul_mx(
-                    acc[:],
-                    lhsT=v2_words[:, col * P : (col + 1) * P].bitcast(FP8X4),
-                    lhsT_scale=v2_plane[:, col * P : (col + 1) * P],
-                    rhs=h_codes[c][:].bitcast(FP8X4),
-                    rhs_scale=h_planes[c][:],
-                    start=True,
-                    stop=True,
-                )
-                nc.scalar.activation(
-                    out=z_rows[c][a][:, t, :], in_=acc[:], func=ACT.Abs, scale=gain_sb[:, col : col + 1]
-                )
+        def z_weave(c, a, lo, hi):
+            weave(z_bf[c][a][:, lo:hi, :], z_rows[c][a][:, :, lo:hi])
 
-        def z_weave(c, a, lo=0, hi=CHUNK):
-            interleave(z_bf[c][a][:, lo:hi, :], z_rows[c][a][:, :, lo:hi])
-
-        def z_quant(c, a, lo=0, hi=CHUNK):
-            nc.vector.quantize_mx(
-                z_codes[c][a][:, lo:hi].bitcast(FP8X4),
-                z_planes[c][a][:, lo:hi],
-                z_bf[c][a][:, lo:hi, :].rearrange("p j t -> p (j t)"),
-            )
+        def z_quantise(c, a, lo, hi):
+            quantise(z_codes[c][a][:, lo:hi], z_planes[c][a][:, lo:hi], z_bf[c][a][:, lo:hi, :])
 
         def y_open(c, lo, hi, groups):
             width = hi - lo
             step = CHUNK if width == CHUNK else BLOCK
-            piece = []
+            accs = []
             for number, tiles in groups:
                 acc = bank(number, [P, len(tiles), width])
-                first = True
-                for k, n in enumerate(tiles):
+                for place, n in enumerate(tiles):
                     for a in range(PASSES):
                         for j in range(0, width, step):
                             js = slice(c * CHUNK + lo + j, c * CHUNK + lo + j + step)
                             nc.tensor.matmul_mx(
-                                acc[:, k, j : j + step],
+                                acc[:, place, j : j + step],
                                 lhsT=wd_codes[:, a, 2 * n * P : 2 * (n + 1) * P].bitcast(FP4X4),
                                 lhsT_scale=wd_planes[:, a, n * P : (n + 1) * P],
                                 rhs=v_words[a][:, js].bitcast(FP8X4),
                                 rhs_scale=v_planes[:, a, js],
-                                start=first,
+                                start=(place == 0 and a == 0 and j == 0),
                                 stop=False,
                             )
-                            first = False
-                piece.append((acc, tiles))
-            return c, lo, hi, piece
+                accs.append((acc, tiles))
+            return c, lo, hi, accs
 
-        def y_mix(y, a):
-            c, lo, hi, piece = y
-            for acc, tiles in piece:
-                for k, n in enumerate(tiles):
-                    cs = slice(a * N + n * P, a * N + (n + 1) * P)
+        def y_mix(piece, a):
+            c, lo, hi, accs = piece
+            for acc, tiles in accs:
+                for place, n in enumerate(tiles):
+                    ns = slice(a * N + n * P, a * N + (n + 1) * P)
                     nc.tensor.matmul_mx(
-                        acc[:, k, :],
-                        lhsT=mix_codes[:, cs].bitcast(FP8X4),
-                        lhsT_scale=mix_planes[:, cs],
+                        acc[:, place, :],
+                        lhsT=mix_codes[:, ns].bitcast(FP8X4),
+                        lhsT_scale=mix_planes[:, ns],
                         rhs=z_codes[c][a][:, lo:hi].bitcast(FP8X4),
                         rhs_scale=z_planes[c][a][:, lo:hi],
                         start=False,
-                        stop=(a == PASSES - 1 and k == len(tiles) - 1),
+                        stop=(a == PASSES - 1 and place == len(tiles) - 1),
                     )
 
         out_view = out.rearrange("(n p) j -> p n j", p=P)
 
-        def y_out(y):
-            c, lo, hi, piece = y
-            for acc, tiles in piece:
+        def y_out(piece):
+            c, lo, hi, accs = piece
+            for acc, tiles in accs:
                 res = sb([P, len(tiles), hi - lo], F32, "res%d_%d_%d" % (c, lo, tiles[0]))
                 nc.scalar.activation(out=res[:], in_=acc[:], func=ACT.Tanh)
-                nc.sync.dma_start(
-                    out_view[:, tiles[0] : tiles[-1] + 1, c * CHUNK + lo : c * CHUNK + hi], res[:]
-                )
+                nc.sync.dma_start(out_view[:, tiles[0] : tiles[-1] + 1, c * CHUNK + lo : c * CHUNK + hi], res[:])
 
-        per_chunk = CHUNK // BLOCK
-        h_accs = [bank(b, [P, PACK, BLOCK]) for b in range(S // BLOCK)]
-        for a in range(PASSES):
-            for b in range(S // BLOCK):
-                for t in range(PACK):
-                    h_pass(h_accs[b], a, t, b * BLOCK)
-        for c in range(CHUNKS):
-            for b in range(per_chunk):
-                h_out(h_accs[c * per_chunk + b], c, b)
-            h_quant(c)
-        mix_sign(0)
-        mix_sign(1)
-        e_stage(0, 0)
-        y0 = y_open(0, 0, CHUNK, ((3, (0,)), (4, (1,)), (5, (2,))))
+        half, three_quarters = CHUNK // 2, 3 * CHUNK // 4
+        first = y_open(0, 0, CHUNK, ((3, (0,)), (4, (1,)), (5, (2,))))
         mix_weave(0)
-        e_stage(0, 1)
-        z_weave(0, 0)
+        z_weave(0, 0, 0, CHUNK)
         mix_weave(1)
-        mix_quant(0, 512)
-        mix_quant(512, PASSES * N)
-        e_stage(1, 0)
-        z_weave(0, 1)
-        z_quant(0, 0)
-        y_mix(y0, 0)
-        y1a = y_open(1, 0, 256, ((6, (0, 1)), (7, (2,))))
-        e_stage(1, 1)
-        y1b = y_open(1, 256, 384, ((1, (0, 1, 2)),))
-        y1c = y_open(1, 384, 512, ((2, (0, 1, 2)),))
-        z_weave(1, 0, 0, 256)
-        z_quant(0, 1)
-        y_mix(y0, 1)
-        y_out(y0)
-        z_weave(1, 1, 0, 256)
-        z_quant(1, 0, 0, 256)
-        y_mix(y1a, 0)
-        z_weave(1, 0, 256, 512)
-        z_quant(1, 1, 0, 256)
-        y_mix(y1a, 1)
-        y_out(y1a)
-        z_weave(1, 1, 256, 384)
-        z_quant(1, 0, 256, 512)
-        y_mix(y1b, 0)
-        y_mix(y1c, 0)
-        z_weave(1, 1, 384, 512)
-        z_quant(1, 1, 256, 384)
-        y_mix(y1b, 1)
-        y_out(y1b)
-        z_quant(1, 1, 384, 512)
-        y_mix(y1c, 1)
-        y_out(y1c)
+        for lo, hi in ((0, CHUNK), (CHUNK, PASSES * N)):
+            quantise(mix_codes[:, lo:hi], mix_planes[:, lo:hi], mix_bf[:, lo:hi, :])
+        z_weave(0, 1, 0, CHUNK)
+        z_quantise(0, 0, 0, CHUNK)
+        y_mix(first, 0)
+        second = y_open(1, 0, half, ((6, (0, 1)), (7, (2,))))
+        third = y_open(1, half, three_quarters, ((1, (0, 1, 2)),))
+        fourth = y_open(1, three_quarters, CHUNK, ((2, (0, 1, 2)),))
+        z_weave(1, 0, 0, half)
+        z_quantise(0, 1, 0, CHUNK)
+        y_mix(first, 1)
+        y_out(first)
+        z_weave(1, 1, 0, half)
+        z_quantise(1, 0, 0, half)
+        y_mix(second, 0)
+        z_weave(1, 0, half, CHUNK)
+        z_quantise(1, 1, 0, half)
+        y_mix(second, 1)
+        y_out(second)
+        z_weave(1, 1, half, three_quarters)
+        z_quantise(1, 0, half, CHUNK)
+        y_mix(third, 0)
+        y_mix(fourth, 0)
+        z_weave(1, 1, three_quarters, CHUNK)
+        z_quantise(1, 1, half, three_quarters)
+        y_mix(third, 1)
+        y_out(third)
+        z_quantise(1, 1, three_quarters, CHUNK)
+        y_mix(fourth, 1)
+        y_out(fourth)

@@ -66,6 +66,8 @@ def tile_list_tutor_progress_matching_kernel(
         nc.vector.memset(v_scale_win[QUAD : 2 * QUAD, :].bitcast(I32), 0)
         nc.vector.memset(v_scale_win[2 * QUAD : P, :].bitcast(I32), 0)
         nc.vector.memset(v_planes[:].bitcast(I32), 0)
+        v2_plane = sb([P, S2], U8, "v2_plane")
+        nc.vector.memset(v2_plane[:].bitcast(I32), 0)
 
         wq_view = wq.rearrange("(a p i) r -> a p i r", a=PASSES, i=PACK)
         mix_view = mix.rearrange("(a p i) n -> a p i n", a=PASSES, i=PACK)
@@ -74,15 +76,11 @@ def tile_list_tutor_progress_matching_kernel(
         nc.sync.dma_start(v_scale_win[0:QUAD, :].bitcast(I32), tab_scales.rearrange("a q x -> q a x").bitcast(I32))
         nc.sync.dma_start(idx2[:], offs2)
         nc.sync.dma_start(v2_word_win[:], words_of(tab2_words, 0))
-        for q in range(QUADS):
-            nc.sync.dma_start(
-                v2_scale_win[QUAD * q : QUAD * q + 4, :].bitcast(I32),
-                tab2_scales[0, 4 * q : 4 * q + 4, :].bitcast(I32),
-            )
+        nc.sync.dma_start(v2_scale_win[0:P:8, :].bitcast(I32), tab2_scales[0].bitcast(I32))
         nc.sync.dma_start(v_word_win0[:], words_of(tab_words, 0))
         nc.sync.dma_start(wq_raw0[:], wq_view[0])
 
-        v_scale_rows = sb([P, S], U8, "v_scale_rows", tag="reuse_e")
+        v_scale_rows = sb([P, S], U8, "v_scale_rows")
         nc.vector.tensor_copy(v_scale_rows[:], v_scale_win[:].indirect(idx[:]))
         for q in range(QUADS):
             nc.sync.dma_start(
@@ -110,14 +108,19 @@ def tile_list_tutor_progress_matching_kernel(
         nc.sync.dma_start(
             gain_sb.rearrange("p (a i) -> p a i", i=PACK), gain.rearrange("(a p i) -> p a i", a=PASSES, i=PACK)
         )
-        v2_plane = sb([P, S2], U8, "v2_plane")
+        v2_scale_rows = sb([P, S2], U8, "v2_scale_rows")
         nc.vector.tensor_copy(
-            v2_plane[:].rearrange("p (a i s) -> p a i s", a=PASSES, i=PACK),
+            v2_scale_rows[:].rearrange("p (a i s) -> p a i s", a=PASSES, i=PACK),
             v2_scale_list[:].rearrange("p (a s i) -> p a i s", a=PASSES, i=PACK),
         )
-        mix_raw = [sb([P, PACK, N], F32, "mix_raw0", tag="reuse_d"), sb([P, PACK, N], F32, "mix_raw1", tag="reuse_e")]
+        mix_raw = sb([P, PASSES, PACK, N], F32, "mix_raw", tag="reuse_d")
         for a in range(PASSES):
-            nc.sync.dma_start(mix_raw[a][:], mix_view[a])
+            nc.sync.dma_start(mix_raw[:, a, :, :], mix_view[a])
+        for q in range(QUADS):
+            nc.sync.dma_start(
+                v2_plane[QUAD * q : QUAD * q + 4, :].bitcast(I32),
+                v2_scale_rows[QUAD * q : QUAD * (q + 1) : 8, :].bitcast(I32),
+            )
 
         v_words = [sb([P, S], U32, "v_words%d" % a) for a in range(PASSES)]
         nc.vector.tensor_copy(v_words[0][:], v_word_win0[:].bitcast(U32).indirect(idx[:]))
@@ -197,7 +200,7 @@ def tile_list_tutor_progress_matching_kernel(
             for t in range(PACK):
                 col = a * PACK + t
                 nc.scalar.activation(
-                    out=mix_rows[a][:, t, :], in_=mix_raw[a][:, t, :], func=ACT.Copy, scale=gain_sign[:, col : col + 1]
+                    out=mix_rows[a][:, t, :], in_=mix_raw[:, a, t, :], func=ACT.Copy, scale=gain_sign[:, col : col + 1]
                 )
 
         def mix_weave(a):

@@ -25,6 +25,7 @@ LIST_ROWS = 16
 CHUNK = 512
 CHUNKS = S // CHUNK
 BLOCK = 128
+WQ_SPLIT = 44
 E_BANKS = (0, 1, 2)
 
 
@@ -66,8 +67,6 @@ def tile_list_tutor_progress_matching_kernel(
         nc.vector.memset(v_scale_win[QUAD : 2 * QUAD, :].bitcast(I32), 0)
         nc.vector.memset(v_scale_win[2 * QUAD : P, :].bitcast(I32), 0)
         nc.vector.memset(v_planes[:].bitcast(I32), 0)
-        v2_plane = sb([P, S2], U8, "v2_plane")
-        nc.vector.memset(v2_plane[:].bitcast(I32), 0)
 
         wq_view = wq.rearrange("(a p i) r -> a p i r", a=PASSES, i=PACK)
         mix_view = mix.rearrange("(a p i) n -> a p i n", a=PASSES, i=PACK)
@@ -76,7 +75,11 @@ def tile_list_tutor_progress_matching_kernel(
         nc.sync.dma_start(v_scale_win[0:QUAD, :].bitcast(I32), tab_scales.rearrange("a q x -> q a x").bitcast(I32))
         nc.sync.dma_start(idx2[:], offs2)
         nc.sync.dma_start(v2_word_win[:], words_of(tab2_words, 0))
-        nc.sync.dma_start(v2_scale_win[0:P:8, :].bitcast(I32), tab2_scales[0].bitcast(I32))
+        for q in range(QUADS):
+            nc.sync.dma_start(
+                v2_scale_win[QUAD * q : QUAD * q + 4, :].bitcast(I32),
+                tab2_scales[0, 4 * q : 4 * q + 4, :].bitcast(I32),
+            )
         nc.sync.dma_start(v_word_win0[:], words_of(tab_words, 0))
         nc.sync.dma_start(wq_raw0[:], wq_view[0])
 
@@ -84,7 +87,8 @@ def tile_list_tutor_progress_matching_kernel(
         nc.vector.tensor_copy(v_scale_rows[:], v_scale_win[:].indirect(idx[:]))
         for q in range(QUADS):
             nc.sync.dma_start(
-                v_planes[QUAD * q : QUAD * q + 4, :, :].bitcast(I32), v_scale_rows[8 * q : 8 * q + 8, :].bitcast(I32)
+                v_planes[QUAD * q : QUAD * q + 4, :, :].bitcast(I32),
+                v_scale_rows[8 * q : 8 * q + 8, :].bitcast(I32),
             )
         v_word_win1 = sb([P, T], I32, "v_word_win1", tag="reuse_a")
         nc.sync.dma_start(v_word_win1[:], words_of(tab_words, 1))
@@ -94,33 +98,26 @@ def tile_list_tutor_progress_matching_kernel(
             v2_words[:].rearrange("p (a i s) -> p a s i", a=PASSES, i=PACK),
             v2_word_win[:].bitcast(U32).indirect(idx2[:]),
         )
-        wq_raw1_low = sb([P, PACK, H // 2], F32, "wq_raw1_low", tag="reuse_b")
-        nc.sync.dma_start(wq_raw1_low[:], wq_view[1][:, :, 0 : H // 2])
+        wq_raw1 = sb([P, PACK, H], F32, "wq_raw1", tag="reuse_b")
+        nc.sync.dma_start(wq_raw1[:], wq_view[1])
         v2_scale_list = sb([P, S2], U8, "v2_scale_list", tag="reuse_d")
         nc.vector.tensor_copy(v2_scale_list[:], v2_scale_win[:].indirect(idx2[:]))
 
-        late = sb([P, 2 * H + 16], F32, "late", tag="reuse_c")
-        wq_raw1_high = late[:, 0 : 2 * H].rearrange("p (i r) -> p i r", i=PACK)
-        bq_sb = late[:, 2 * H : 2 * H + PACK]
-        gain_sb = late[:, 2 * H + 8 : 2 * H + 16]
-        nc.sync.dma_start(wq_raw1_high, wq_view[1][:, :, H // 2 : H])
+        late = sb([P, 16], F32, "late", tag="reuse_c")
+        bq_sb = late[:, 0:PACK]
+        gain_sb = late[:, 8:16]
         nc.sync.dma_start(bq_sb, bq.rearrange("(p i) -> p i", i=PACK))
         nc.sync.dma_start(
             gain_sb.rearrange("p (a i) -> p a i", i=PACK), gain.rearrange("(a p i) -> p a i", a=PASSES, i=PACK)
         )
-        v2_scale_rows = sb([P, S2], U8, "v2_scale_rows")
+        v2_plane = sb([P, S2], U8, "v2_plane")
         nc.vector.tensor_copy(
-            v2_scale_rows[:].rearrange("p (a i s) -> p a i s", a=PASSES, i=PACK),
+            v2_plane[:].rearrange("p (a i s) -> p a i s", a=PASSES, i=PACK),
             v2_scale_list[:].rearrange("p (a s i) -> p a i s", a=PASSES, i=PACK),
         )
         mix_raw = sb([P, PASSES, PACK, N], F32, "mix_raw", tag="reuse_d")
         for a in range(PASSES):
             nc.sync.dma_start(mix_raw[:, a, :, :], mix_view[a])
-        for q in range(QUADS):
-            nc.sync.dma_start(
-                v2_plane[QUAD * q : QUAD * q + 4, :].bitcast(I32),
-                v2_scale_rows[QUAD * q : QUAD * (q + 1) : 8, :].bitcast(I32),
-            )
 
         v_words = [sb([P, S], U32, "v_words%d" % a) for a in range(PASSES)]
         nc.vector.tensor_copy(v_words[0][:], v_word_win0[:].bitcast(U32).indirect(idx[:]))
@@ -134,15 +131,17 @@ def tile_list_tutor_progress_matching_kernel(
         def wq_views(a, raw, s0):
             count = raw.shape[2] // PACK
             return (
-                wq_bf[a][:, :, s0 : s0 + count, :].rearrange("p t s i -> p s t i"),
-                raw.rearrange("p i (s t) -> p s t i", t=PACK),
+                wq_bf[a][:, :, s0 : s0 + count, :].rearrange("p t s i -> p s i t"),
+                raw.rearrange("p i (s t) -> p s i t", t=PACK),
             )
 
-        def wq_quantise(a):
-            quantise(wq_codes[:, a, :], wq_planes[:, a, :], wq_bf[a][:].rearrange("p t s i -> p (t s) i"))
+        def wq_quantise(a, t0, t1):
+            cols = slice(t0 * P, t1 * P)
+            woven = wq_bf[a][:, t0:t1, :, :].rearrange("p t s i -> p (t s) i")
+            quantise(wq_codes[:, a, cols], wq_planes[:, a, cols], woven)
 
         nc.scalar.copy(*wq_views(0, wq_raw0[:], 0))
-        wq_quantise(0)
+        wq_quantise(0, 0, PACK)
         wd_planes = sb([P, PASSES, N], U8, "wd_planes", tag="reuse_g")
         nc.vector.memset(wd_planes[:].bitcast(I32), 0)
         for q in range(QUADS):
@@ -156,9 +155,10 @@ def tile_list_tutor_progress_matching_kernel(
                 v_words[1][:, c * CHUNK : (c + 1) * CHUNK],
                 v_word_win1[:].bitcast(U32).indirect(idx[:, c * list_cols : (c + 1) * list_cols]),
             )
-        nc.scalar.copy(*wq_views(1, wq_raw1_low[:], 0))
-        nc.vector.tensor_copy(*wq_views(1, wq_raw1_high, P // 2))
-        wq_quantise(1)
+        nc.scalar.copy(*wq_views(1, wq_raw1[:, :, 0 : PACK * WQ_SPLIT], 0))
+        nc.vector.tensor_copy(*wq_views(1, wq_raw1[:, :, PACK * WQ_SPLIT : H], WQ_SPLIT))
+        wq_quantise(1, 0, PACK // 2)
+        wq_quantise(1, PACK // 2, PACK)
 
         gain_sign0 = sb([P, PASSES * PACK], F32, "gain_sign0")
         gain_sign = sb([P, PASSES * PACK], F32, "gain_sign")
@@ -169,8 +169,11 @@ def tile_list_tutor_progress_matching_kernel(
         h_codes = [sb([P, CHUNK], U32, "h_codes%d" % c) for c in range(CHUNKS)]
         h_planes = [sb([P, CHUNK], U8, "h_planes%d" % c) for c in range(CHUNKS)]
         h_accs = [bank(b, [P, PACK, BLOCK]) for b in range(S // BLOCK)]
-        for a in range(PASSES):
-            for b in range(S // BLOCK):
+        per_chunk = CHUNK // BLOCK
+        half = CHUNK // 2
+
+        def h_passes(a, blocks):
+            for b in blocks:
                 for t in range(PACK):
                     nc.tensor.matmul_mx(
                         h_accs[b][:, t, :],
@@ -181,16 +184,19 @@ def tile_list_tutor_progress_matching_kernel(
                         start=(a == 0 and t == 0),
                         stop=(a == PASSES - 1 and t == PACK - 1),
                     )
-        per_chunk = CHUNK // BLOCK
-        for c in range(CHUNKS):
-            for b in range(per_chunk):
+
+        def h_empty(blocks):
+            for b in blocks:
+                c, lo = b // per_chunk, (b % per_chunk) * BLOCK
                 nc.vector.tensor_tensor(
-                    h_bf[c][:, b * BLOCK : (b + 1) * BLOCK, :].rearrange("p (j i) t -> p j t i", i=2),
-                    h_accs[c * per_chunk + b][:].rearrange("p t (j i) -> p j t i", i=2),
+                    h_bf[c][:, lo : lo + BLOCK, :].rearrange("p (j i) t -> p j t i", i=2),
+                    h_accs[b][:].rearrange("p t (j i) -> p j t i", i=2),
                     bq_sb.unsqueeze(1).unsqueeze(3).to_broadcast([P, BLOCK // 2, PACK, 2]),
                     ALU.add,
                 )
-            quantise(h_codes[c][:], h_planes[c][:], h_bf[c][:])
+
+        def h_quantise(c, lo, hi):
+            quantise(h_codes[c][:, lo:hi], h_planes[c][:, lo:hi], h_bf[c][:, lo:hi, :])
 
         mix_rows = [sb([P, PACK, N], BF16, "mix_rows%d" % a) for a in range(PASSES)]
         mix_bf = sb([P, PASSES * N, PACK], BF16, "mix_bf")
@@ -210,23 +216,46 @@ def tile_list_tutor_progress_matching_kernel(
         z_bf = [[sb([P, CHUNK, PACK], BF16, "z_bf%d%d" % (c, a)) for a in range(PASSES)] for c in range(CHUNKS)]
         z_codes = [[sb([P, CHUNK], U32, "z_codes%d%d" % (c, a)) for a in range(PASSES)] for c in range(CHUNKS)]
         z_planes = [[sb([P, CHUNK], U8, "z_planes%d%d" % (c, a)) for a in range(PASSES)] for c in range(CHUNKS)]
-        for c in range(CHUNKS):
-            for a in range(PASSES):
-                for t in range(PACK):
-                    col = a * PACK + t
-                    acc = bank(E_BANKS[(c * PASSES * PACK + col) % len(E_BANKS)], [P, CHUNK])
-                    nc.tensor.matmul_mx(
-                        acc[:],
-                        lhsT=v2_words[:, col * P : (col + 1) * P].bitcast(FP8X4),
-                        lhsT_scale=v2_plane[:, col * P : (col + 1) * P],
-                        rhs=h_codes[c][:].bitcast(FP8X4),
-                        rhs_scale=h_planes[c][:],
-                        start=True,
-                        stop=True,
-                    )
-                    nc.scalar.activation(
-                        out=z_rows[c][a][:, t, :], in_=acc[:], func=ACT.Abs, scale=gain_sb[:, col : col + 1]
-                    )
+
+        def e_bank(number, c, a, slices, lo, hi):
+            acc = bank(number, [P, len(slices), hi - lo])
+            for place, t in enumerate(slices):
+                col = a * PACK + t
+                nc.tensor.matmul_mx(
+                    acc[:, place, :],
+                    lhsT=v2_words[:, col * P : (col + 1) * P].bitcast(FP8X4),
+                    lhsT_scale=v2_plane[:, col * P : (col + 1) * P],
+                    rhs=h_codes[c][:, lo:hi].bitcast(FP8X4),
+                    rhs_scale=h_planes[c][:, lo:hi],
+                    start=True,
+                    stop=True,
+                )
+            for place, t in enumerate(slices):
+                col = a * PACK + t
+                nc.scalar.activation(
+                    out=z_rows[c][a][:, t, lo:hi], in_=acc[:, place, :], func=ACT.Abs, scale=gain_sb[:, col : col + 1]
+                )
+
+        h_passes(0, range(S // BLOCK))
+        h_passes(1, range(per_chunk))
+        h_empty((0, 1))
+        h_quantise(0, 0, half)
+        e_bank(0, 0, 0, (0, 1), 0, half)
+        e_bank(1, 0, 0, (2, 3), 0, half)
+        h_passes(1, range(per_chunk, 2 * per_chunk))
+        h_empty((2, 3))
+        h_quantise(0, half, CHUNK)
+        e_bank(2, 0, 0, (0, 1), half, CHUNK)
+        e_bank(3, 0, 0, (2, 3), half, CHUNK)
+        h_empty(range(per_chunk, 2 * per_chunk))
+        h_quantise(1, 0, CHUNK)
+        for t in range(PACK):
+            e_bank(per_chunk + t, 0, 1, (t,), 0, CHUNK)
+        turns = []
+        for lo in (0, half):
+            turns.extend([(1, a, pair, lo, lo + half) for a in range(PASSES) for pair in ((0, 1), (2, 3))])
+        for turn, fill in enumerate(turns):
+            e_bank(E_BANKS[turn % len(E_BANKS)], *fill)
 
         def z_weave(c, a, lo, hi):
             weave(z_bf[c][a][:, lo:hi, :], z_rows[c][a][:, :, lo:hi])
@@ -280,7 +309,6 @@ def tile_list_tutor_progress_matching_kernel(
                 nc.scalar.activation(out=res[:], in_=acc[:], func=ACT.Tanh)
                 nc.sync.dma_start(out_view[:, tiles[0] : tiles[-1] + 1, c * CHUNK + lo : c * CHUNK + hi], res[:])
 
-        half, three_quarters = CHUNK // 2, 3 * CHUNK // 4
         first = y_open(0, 0, CHUNK, ((3, (0,)), (4, (1,)), (5, (2,))))
         mix_weave(0)
         z_weave(0, 0, 0, CHUNK)
@@ -290,9 +318,8 @@ def tile_list_tutor_progress_matching_kernel(
         z_weave(0, 1, 0, CHUNK)
         z_quantise(0, 0, 0, CHUNK)
         y_mix(first, 0)
+        three_quarters = 3 * CHUNK // 4
         second = y_open(1, 0, half, ((6, (0, 1)), (7, (2,))))
-        third = y_open(1, half, three_quarters, ((1, (0, 1, 2)),))
-        fourth = y_open(1, three_quarters, CHUNK, ((2, (0, 1, 2)),))
         z_weave(1, 0, 0, half)
         z_quantise(0, 1, 0, CHUNK)
         y_mix(first, 1)
@@ -304,14 +331,16 @@ def tile_list_tutor_progress_matching_kernel(
         z_quantise(1, 1, 0, half)
         y_mix(second, 1)
         y_out(second)
+        third = y_open(1, half, three_quarters, ((2, (0, 1, 2)),))
+        fourth = y_open(1, three_quarters, CHUNK, ((0, (0, 1)), (1, (2,))))
         z_weave(1, 1, half, three_quarters)
         z_quantise(1, 0, half, CHUNK)
-        y_mix(third, 0)
-        y_mix(fourth, 0)
-        z_weave(1, 1, three_quarters, CHUNK)
         z_quantise(1, 1, half, three_quarters)
+        y_mix(third, 0)
         y_mix(third, 1)
         y_out(third)
+        y_mix(fourth, 0)
+        z_weave(1, 1, three_quarters, CHUNK)
         z_quantise(1, 1, three_quarters, CHUNK)
         y_mix(fourth, 1)
         y_out(fourth)

@@ -26,6 +26,7 @@ CHUNK = 512
 CHUNKS = S // CHUNK
 BLOCK = 128
 WQ_SPLIT = 44
+MIX_SCALAR = (384, 256)
 E_BANKS = (0, 1, 2)
 
 
@@ -63,7 +64,7 @@ def tile_list_tutor_progress_matching_kernel(
         wq_raw0 = sb([P, PACK, H], F32, "wq_raw0", tag="reuse_g")
         v_planes = sb([P, PASSES, S], U8, "v_planes")
 
-        nc.gpsimd.memset(v2_scale_win[:].bitcast(I32), 0)
+        nc.vector.memset(v2_scale_win[:].bitcast(I32), 0)
         nc.vector.memset(v_scale_win[QUAD : 2 * QUAD, :].bitcast(I32), 0)
         nc.vector.memset(v_scale_win[2 * QUAD : P, :].bitcast(I32), 0)
         nc.vector.memset(v_planes[:].bitcast(I32), 0)
@@ -85,13 +86,13 @@ def tile_list_tutor_progress_matching_kernel(
 
         v_scale_rows = sb([P, S], U8, "v_scale_rows")
         nc.vector.tensor_copy(v_scale_rows[:], v_scale_win[:].indirect(idx[:]))
+        v_word_win1 = sb([P, T], I32, "v_word_win1", tag="reuse_a")
+        nc.sync.dma_start(v_word_win1[:], words_of(tab_words, 1))
         for q in range(QUADS):
             nc.sync.dma_start(
                 v_planes[QUAD * q : QUAD * q + 4, :, :].bitcast(I32),
                 v_scale_rows[8 * q : 8 * q + 8, :].bitcast(I32),
             )
-        v_word_win1 = sb([P, T], I32, "v_word_win1", tag="reuse_a")
-        nc.sync.dma_start(v_word_win1[:], words_of(tab_words, 1))
 
         v2_words = sb([P, S2], U32, "v2_words")
         nc.vector.tensor_copy(
@@ -206,11 +207,25 @@ def tile_list_tutor_progress_matching_kernel(
             for t in range(PACK):
                 col = a * PACK + t
                 nc.scalar.activation(
-                    out=mix_rows[a][:, t, :], in_=mix_raw[:, a, t, :], func=ACT.Copy, scale=gain_sign[:, col : col + 1]
+                    out=mix_rows[a][:, t, 0 : MIX_SCALAR[a]],
+                    in_=mix_raw[:, a, t, 0 : MIX_SCALAR[a]],
+                    func=ACT.Copy,
+                    scale=gain_sign[:, col : col + 1],
                 )
 
         def mix_weave(a):
-            weave(mix_bf[:, a * N : (a + 1) * N, :], mix_rows[a][:])
+            cut = MIX_SCALAR[a]
+            weave(mix_bf[:, a * N : a * N + cut, :], mix_rows[a][:, :, 0:cut])
+            if cut < N:
+                nc.vector.tensor_tensor(
+                    mix_bf[:, a * N + cut : (a + 1) * N, :].rearrange("p (c i) t -> p c t i", i=4),
+                    mix_raw[:, a, :, cut:N].rearrange("p t (c i) -> p c t i", i=4),
+                    gain_sign[:, a * PACK : (a + 1) * PACK]
+                    .unsqueeze(1)
+                    .unsqueeze(3)
+                    .to_broadcast([P, (N - cut) // 4, PACK, 4]),
+                    ALU.mult,
+                )
 
         z_rows = [[sb([P, PACK, CHUNK], BF16, "z_rows%d%d" % (c, a)) for a in range(PASSES)] for c in range(CHUNKS)]
         z_bf = [[sb([P, CHUNK, PACK], BF16, "z_bf%d%d" % (c, a)) for a in range(PASSES)] for c in range(CHUNKS)]
@@ -238,16 +253,17 @@ def tile_list_tutor_progress_matching_kernel(
 
         h_passes(0, range(S // BLOCK))
         h_passes(1, range(per_chunk))
-        h_empty((0, 1))
+        h_empty((0, 1, 2))
         h_quantise(0, 0, half)
         e_bank(0, 0, 0, (0, 1), 0, half)
         e_bank(1, 0, 0, (2, 3), 0, half)
         h_passes(1, range(per_chunk, 2 * per_chunk))
-        h_empty((2, 3))
+        h_empty((3, 4))
         h_quantise(0, half, CHUNK)
         e_bank(2, 0, 0, (0, 1), half, CHUNK)
         e_bank(3, 0, 0, (2, 3), half, CHUNK)
-        h_empty(range(per_chunk, 2 * per_chunk))
+        h_empty((5, 6, 7))
+        mix_weave(0)
         h_quantise(1, 0, CHUNK)
         for t in range(PACK):
             e_bank(per_chunk + t, 0, 1, (t,), 0, CHUNK)
@@ -302,15 +318,15 @@ def tile_list_tutor_progress_matching_kernel(
 
         out_view = out.rearrange("(n p) j -> p n j", p=P)
 
-        def y_out(piece):
+        def y_out(piece, last_queue=nc.sync):
             c, lo, hi, accs = piece
             for acc, tiles in accs:
                 res = sb([P, len(tiles), hi - lo], F32, "res%d_%d_%d" % (c, lo, tiles[0]))
                 nc.scalar.activation(out=res[:], in_=acc[:], func=ACT.Tanh)
-                nc.sync.dma_start(out_view[:, tiles[0] : tiles[-1] + 1, c * CHUNK + lo : c * CHUNK + hi], res[:])
+                queue = last_queue if tiles[-1] == N // P - 1 else nc.sync
+                queue.dma_start(out_view[:, tiles[0] : tiles[-1] + 1, c * CHUNK + lo : c * CHUNK + hi], res[:])
 
         first = y_open(0, 0, CHUNK, ((3, (0,)), (4, (1,)), (5, (2,))))
-        mix_weave(0)
         z_weave(0, 0, 0, CHUNK)
         mix_weave(1)
         for lo, hi in ((0, CHUNK), (CHUNK, PASSES * N)):
@@ -318,7 +334,6 @@ def tile_list_tutor_progress_matching_kernel(
         z_weave(0, 1, 0, CHUNK)
         z_quantise(0, 0, 0, CHUNK)
         y_mix(first, 0)
-        three_quarters = 3 * CHUNK // 4
         second = y_open(1, 0, half, ((6, (0, 1)), (7, (2,))))
         z_weave(1, 0, 0, half)
         z_quantise(0, 1, 0, CHUNK)
@@ -331,16 +346,10 @@ def tile_list_tutor_progress_matching_kernel(
         z_quantise(1, 1, 0, half)
         y_mix(second, 1)
         y_out(second)
-        third = y_open(1, half, three_quarters, ((2, (0, 1, 2)),))
-        fourth = y_open(1, three_quarters, CHUNK, ((0, (0, 1)), (1, (2,))))
-        z_weave(1, 1, half, three_quarters)
+        third = y_open(1, half, CHUNK, ((2, (0,)), (0, (1,)), (1, (2,))))
+        z_weave(1, 1, half, CHUNK)
         z_quantise(1, 0, half, CHUNK)
-        z_quantise(1, 1, half, three_quarters)
         y_mix(third, 0)
+        z_quantise(1, 1, half, CHUNK)
         y_mix(third, 1)
-        y_out(third)
-        y_mix(fourth, 0)
-        z_weave(1, 1, three_quarters, CHUNK)
-        z_quantise(1, 1, three_quarters, CHUNK)
-        y_mix(fourth, 1)
-        y_out(fourth)
+        y_out(third, nc.scalar)

@@ -26,7 +26,7 @@ CHUNK = 512
 CHUNKS = S // CHUNK
 BLOCK = 128
 WQ_SPLIT = 44
-MIX_SCALAR = (384, 256)
+MIX_PART = 256
 E_BANKS = (0, 1, 2)
 
 
@@ -166,12 +166,18 @@ def tile_list_tutor_progress_matching_kernel(
         nc.scalar.activation(out=gain_sign0[:], in_=gain_sb, func=ACT.Sign)
         nc.scalar.activation(out=gain_sign[:], in_=gain_sign0[:], func=ACT.Sign, scale=2.0, bias=1.0)
 
-        h_bf = [sb([P, CHUNK, PACK], BF16, "h_bf%d" % c) for c in range(CHUNKS)]
+        half = CHUNK // 2
+        h_first = [sb([P, half, PACK], BF16, "h_first%d" % u) for u in range(2)]
+        h_second = sb([P, CHUNK, PACK], BF16, "h_second")
         h_codes = [sb([P, CHUNK], U32, "h_codes%d" % c) for c in range(CHUNKS)]
         h_planes = [sb([P, CHUNK], U8, "h_planes%d" % c) for c in range(CHUNKS)]
         h_accs = [bank(b, [P, PACK, BLOCK]) for b in range(S // BLOCK)]
         per_chunk = CHUNK // BLOCK
-        half = CHUNK // 2
+
+        def h_woven(c, lo, hi):
+            if c == 1:
+                return h_second[:, lo:hi, :]
+            return h_first[lo // half][:, lo % half : lo % half + hi - lo, :]
 
         def h_passes(a, blocks):
             for b in blocks:
@@ -190,42 +196,48 @@ def tile_list_tutor_progress_matching_kernel(
             for b in blocks:
                 c, lo = b // per_chunk, (b % per_chunk) * BLOCK
                 nc.vector.tensor_tensor(
-                    h_bf[c][:, lo : lo + BLOCK, :].rearrange("p (j i) t -> p j t i", i=2),
+                    h_woven(c, lo, lo + BLOCK).rearrange("p (j i) t -> p j t i", i=2),
                     h_accs[b][:].rearrange("p t (j i) -> p j t i", i=2),
                     bq_sb.unsqueeze(1).unsqueeze(3).to_broadcast([P, BLOCK // 2, PACK, 2]),
                     ALU.add,
                 )
 
         def h_quantise(c, lo, hi):
-            quantise(h_codes[c][:, lo:hi], h_planes[c][:, lo:hi], h_bf[c][:, lo:hi, :])
+            quantise(h_codes[c][:, lo:hi], h_planes[c][:, lo:hi], h_woven(c, lo, hi))
 
-        mix_rows = [sb([P, PACK, N], BF16, "mix_rows%d" % a) for a in range(PASSES)]
-        mix_bf = sb([P, PASSES * N, PACK], BF16, "mix_bf")
+        signed = 2 * MIX_PART
+        mix_rows = sb([P, PACK, signed], BF16, "mix_rows")
+        mix_rest = sb([P, MIX_PART, PACK], BF16, "mix_rest")
         mix_codes = sb([P, PASSES * N], U32, "mix_codes")
         mix_planes = sb([P, PASSES * N], U8, "mix_planes")
         for a in range(PASSES):
+            width = min(N, signed - a * N)
             for t in range(PACK):
                 col = a * PACK + t
                 nc.scalar.activation(
-                    out=mix_rows[a][:, t, 0 : MIX_SCALAR[a]],
-                    in_=mix_raw[:, a, t, 0 : MIX_SCALAR[a]],
+                    out=mix_rows[:, t, a * N : a * N + width],
+                    in_=mix_raw[:, a, t, 0:width],
                     func=ACT.Copy,
                     scale=gain_sign[:, col : col + 1],
                 )
 
-        def mix_weave(a):
-            cut = MIX_SCALAR[a]
-            weave(mix_bf[:, a * N : a * N + cut, :], mix_rows[a][:, :, 0:cut])
-            if cut < N:
-                nc.vector.tensor_tensor(
-                    mix_bf[:, a * N + cut : (a + 1) * N, :].rearrange("p (c i) t -> p c t i", i=4),
-                    mix_raw[:, a, :, cut:N].rearrange("p t (c i) -> p c t i", i=4),
-                    gain_sign[:, a * PACK : (a + 1) * PACK]
-                    .unsqueeze(1)
-                    .unsqueeze(3)
-                    .to_broadcast([P, (N - cut) // 4, PACK, 4]),
-                    ALU.mult,
-                )
+        def mix_weave(part):
+            woven = sb([P, MIX_PART, PACK], BF16, "mix_bf%d" % part, tag="h_first%d" % part)
+            rows = mix_rows[:, :, part * MIX_PART : (part + 1) * MIX_PART]
+            nc.gpsimd.tensor_scalar(woven[:], rows.rearrange("p t c -> p c t"), 1.0, 0.0, ALU.mult, ALU.add)
+            return woven
+
+        def mix_sign_rest():
+            nc.vector.tensor_tensor(
+                mix_rest[:].rearrange("p (c i) t -> p c t i", i=4),
+                mix_raw[:, 1, :, N - MIX_PART : N].rearrange("p t (c i) -> p c t i", i=4),
+                gain_sign[:, PACK : 2 * PACK].unsqueeze(1).unsqueeze(3).to_broadcast([P, MIX_PART // 4, PACK, 4]),
+                ALU.mult,
+            )
+
+        def mix_quantise(lo, woven):
+            hi = lo + woven.shape[1]
+            quantise(mix_codes[:, lo:hi], mix_planes[:, lo:hi], woven)
 
         z_rows = [[sb([P, PACK, CHUNK], BF16, "z_rows%d%d" % (c, a)) for a in range(PASSES)] for c in range(CHUNKS)]
         z_bf = [[sb([P, CHUNK, PACK], BF16, "z_bf%d%d" % (c, a)) for a in range(PASSES)] for c in range(CHUNKS)]
@@ -251,27 +263,35 @@ def tile_list_tutor_progress_matching_kernel(
                     out=z_rows[c][a][:, t, lo:hi], in_=acc[:, place, :], func=ACT.Abs, scale=gain_sb[:, col : col + 1]
                 )
 
+        fills = [
+            (c, a, pair, lo, lo + half)
+            for c in range(CHUNKS)
+            for lo in (0, half)
+            for a in range(PASSES)
+            for pair in ((0, 1), (2, 3))
+        ]
+
+        def e_fills(first, last):
+            for turn in range(first, last):
+                number = turn if turn < 4 else E_BANKS[(turn - 4) % len(E_BANKS)]
+                e_bank(number, *fills[turn])
+
         h_passes(0, range(S // BLOCK))
         h_passes(1, range(per_chunk))
-        h_empty((0, 1, 2))
+        h_empty((0, 1))
         h_quantise(0, 0, half)
-        e_bank(0, 0, 0, (0, 1), 0, half)
-        e_bank(1, 0, 0, (2, 3), 0, half)
+        mix_woven = [mix_weave(0)]
+        e_fills(0, 2)
         h_passes(1, range(per_chunk, 2 * per_chunk))
-        h_empty((3, 4))
+        h_empty((2, 3, 4))
+        e_fills(2, 4)
         h_quantise(0, half, CHUNK)
-        e_bank(2, 0, 0, (0, 1), half, CHUNK)
-        e_bank(3, 0, 0, (2, 3), half, CHUNK)
+        mix_woven.append(mix_weave(1))
+        e_fills(4, 8)
         h_empty((5, 6, 7))
-        mix_weave(0)
+        mix_sign_rest()
         h_quantise(1, 0, CHUNK)
-        for t in range(PACK):
-            e_bank(per_chunk + t, 0, 1, (t,), 0, CHUNK)
-        turns = []
-        for lo in (0, half):
-            turns.extend([(1, a, pair, lo, lo + half) for a in range(PASSES) for pair in ((0, 1), (2, 3))])
-        for turn, fill in enumerate(turns):
-            e_bank(E_BANKS[turn % len(E_BANKS)], *fill)
+        e_fills(8, 16)
 
         def z_weave(c, a, lo, hi):
             weave(z_bf[c][a][:, lo:hi, :], z_rows[c][a][:, :, lo:hi])
@@ -281,7 +301,7 @@ def tile_list_tutor_progress_matching_kernel(
 
         def y_open(c, lo, hi, groups):
             width = hi - lo
-            step = CHUNK if width == CHUNK else BLOCK
+            step = width
             accs = []
             for number, tiles in groups:
                 acc = bank(number, [P, len(tiles), width])
@@ -326,15 +346,14 @@ def tile_list_tutor_progress_matching_kernel(
                 queue = last_queue if tiles[-1] == N // P - 1 else nc.sync
                 queue.dma_start(out_view[:, tiles[0] : tiles[-1] + 1, c * CHUNK + lo : c * CHUNK + hi], res[:])
 
-        first = y_open(0, 0, CHUNK, ((3, (0,)), (4, (1,)), (5, (2,))))
+        first = y_open(0, 0, CHUNK, ((4, (0,)), (5, (1,)), (6, (2,))))
+        for part, woven in enumerate(mix_woven + [mix_rest]):
+            mix_quantise(part * MIX_PART, woven[:])
         z_weave(0, 0, 0, CHUNK)
-        mix_weave(1)
-        for lo, hi in ((0, CHUNK), (CHUNK, PASSES * N)):
-            quantise(mix_codes[:, lo:hi], mix_planes[:, lo:hi], mix_bf[:, lo:hi, :])
         z_weave(0, 1, 0, CHUNK)
         z_quantise(0, 0, 0, CHUNK)
         y_mix(first, 0)
-        second = y_open(1, 0, half, ((6, (0, 1)), (7, (2,))))
+        second = y_open(1, 0, half, ((7, (0, 1)), (3, (2,))))
         z_weave(1, 0, 0, half)
         z_quantise(0, 1, 0, CHUNK)
         y_mix(first, 1)
@@ -346,7 +365,7 @@ def tile_list_tutor_progress_matching_kernel(
         z_quantise(1, 1, 0, half)
         y_mix(second, 1)
         y_out(second)
-        third = y_open(1, half, CHUNK, ((2, (0,)), (0, (1,)), (1, (2,))))
+        third = y_open(1, half, CHUNK, ((0, (0,)), (1, (1,)), (2, (2,))))
         z_weave(1, 1, half, CHUNK)
         z_quantise(1, 0, half, CHUNK)
         y_mix(third, 0)

@@ -26,7 +26,7 @@ CHUNK = 512
 CHUNKS = S // CHUNK
 BLOCK = 128
 WQ_SPLIT = 44
-MIX_PART = 256
+MIX_PARTS = ((0, 256), (256, 384))
 E_BANKS = (0, 1, 2)
 
 
@@ -205,33 +205,27 @@ def tile_list_tutor_progress_matching_kernel(
         def h_quantise(c, lo, hi):
             quantise(h_codes[c][:, lo:hi], h_planes[c][:, lo:hi], h_woven(c, lo, hi))
 
-        signed = 2 * MIX_PART
-        mix_rows = sb([P, PACK, signed], BF16, "mix_rows")
-        mix_rest = sb([P, MIX_PART, PACK], BF16, "mix_rest")
+        mix_rows = sb([P, PACK, N], BF16, "mix_rows")
+        mix_last = sb([P, N, PACK], BF16, "mix_last")
         mix_codes = sb([P, PASSES * N], U32, "mix_codes")
         mix_planes = sb([P, PASSES * N], U8, "mix_planes")
-        for a in range(PASSES):
-            width = min(N, signed - a * N)
-            for t in range(PACK):
-                col = a * PACK + t
-                nc.scalar.activation(
-                    out=mix_rows[:, t, a * N : a * N + width],
-                    in_=mix_raw[:, a, t, 0:width],
-                    func=ACT.Copy,
-                    scale=gain_sign[:, col : col + 1],
-                )
+        for t in range(PACK):
+            nc.scalar.activation(
+                out=mix_rows[:, t, :], in_=mix_raw[:, 0, t, :], func=ACT.Copy, scale=gain_sign[:, t : t + 1]
+            )
 
         def mix_weave(part):
-            woven = sb([P, MIX_PART, PACK], BF16, "mix_bf%d" % part, tag="h_first%d" % part)
-            rows = mix_rows[:, :, part * MIX_PART : (part + 1) * MIX_PART]
-            nc.gpsimd.tensor_scalar(woven[:], rows.rearrange("p t c -> p c t"), 1.0, 0.0, ALU.mult, ALU.add)
+            lo, hi = MIX_PARTS[part]
+            woven = sb([P, hi - lo, PACK], BF16, "mix_bf%d" % part, tag="h_first%d" % part)
+            rows = mix_rows[:, :, lo:hi].rearrange("p t c -> p c t")
+            nc.gpsimd.tensor_scalar(woven[:], rows, 1.0, 0.0, ALU.mult, ALU.add)
             return woven
 
-        def mix_sign_rest():
+        def mix_sign_last():
             nc.vector.tensor_tensor(
-                mix_rest[:].rearrange("p (c i) t -> p c t i", i=4),
-                mix_raw[:, 1, :, N - MIX_PART : N].rearrange("p t (c i) -> p c t i", i=4),
-                gain_sign[:, PACK : 2 * PACK].unsqueeze(1).unsqueeze(3).to_broadcast([P, MIX_PART // 4, PACK, 4]),
+                mix_last[:].rearrange("p (c i) t -> p c t i", i=4),
+                mix_raw[:, 1, :, :].rearrange("p t (c i) -> p c t i", i=4),
+                gain_sign[:, PACK : 2 * PACK].unsqueeze(1).unsqueeze(3).to_broadcast([P, N // 4, PACK, 4]),
                 ALU.mult,
             )
 
@@ -276,6 +270,12 @@ def tile_list_tutor_progress_matching_kernel(
                 number = turn if turn < 4 else E_BANKS[(turn - 4) % len(E_BANKS)]
                 e_bank(number, *fills[turn])
 
+        def z_weave(c, a, lo, hi):
+            weave(z_bf[c][a][:, lo:hi, :], z_rows[c][a][:, :, lo:hi])
+
+        def z_quantise(c, a, lo, hi):
+            quantise(z_codes[c][a][:, lo:hi], z_planes[c][a][:, lo:hi], z_bf[c][a][:, lo:hi, :])
+
         h_passes(0, range(S // BLOCK))
         h_passes(1, range(per_chunk))
         h_empty((0, 1))
@@ -289,15 +289,9 @@ def tile_list_tutor_progress_matching_kernel(
         mix_woven.append(mix_weave(1))
         e_fills(4, 8)
         h_empty((5, 6, 7))
-        mix_sign_rest()
+        z_weave(0, 0, 0, half)
         h_quantise(1, 0, CHUNK)
         e_fills(8, 16)
-
-        def z_weave(c, a, lo, hi):
-            weave(z_bf[c][a][:, lo:hi, :], z_rows[c][a][:, :, lo:hi])
-
-        def z_quantise(c, a, lo, hi):
-            quantise(z_codes[c][a][:, lo:hi], z_planes[c][a][:, lo:hi], z_bf[c][a][:, lo:hi, :])
 
         def y_open(c, lo, hi, groups):
             width = hi - lo
@@ -321,19 +315,20 @@ def tile_list_tutor_progress_matching_kernel(
                 accs.append((acc, tiles))
             return c, lo, hi, accs
 
-        def y_mix(piece, a):
-            c, lo, hi, accs = piece
+        def y_mix(piece, a, part=None):
+            c, base, end, accs = piece
+            lo, hi = part or (base, end)
             for acc, tiles in accs:
                 for place, n in enumerate(tiles):
                     ns = slice(a * N + n * P, a * N + (n + 1) * P)
                     nc.tensor.matmul_mx(
-                        acc[:, place, :],
+                        acc[:, place, lo - base : hi - base],
                         lhsT=mix_codes[:, ns].bitcast(FP8X4),
                         lhsT_scale=mix_planes[:, ns],
                         rhs=z_codes[c][a][:, lo:hi].bitcast(FP8X4),
                         rhs_scale=z_planes[c][a][:, lo:hi],
                         start=False,
-                        stop=(a == PASSES - 1 and place == len(tiles) - 1),
+                        stop=(a == PASSES - 1 and place == len(tiles) - 1 and hi == end),
                     )
 
         out_view = out.rearrange("(n p) j -> p n j", p=P)
@@ -347,9 +342,11 @@ def tile_list_tutor_progress_matching_kernel(
                 queue.dma_start(out_view[:, tiles[0] : tiles[-1] + 1, c * CHUNK + lo : c * CHUNK + hi], res[:])
 
         first = y_open(0, 0, CHUNK, ((4, (0,)), (5, (1,)), (6, (2,))))
-        for part, woven in enumerate(mix_woven + [mix_rest]):
-            mix_quantise(part * MIX_PART, woven[:])
-        z_weave(0, 0, 0, CHUNK)
+        mix_sign_last()
+        for part, woven in zip(MIX_PARTS, mix_woven):
+            mix_quantise(part[0], woven[:])
+        z_weave(0, 0, half, CHUNK)
+        mix_quantise(N, mix_last[:])
         z_weave(0, 1, 0, CHUNK)
         z_quantise(0, 0, 0, CHUNK)
         y_mix(first, 0)
@@ -366,9 +363,12 @@ def tile_list_tutor_progress_matching_kernel(
         y_mix(second, 1)
         y_out(second)
         third = y_open(1, half, CHUNK, ((0, (0,)), (1, (1,)), (2, (2,))))
-        z_weave(1, 1, half, CHUNK)
         z_quantise(1, 0, half, CHUNK)
         y_mix(third, 0)
-        z_quantise(1, 1, half, CHUNK)
-        y_mix(third, 1)
+        ends = ((half, half + BLOCK), (half + BLOCK, CHUNK))
+        for part in ends:
+            z_weave(1, 1, *part)
+        for part in ends:
+            z_quantise(1, 1, *part)
+            y_mix(third, 1, part)
         y_out(third, nc.scalar)

@@ -1,6 +1,7 @@
 from contextlib import ExitStack
 
 import concourse.mybir as mybir
+from concourse.masks import make_identity
 
 K, H, N, T, S, T2, S2 = 1024, 512, 384, 4096, 1024, 2048, 1024
 FLOPS = 2 * S * (K * H + H * S2 + S2 * N + K * N)
@@ -19,15 +20,18 @@ ACT = mybir.ActivationFunctionType
 P = 128
 PACK = 4
 PASSES = 2
+PASS = P * PACK
 QUADS = 4
 QUAD = P // QUADS
+QUAD_ORDER = (0, 2, 1, 3)
 LIST_ROWS = 16
 CHUNK = 512
 CHUNKS = S // CHUNK
+HALF = CHUNK // 2
 BLOCK = 128
 WQ_SPLIT = 44
-MIX_PARTS = ((0, 256), (256, 384))
-E_BANKS = (0, 1, 2)
+BANKS = 8
+E_BANKS = (0, 1, 2, 6, 7)
 
 
 def tile_list_tutor_progress_matching_kernel(
@@ -36,6 +40,8 @@ def tile_list_tutor_progress_matching_kernel(
     nc = tc.nc
     with ExitStack() as ctx:
         held = ctx.enter_context(tc.tile_pool(name="held", bufs=1))
+        later = ctx.enter_context(tc.tile_pool(name="later", bufs=1))
+        shared = ctx.enter_context(tc.tile_pool(name="shared", bufs=1))
         psum = ctx.enter_context(tc.psum_pool(name="psum", bufs=1))
 
         def sb(shape, dtype, name, tag=None):
@@ -50,24 +56,26 @@ def tile_list_tutor_progress_matching_kernel(
         def quantise(codes, plane, woven):
             nc.vector.quantize_mx(codes.bitcast(FP8X4), plane, woven.rearrange("p c t -> p (c t)"))
 
-        def weave(woven, slices):
-            nc.vector.tensor_copy(
-                woven.rearrange("p (c i) t -> p c t i", i=4), slices.rearrange("p t (c i) -> p c t i", i=4)
+        def weave_views(woven, slices):
+            return (
+                woven.rearrange("p (c i) t -> p c t i", i=4),
+                slices.rearrange("p t (c i) -> p c t i", i=4),
             )
 
         idx = held.tile([P, S // LIST_ROWS], U16, name="idx")
         idx2 = held.tile([P, S2 // LIST_ROWS], U16, name="idx2")
         v_scale_win = sb([P, T], U8, "v_scale_win", tag="reuse_a")
-        v2_word_win = sb([P, T2], I32, "v2_word_win", tag="reuse_b")
-        v2_scale_win = sb([P, T2], U8, "v2_scale_win", tag="reuse_c")
-        v_word_win0 = sb([P, T], I32, "v_word_win0", tag="reuse_f")
-        wq_raw0 = sb([P, PACK, H], F32, "wq_raw0", tag="reuse_g")
+        v2_scale_win = sb([P, T2], U8, "v2_scale_win", tag="reuse_b")
+        v_word_win0 = sb([P, T], I32, "v_word_win0", tag="reuse_c")
+        wq_raw0 = later.tile([P, PACK, H], F32, name="wq_raw0", align_bytes=64, offset=0)
         v_planes = sb([P, PASSES, S], U8, "v_planes")
+        v2_plane = sb([P, S2], U8, "v2_plane")
 
         nc.vector.memset(v2_scale_win[:].bitcast(I32), 0)
         nc.vector.memset(v_scale_win[QUAD : 2 * QUAD, :].bitcast(I32), 0)
         nc.vector.memset(v_scale_win[2 * QUAD : P, :].bitcast(I32), 0)
         nc.vector.memset(v_planes[:].bitcast(I32), 0)
+        nc.vector.memset(v2_plane[:].bitcast(I32), 0)
 
         wq_view = wq.rearrange("(a p i) r -> a p i r", a=PASSES, i=PACK)
         mix_view = mix.rearrange("(a p i) n -> a p i n", a=PASSES, i=PACK)
@@ -75,57 +83,62 @@ def tile_list_tutor_progress_matching_kernel(
         nc.sync.dma_start(idx[:], offs)
         nc.sync.dma_start(v_scale_win[0:QUAD, :].bitcast(I32), tab_scales.rearrange("a q x -> q a x").bitcast(I32))
         nc.sync.dma_start(idx2[:], offs2)
-        nc.sync.dma_start(v2_word_win[:], words_of(tab2_words, 0))
-        for q in range(QUADS):
-            nc.sync.dma_start(
-                v2_scale_win[QUAD * q : QUAD * q + 4, :].bitcast(I32),
-                tab2_scales[0, 4 * q : 4 * q + 4, :].bitcast(I32),
-            )
+        nc.sync.dma_start(v2_scale_win[0:P:8, :].bitcast(I32), tab2_scales[0].bitcast(I32))
         nc.sync.dma_start(v_word_win0[:], words_of(tab_words, 0))
         nc.sync.dma_start(wq_raw0[:], wq_view[0])
+        vec_rows = sb([P, PACK * P], F32, "vec_rows")
+        identity = sb([P, P], F32, "identity")
+        nc.gpsimd.memset(vec_rows[:], 0.0)
+        make_identity(nc, identity[:])
+        nc.sync.dma_start(vec_rows[0:PASSES, :], gain.rearrange("(a x) -> a x", a=PASSES))
+        nc.sync.dma_start(vec_rows[PASSES : PASSES + 1, :], bq.unsqueeze(0))
 
         v_scale_rows = sb([P, S], U8, "v_scale_rows")
         nc.vector.tensor_copy(v_scale_rows[:], v_scale_win[:].indirect(idx[:]))
-        v_word_win1 = sb([P, T], I32, "v_word_win1", tag="reuse_a")
-        nc.sync.dma_start(v_word_win1[:], words_of(tab_words, 1))
-        for q in range(QUADS):
+        for q in QUAD_ORDER:
             nc.sync.dma_start(
                 v_planes[QUAD * q : QUAD * q + 4, :, :].bitcast(I32),
                 v_scale_rows[8 * q : 8 * q + 8, :].bitcast(I32),
             )
+        v_word_win1 = sb([P, T], I32, "v_word_win1", tag="reuse_a")
+        nc.sync.dma_start(v_word_win1[:], words_of(tab_words, 1))
 
-        v2_words = sb([P, S2], U32, "v2_words")
+        v2_scale_rows = sb([P, S2], U8, "v2_scale_rows")
         nc.vector.tensor_copy(
-            v2_words[:].rearrange("p (a i s) -> p a s i", a=PASSES, i=PACK),
-            v2_word_win[:].bitcast(U32).indirect(idx2[:]),
+            v2_scale_rows[:].rearrange("p (a i s) -> p a s i", a=PASSES, i=PACK), v2_scale_win[:].indirect(idx2[:])
         )
+
         wq_raw1 = sb([P, PACK, H], F32, "wq_raw1", tag="reuse_b")
         nc.sync.dma_start(wq_raw1[:], wq_view[1])
-        v2_scale_list = sb([P, S2], U8, "v2_scale_list", tag="reuse_d")
-        nc.vector.tensor_copy(v2_scale_list[:], v2_scale_win[:].indirect(idx2[:]))
+        for q in QUAD_ORDER:
+            nc.sync.dma_start(
+                v2_plane[QUAD * q : QUAD * q + 4, :].bitcast(I32),
+                v2_scale_rows[QUAD * q : QUAD * (q + 1) : 8, :].bitcast(I32),
+            )
 
-        late = sb([P, 16], F32, "late", tag="reuse_c")
-        bq_sb = late[:, 0:PACK]
-        gain_sb = late[:, 8:16]
-        nc.sync.dma_start(bq_sb, bq.rearrange("(p i) -> p i", i=PACK))
-        nc.sync.dma_start(
-            gain_sb.rearrange("p (a i) -> p a i", i=PACK), gain.rearrange("(a p i) -> p a i", a=PASSES, i=PACK)
-        )
-        v2_plane = sb([P, S2], U8, "v2_plane")
-        nc.vector.tensor_copy(
-            v2_plane[:].rearrange("p (a i s) -> p a i s", a=PASSES, i=PACK),
-            v2_scale_list[:].rearrange("p (a s i) -> p a i s", a=PASSES, i=PACK),
-        )
-        mix_raw = sb([P, PASSES, PACK, N], F32, "mix_raw", tag="reuse_d")
-        for a in range(PASSES):
-            nc.sync.dma_start(mix_raw[:, a, :, :], mix_view[a])
+        turned = bank(0, [P, PACK, P])
+        for t in range(PACK):
+            nc.tensor.transpose(turned[:, t, :], vec_rows[:, t : PACK * P : PACK], identity[:])
+        vec_cols = sb([P, PASSES + 1, PACK], F32, "vec_cols")
+        nc.scalar.copy(vec_cols[:], turned[:, :, 0 : PASSES + 1].rearrange("p t w -> p w t"))
+        gain_sb = vec_cols[:, 0:PASSES, :].rearrange("p a t -> p (a t)")
+        bq_sb = vec_cols[:, PASSES, :]
+
+        gain_sign0 = sb([P, PASSES * PACK], F32, "gain_sign0")
+        gain_sign = sb([P, PASSES * PACK], F32, "gain_sign")
+        nc.scalar.activation(out=gain_sign0[:], in_=gain_sb, func=ACT.Sign)
+        nc.scalar.activation(out=gain_sign[:], in_=gain_sign0[:], func=ACT.Sign, scale=2.0, bias=1.0)
 
         v_words = [sb([P, S], U32, "v_words%d" % a) for a in range(PASSES)]
         nc.vector.tensor_copy(v_words[0][:], v_word_win0[:].bitcast(U32).indirect(idx[:]))
-        wd_codes = sb([P, PASSES, 2 * N], U8, "wd_codes", tag="reuse_f")
-        nc.sync.dma_start(wd_codes[:].bitcast(I32), wd_words.rearrange("a p c -> p a c").bitcast(I32))
+        mix_raw = sb([P, PASSES, PACK, N], F32, "mix_raw", tag="reuse_c")
+        for a in range(PASSES):
+            nc.sync.dma_start(mix_raw[:, a, :, :], mix_view[a])
 
-        wq_bf = [sb([P, PACK, P, PACK], BF16, "wq_bf%d" % a) for a in range(PASSES)]
+        wq_bf = [
+            shared.tile([P, PACK, P, PACK], BF16, name="wq_bf0", align_bytes=64, offset=0),
+            sb([P, PACK, P, PACK], BF16, "wq_bf1"),
+        ]
         wq_codes = sb([P, PASSES, H], U32, "wq_codes")
         wq_planes = sb([P, PASSES, H], U8, "wq_planes")
 
@@ -142,45 +155,37 @@ def tile_list_tutor_progress_matching_kernel(
             quantise(wq_codes[:, a, cols], wq_planes[:, a, cols], woven)
 
         nc.scalar.copy(*wq_views(0, wq_raw0[:], 0))
+        v2_word_win = later.tile([P, T2], I32, name="v2_word_win", align_bytes=64, offset=0)
+        nc.sync.dma_start(v2_word_win[:], words_of(tab2_words, 0))
         wq_quantise(0, 0, PACK)
-        wd_planes = sb([P, PASSES, N], U8, "wd_planes", tag="reuse_g")
+
+        wd_planes = shared.tile([P, PASSES, N], U8, name="wd_planes", align_bytes=64, offset=S2)
+        wd_codes = shared.tile([P, PASSES, 2 * N], U8, name="wd_codes", align_bytes=64, offset=2 * S2)
         nc.vector.memset(wd_planes[:].bitcast(I32), 0)
-        for q in range(QUADS):
+        nc.sync.dma_start(wd_codes[:].bitcast(I32), wd_words.rearrange("a p c -> p a c").bitcast(I32))
+        for q in QUAD_ORDER:
             nc.sync.dma_start(
                 wd_planes[QUAD * q : QUAD * q + 4, :, :].bitcast(I32),
                 wd_scales[:, 4 * q : 4 * q + 4, :].rearrange("a r c -> r a c").bitcast(I32),
             )
-        list_cols = CHUNK // LIST_ROWS
-        for c in range(CHUNKS):
-            nc.vector.tensor_copy(
-                v_words[1][:, c * CHUNK : (c + 1) * CHUNK],
-                v_word_win1[:].bitcast(U32).indirect(idx[:, c * list_cols : (c + 1) * list_cols]),
-            )
+
+        nc.vector.tensor_copy(v_words[1][:], v_word_win1[:].bitcast(U32).indirect(idx[:]))
         nc.scalar.copy(*wq_views(1, wq_raw1[:, :, 0 : PACK * WQ_SPLIT], 0))
         nc.vector.tensor_copy(*wq_views(1, wq_raw1[:, :, PACK * WQ_SPLIT : H], WQ_SPLIT))
         wq_quantise(1, 0, PACK // 2)
         wq_quantise(1, PACK // 2, PACK)
 
-        gain_sign0 = sb([P, PASSES * PACK], F32, "gain_sign0")
-        gain_sign = sb([P, PASSES * PACK], F32, "gain_sign")
-        nc.scalar.activation(out=gain_sign0[:], in_=gain_sb, func=ACT.Sign)
-        nc.scalar.activation(out=gain_sign[:], in_=gain_sign0[:], func=ACT.Sign, scale=2.0, bias=1.0)
-
-        half = CHUNK // 2
-        h_first = [sb([P, half, PACK], BF16, "h_first%d" % u) for u in range(2)]
-        h_second = sb([P, CHUNK, PACK], BF16, "h_second")
+        h_bf = [
+            sb([P, CHUNK, PACK], BF16, "h_bf0"),
+            later.tile([P, CHUNK, PACK], BF16, name="h_bf1", align_bytes=64, offset=0),
+        ]
         h_codes = [sb([P, CHUNK], U32, "h_codes%d" % c) for c in range(CHUNKS)]
         h_planes = [sb([P, CHUNK], U8, "h_planes%d" % c) for c in range(CHUNKS)]
         h_accs = [bank(b, [P, PACK, BLOCK]) for b in range(S // BLOCK)]
         per_chunk = CHUNK // BLOCK
 
-        def h_woven(c, lo, hi):
-            if c == 1:
-                return h_second[:, lo:hi, :]
-            return h_first[lo // half][:, lo % half : lo % half + hi - lo, :]
-
-        def h_passes(a, blocks):
-            for b in blocks:
+        def h_passes(a):
+            for b in range(S // BLOCK):
                 for t in range(PACK):
                     nc.tensor.matmul_mx(
                         h_accs[b][:, t, :],
@@ -191,6 +196,9 @@ def tile_list_tutor_progress_matching_kernel(
                         start=(a == 0 and t == 0),
                         stop=(a == PASSES - 1 and t == PACK - 1),
                     )
+
+        def h_woven(c, lo, hi):
+            return h_bf[c][:, lo:hi, :]
 
         def h_empty(blocks):
             for b in blocks:
@@ -205,113 +213,100 @@ def tile_list_tutor_progress_matching_kernel(
         def h_quantise(c, lo, hi):
             quantise(h_codes[c][:, lo:hi], h_planes[c][:, lo:hi], h_woven(c, lo, hi))
 
-        mix_rows = sb([P, PACK, N], BF16, "mix_rows")
-        mix_last = sb([P, N, PACK], BF16, "mix_last")
-        mix_codes = sb([P, PASSES * N], U32, "mix_codes")
+        mix_rows = [sb([P, PACK, N], BF16, "mix_rows%d" % a) for a in range(PASSES)]
+        mix_bf = [
+            sb([P, N, PACK], BF16, "mix_bf0"),
+            later.tile([P, N, PACK], BF16, name="mix_bf1", align_bytes=64, offset=2 * CHUNK * PACK),
+        ]
+        mix_codes = later.tile(
+            [P, PASSES * N], U32, name="mix_codes", align_bytes=64, offset=2 * (CHUNK + N) * PACK
+        )
         mix_planes = sb([P, PASSES * N], U8, "mix_planes")
-        for t in range(PACK):
-            nc.scalar.activation(
-                out=mix_rows[:, t, :], in_=mix_raw[:, 0, t, :], func=ACT.Copy, scale=gain_sign[:, t : t + 1]
+        for a in range(PASSES):
+            for t in range(PACK):
+                col = a * PACK + t
+                nc.scalar.activation(
+                    out=mix_rows[a][:, t, :], in_=mix_raw[:, a, t, :], func=ACT.Copy, scale=gain_sign[:, col : col + 1]
+                )
+        nc.scalar.copy(*weave_views(mix_bf[0][:], mix_rows[0][:]))
+
+        def mix_quantise(a):
+            quantise(mix_codes[:, a * N : (a + 1) * N], mix_planes[:, a * N : (a + 1) * N], mix_bf[a][:])
+
+        v2_words = [sb([P, PASS], U32, "v2_words%d" % a) for a in range(PASSES)]
+        list_cols = PASS // LIST_ROWS
+
+        def v2_gather(a):
+            nc.vector.tensor_copy(
+                v2_words[a][:].rearrange("p (i s) -> p s i", i=PACK),
+                v2_word_win[:].bitcast(U32).indirect(idx2[:, a * list_cols : (a + 1) * list_cols]),
             )
-
-        def mix_weave(part):
-            lo, hi = MIX_PARTS[part]
-            woven = sb([P, hi - lo, PACK], BF16, "mix_bf%d" % part, tag="h_first%d" % part)
-            rows = mix_rows[:, :, lo:hi].rearrange("p t c -> p c t")
-            nc.gpsimd.tensor_scalar(woven[:], rows, 1.0, 0.0, ALU.mult, ALU.add)
-            return woven
-
-        def mix_sign_last():
-            nc.vector.tensor_tensor(
-                mix_last[:].rearrange("p (c i) t -> p c t i", i=4),
-                mix_raw[:, 1, :, :].rearrange("p t (c i) -> p c t i", i=4),
-                gain_sign[:, PACK : 2 * PACK].unsqueeze(1).unsqueeze(3).to_broadcast([P, N // 4, PACK, 4]),
-                ALU.mult,
-            )
-
-        def mix_quantise(lo, woven):
-            hi = lo + woven.shape[1]
-            quantise(mix_codes[:, lo:hi], mix_planes[:, lo:hi], woven)
 
         z_rows = [[sb([P, PACK, CHUNK], BF16, "z_rows%d%d" % (c, a)) for a in range(PASSES)] for c in range(CHUNKS)]
         z_bf = [[sb([P, CHUNK, PACK], BF16, "z_bf%d%d" % (c, a)) for a in range(PASSES)] for c in range(CHUNKS)]
-        z_codes = [[sb([P, CHUNK], U32, "z_codes%d%d" % (c, a)) for a in range(PASSES)] for c in range(CHUNKS)]
+        z_codes = [
+            [sb([P, CHUNK], U32, "z_codes%d%d" % (c, a), tag="v2_words0" if c + a == 0 else None) for a in range(PASSES)]
+            for c in range(CHUNKS)
+        ]
         z_planes = [[sb([P, CHUNK], U8, "z_planes%d%d" % (c, a)) for a in range(PASSES)] for c in range(CHUNKS)]
 
-        def e_bank(number, c, a, slices, lo, hi):
-            acc = bank(number, [P, len(slices), hi - lo])
-            for place, t in enumerate(slices):
+        def e_slices(c, a):
+            for t in range(PACK):
                 col = a * PACK + t
+                turn = c * PASSES * PACK + col
+                acc = bank(turn if turn < BANKS else E_BANKS[(turn - BANKS) % len(E_BANKS)], [P, CHUNK])
                 nc.tensor.matmul_mx(
-                    acc[:, place, :],
-                    lhsT=v2_words[:, col * P : (col + 1) * P].bitcast(FP8X4),
+                    acc[:],
+                    lhsT=v2_words[a][:, t * P : (t + 1) * P].bitcast(FP8X4),
                     lhsT_scale=v2_plane[:, col * P : (col + 1) * P],
-                    rhs=h_codes[c][:, lo:hi].bitcast(FP8X4),
-                    rhs_scale=h_planes[c][:, lo:hi],
+                    rhs=h_codes[c][:].bitcast(FP8X4),
+                    rhs_scale=h_planes[c][:],
                     start=True,
                     stop=True,
                 )
-            for place, t in enumerate(slices):
-                col = a * PACK + t
                 nc.scalar.activation(
-                    out=z_rows[c][a][:, t, lo:hi], in_=acc[:, place, :], func=ACT.Abs, scale=gain_sb[:, col : col + 1]
+                    out=z_rows[c][a][:, t, :], in_=acc[:], func=ACT.Abs, scale=gain_sb[:, col : col + 1]
                 )
 
-        fills = [
-            (c, a, pair, lo, lo + half)
-            for c in range(CHUNKS)
-            for lo in (0, half)
-            for a in range(PASSES)
-            for pair in ((0, 1), (2, 3))
-        ]
-
-        def e_fills(first, last):
-            for turn in range(first, last):
-                number = turn if turn < 4 else E_BANKS[(turn - 4) % len(E_BANKS)]
-                e_bank(number, *fills[turn])
-
         def z_weave(c, a, lo, hi):
-            weave(z_bf[c][a][:, lo:hi, :], z_rows[c][a][:, :, lo:hi])
+            nc.vector.tensor_copy(*weave_views(z_bf[c][a][:, lo:hi, :], z_rows[c][a][:, :, lo:hi]))
 
         def z_quantise(c, a, lo, hi):
             quantise(z_codes[c][a][:, lo:hi], z_planes[c][a][:, lo:hi], z_bf[c][a][:, lo:hi, :])
 
-        h_passes(0, range(S // BLOCK))
-        h_passes(1, range(per_chunk))
-        h_empty((0, 1))
-        h_quantise(0, 0, half)
-        mix_woven = [mix_weave(0)]
-        e_fills(0, 2)
-        h_passes(1, range(per_chunk, 2 * per_chunk))
-        h_empty((2, 3, 4))
-        e_fills(2, 4)
-        h_quantise(0, half, CHUNK)
-        mix_woven.append(mix_weave(1))
-        e_fills(4, 8)
-        h_empty((5, 6, 7))
-        z_weave(0, 0, 0, half)
+        h_passes(0)
+        h_passes(1)
+        h_empty(range(per_chunk))
+        h_quantise(0, 0, CHUNK)
+        v2_gather(0)
+        e_slices(0, 0)
+        v2_gather(1)
+        nc.gpsimd.tensor_scalar(
+            mix_bf[1][:], mix_rows[1][:].rearrange("p t c -> p c t"), 1.0, 0.0, ALU.mult, ALU.add
+        )
+        h_empty(range(per_chunk, 2 * per_chunk))
+        e_slices(0, 1)
+        mix_quantise(0)
         h_quantise(1, 0, CHUNK)
-        e_fills(8, 16)
+        e_slices(1, 0)
+        e_slices(1, 1)
 
         def y_open(c, lo, hi, groups):
-            width = hi - lo
-            step = width
+            js = slice(c * CHUNK + lo, c * CHUNK + hi)
             accs = []
             for number, tiles in groups:
-                acc = bank(number, [P, len(tiles), width])
+                acc = bank(number, [P, len(tiles), hi - lo])
                 for place, n in enumerate(tiles):
                     for a in range(PASSES):
-                        for j in range(0, width, step):
-                            js = slice(c * CHUNK + lo + j, c * CHUNK + lo + j + step)
-                            nc.tensor.matmul_mx(
-                                acc[:, place, j : j + step],
-                                lhsT=wd_codes[:, a, 2 * n * P : 2 * (n + 1) * P].bitcast(FP4X4),
-                                lhsT_scale=wd_planes[:, a, n * P : (n + 1) * P],
-                                rhs=v_words[a][:, js].bitcast(FP8X4),
-                                rhs_scale=v_planes[:, a, js],
-                                start=(place == 0 and a == 0 and j == 0),
-                                stop=False,
-                            )
+                        nc.tensor.matmul_mx(
+                            acc[:, place, :],
+                            lhsT=wd_codes[:, a, 2 * n * P : 2 * (n + 1) * P].bitcast(FP4X4),
+                            lhsT_scale=wd_planes[:, a, n * P : (n + 1) * P],
+                            rhs=v_words[a][:, js].bitcast(FP8X4),
+                            rhs_scale=v_planes[:, a, js],
+                            start=(place == 0 and a == 0),
+                            stop=False,
+                        )
                 accs.append((acc, tiles))
             return c, lo, hi, accs
 
@@ -341,31 +336,28 @@ def tile_list_tutor_progress_matching_kernel(
                 queue = last_queue if tiles[-1] == N // P - 1 else nc.sync
                 queue.dma_start(out_view[:, tiles[0] : tiles[-1] + 1, c * CHUNK + lo : c * CHUNK + hi], res[:])
 
-        first = y_open(0, 0, CHUNK, ((4, (0,)), (5, (1,)), (6, (2,))))
-        mix_sign_last()
-        for part, woven in zip(MIX_PARTS, mix_woven):
-            mix_quantise(part[0], woven[:])
-        z_weave(0, 0, half, CHUNK)
-        mix_quantise(N, mix_last[:])
-        z_weave(0, 1, 0, CHUNK)
+        first = y_open(0, 0, CHUNK, ((3, (0,)), (4, (1,)), (5, (2,))))
+        z_weave(0, 0, 0, CHUNK)
+        mix_quantise(1)
         z_quantise(0, 0, 0, CHUNK)
         y_mix(first, 0)
-        second = y_open(1, 0, half, ((7, (0, 1)), (3, (2,))))
-        z_weave(1, 0, 0, half)
+        z_weave(0, 1, 0, CHUNK)
+        z_weave(1, 0, 0, HALF)
         z_quantise(0, 1, 0, CHUNK)
         y_mix(first, 1)
         y_out(first)
-        z_weave(1, 1, 0, half)
-        z_quantise(1, 0, 0, half)
+        second = y_open(1, 0, HALF, ((6, (0, 1)), (7, (2,))))
+        third = y_open(1, HALF, CHUNK, ((0, (0,)), (1, (1,)), (2, (2,))))
+        z_weave(1, 0, HALF, CHUNK)
+        z_quantise(1, 0, 0, HALF)
         y_mix(second, 0)
-        z_weave(1, 0, half, CHUNK)
-        z_quantise(1, 1, 0, half)
+        z_weave(1, 1, 0, HALF)
+        z_quantise(1, 0, HALF, CHUNK)
+        z_quantise(1, 1, 0, HALF)
         y_mix(second, 1)
         y_out(second)
-        third = y_open(1, half, CHUNK, ((0, (0,)), (1, (1,)), (2, (2,))))
-        z_quantise(1, 0, half, CHUNK)
         y_mix(third, 0)
-        ends = ((half, half + BLOCK), (half + BLOCK, CHUNK))
+        ends = ((HALF, HALF + BLOCK), (HALF + BLOCK, CHUNK))
         for part in ends:
             z_weave(1, 1, *part)
         for part in ends:

@@ -30,8 +30,7 @@ CHUNKS = S // CHUNK
 HALF = CHUNK // 2
 BLOCK = 128
 WQ_SPLIT = 44
-BANKS = 8
-E_BANKS = (0, 1, 2, 6, 7)
+E_TURNS = (0, 1, 2, 3, 4, 5, 6, 7) + (0, 1, 2, 7) + (0, 1, 2, 0)
 
 
 def tile_list_tutor_progress_matching_kernel(
@@ -250,23 +249,31 @@ def tile_list_tutor_progress_matching_kernel(
         ]
         z_planes = [[sb([P, CHUNK], U8, "z_planes%d%d" % (c, a)) for a in range(PASSES)] for c in range(CHUNKS)]
 
-        def e_slices(c, a):
-            for t in range(PACK):
+        def e_bank(number, c, a, slices, lo, hi):
+            acc = bank(number, [P, len(slices), hi - lo])
+            for place, t in enumerate(slices):
                 col = a * PACK + t
-                turn = c * PASSES * PACK + col
-                acc = bank(turn if turn < BANKS else E_BANKS[(turn - BANKS) % len(E_BANKS)], [P, CHUNK])
                 nc.tensor.matmul_mx(
-                    acc[:],
+                    acc[:, place, :],
                     lhsT=v2_words[a][:, t * P : (t + 1) * P].bitcast(FP8X4),
                     lhsT_scale=v2_plane[:, col * P : (col + 1) * P],
-                    rhs=h_codes[c][:].bitcast(FP8X4),
-                    rhs_scale=h_planes[c][:],
+                    rhs=h_codes[c][:, lo:hi].bitcast(FP8X4),
+                    rhs_scale=h_planes[c][:, lo:hi],
                     start=True,
                     stop=True,
                 )
+            for place, t in enumerate(slices):
+                col = a * PACK + t
                 nc.scalar.activation(
-                    out=z_rows[c][a][:, t, :], in_=acc[:], func=ACT.Abs, scale=gain_sb[:, col : col + 1]
+                    out=z_rows[c][a][:, t, lo:hi], in_=acc[:, place, :], func=ACT.Abs, scale=gain_sb[:, col : col + 1]
                 )
+
+        fills = [(c, a, (t,), 0, CHUNK) for c, a in ((0, 0), (0, 1), (1, 0)) for t in range(PACK)]
+        fills.extend((1, 1, pair, lo, lo + HALF) for lo in (0, HALF) for pair in ((0, 1), (2, 3)))
+
+        def e_fills(first, last):
+            for turn in range(first, last):
+                e_bank(E_TURNS[turn], *fills[turn])
 
         def z_weave(c, a, lo, hi):
             nc.vector.tensor_copy(*weave_views(z_bf[c][a][:, lo:hi, :], z_rows[c][a][:, :, lo:hi]))
@@ -279,17 +286,16 @@ def tile_list_tutor_progress_matching_kernel(
         h_empty(range(per_chunk))
         h_quantise(0, 0, CHUNK)
         v2_gather(0)
-        e_slices(0, 0)
+        e_fills(0, 4)
         v2_gather(1)
         nc.gpsimd.tensor_scalar(
             mix_bf[1][:], mix_rows[1][:].rearrange("p t c -> p c t"), 1.0, 0.0, ALU.mult, ALU.add
         )
         h_empty(range(per_chunk, 2 * per_chunk))
-        e_slices(0, 1)
+        e_fills(4, 8)
         mix_quantise(0)
         h_quantise(1, 0, CHUNK)
-        e_slices(1, 0)
-        e_slices(1, 1)
+        e_fills(8, 16)
 
         def y_open(c, lo, hi, groups):
             js = slice(c * CHUNK + lo, c * CHUNK + hi)
@@ -337,6 +343,7 @@ def tile_list_tutor_progress_matching_kernel(
                 queue.dma_start(out_view[:, tiles[0] : tiles[-1] + 1, c * CHUNK + lo : c * CHUNK + hi], res[:])
 
         first = y_open(0, 0, CHUNK, ((3, (0,)), (4, (1,)), (5, (2,))))
+        second = y_open(1, 0, HALF, ((6, (0, 1)), (7, (2,))))
         z_weave(0, 0, 0, CHUNK)
         mix_quantise(1)
         z_quantise(0, 0, 0, CHUNK)
@@ -346,20 +353,19 @@ def tile_list_tutor_progress_matching_kernel(
         z_quantise(0, 1, 0, CHUNK)
         y_mix(first, 1)
         y_out(first)
-        second = y_open(1, 0, HALF, ((6, (0, 1)), (7, (2,))))
-        third = y_open(1, HALF, CHUNK, ((0, (0,)), (1, (1,)), (2, (2,))))
-        z_weave(1, 0, HALF, CHUNK)
+        third = y_open(1, HALF, CHUNK, ((1, (0,)), (2, (1,)), (0, (2,))))
+        z_weave(1, 1, 0, HALF)
         z_quantise(1, 0, 0, HALF)
         y_mix(second, 0)
-        z_weave(1, 1, 0, HALF)
-        z_quantise(1, 0, HALF, CHUNK)
+        z_weave(1, 0, HALF, CHUNK)
         z_quantise(1, 1, 0, HALF)
         y_mix(second, 1)
         y_out(second)
-        y_mix(third, 0)
         ends = ((HALF, HALF + BLOCK), (HALF + BLOCK, CHUNK))
-        for part in ends:
-            z_weave(1, 1, *part)
+        z_weave(1, 1, *ends[0])
+        z_quantise(1, 0, HALF, CHUNK)
+        y_mix(third, 0)
+        z_weave(1, 1, *ends[1])
         for part in ends:
             z_quantise(1, 1, *part)
             y_mix(third, 1, part)

@@ -29,8 +29,9 @@ CHUNK = 512
 CHUNKS = S // CHUNK
 HALF = CHUNK // 2
 BLOCK = 128
+MIX_POOL = 304
 WQ_SPLIT = 44
-E_TURNS = (0, 1, 2, 3, 4, 5, 6, 7) + (0, 1, 2, 7) + (0, 1, 2, 0)
+E_TURNS = (4, 5, 6, 7) * 3 + (4, 5, 6, 4)
 
 
 def tile_list_tutor_progress_matching_kernel(
@@ -39,6 +40,7 @@ def tile_list_tutor_progress_matching_kernel(
     nc = tc.nc
     with ExitStack() as ctx:
         held = ctx.enter_context(tc.tile_pool(name="held", bufs=1))
+        first_tab = ctx.enter_context(tc.tile_pool(name="first_tab", bufs=1))
         later = ctx.enter_context(tc.tile_pool(name="later", bufs=1))
         shared = ctx.enter_context(tc.tile_pool(name="shared", bufs=1))
         psum = ctx.enter_context(tc.psum_pool(name="psum", bufs=1))
@@ -64,17 +66,16 @@ def tile_list_tutor_progress_matching_kernel(
         idx = held.tile([P, S // LIST_ROWS], U16, name="idx")
         idx2 = held.tile([P, S2 // LIST_ROWS], U16, name="idx2")
         v_scale_win = sb([P, T], U8, "v_scale_win", tag="reuse_a")
-        v2_scale_win = sb([P, T2], U8, "v2_scale_win", tag="reuse_b")
-        v_word_win0 = sb([P, T], I32, "v_word_win0", tag="reuse_c")
+        v2_scale_win = sb([P, T2], U8, "v2_scale_win")
+        v_word_win0 = first_tab.tile([P, T], I32, name="v_word_win0", align_bytes=64, offset=0)
+        v_word_win1 = sb([P, T], I32, "v_word_win1")
         wq_raw0 = later.tile([P, PACK, H], F32, name="wq_raw0", align_bytes=64, offset=0)
         v_planes = sb([P, PASSES, S], U8, "v_planes")
-        v2_plane = sb([P, S2], U8, "v2_plane")
 
         nc.vector.memset(v2_scale_win[:].bitcast(I32), 0)
         nc.vector.memset(v_scale_win[QUAD : 2 * QUAD, :].bitcast(I32), 0)
         nc.vector.memset(v_scale_win[2 * QUAD : P, :].bitcast(I32), 0)
         nc.vector.memset(v_planes[:].bitcast(I32), 0)
-        nc.vector.memset(v2_plane[:].bitcast(I32), 0)
 
         wq_view = wq.rearrange("(a p i) r -> a p i r", a=PASSES, i=PACK)
         mix_view = mix.rearrange("(a p i) n -> a p i n", a=PASSES, i=PACK)
@@ -91,6 +92,7 @@ def tile_list_tutor_progress_matching_kernel(
         make_identity(nc, identity[:])
         nc.sync.dma_start(vec_rows[0:PASSES, :], gain.rearrange("(a x) -> a x", a=PASSES))
         nc.sync.dma_start(vec_rows[PASSES : PASSES + 1, :], bq.unsqueeze(0))
+        nc.sync.dma_start(v_word_win1[:], words_of(tab_words, 1))
 
         v_scale_rows = sb([P, S], U8, "v_scale_rows")
         nc.vector.tensor_copy(v_scale_rows[:], v_scale_win[:].indirect(idx[:]))
@@ -99,21 +101,14 @@ def tile_list_tutor_progress_matching_kernel(
                 v_planes[QUAD * q : QUAD * q + 4, :, :].bitcast(I32),
                 v_scale_rows[8 * q : 8 * q + 8, :].bitcast(I32),
             )
-        v_word_win1 = sb([P, T], I32, "v_word_win1", tag="reuse_a")
-        nc.sync.dma_start(v_word_win1[:], words_of(tab_words, 1))
+        wq_raw1 = sb([P, PACK, H], F32, "wq_raw1", tag="reuse_a")
+        nc.sync.dma_start(wq_raw1[:], wq_view[1])
 
         v2_scale_rows = sb([P, S2], U8, "v2_scale_rows")
         nc.vector.tensor_copy(
             v2_scale_rows[:].rearrange("p (a i s) -> p a s i", a=PASSES, i=PACK), v2_scale_win[:].indirect(idx2[:])
         )
 
-        wq_raw1 = sb([P, PACK, H], F32, "wq_raw1", tag="reuse_b")
-        nc.sync.dma_start(wq_raw1[:], wq_view[1])
-        for q in QUAD_ORDER:
-            nc.sync.dma_start(
-                v2_plane[QUAD * q : QUAD * q + 4, :].bitcast(I32),
-                v2_scale_rows[QUAD * q : QUAD * (q + 1) : 8, :].bitcast(I32),
-            )
 
         turned = bank(0, [P, PACK, P])
         for t in range(PACK):
@@ -130,9 +125,16 @@ def tile_list_tutor_progress_matching_kernel(
 
         v_words = [sb([P, S], U32, "v_words%d" % a) for a in range(PASSES)]
         nc.vector.tensor_copy(v_words[0][:], v_word_win0[:].bitcast(U32).indirect(idx[:]))
-        mix_raw = sb([P, PASSES, PACK, N], F32, "mix_raw", tag="reuse_c")
+        mix_raw = first_tab.tile([P, PASSES, PACK, N], F32, name="mix_raw", align_bytes=64, offset=0)
+        v2_plane = first_tab.tile([P, S2], U8, name="v2_plane", align_bytes=64, offset=4 * PASSES * PACK * N)
         for a in range(PASSES):
             nc.sync.dma_start(mix_raw[:, a, :, :], mix_view[a])
+        nc.vector.memset(v2_plane[:].bitcast(I32), 0)
+        for q in QUAD_ORDER:
+            nc.sync.dma_start(
+                v2_plane[QUAD * q : QUAD * q + 4, :].bitcast(I32),
+                v2_scale_rows[QUAD * q : QUAD * (q + 1) : 8, :].bitcast(I32),
+            )
 
         wq_bf = [
             shared.tile([P, PACK, P, PACK], BF16, name="wq_bf0", align_bytes=64, offset=0),
@@ -174,17 +176,21 @@ def tile_list_tutor_progress_matching_kernel(
         wq_quantise(1, 0, PACK // 2)
         wq_quantise(1, PACK // 2, PACK)
 
-        h_bf = [
-            sb([P, CHUNK, PACK], BF16, "h_bf0"),
-            later.tile([P, CHUNK, PACK], BF16, name="h_bf1", align_bytes=64, offset=0),
-        ]
+        h_first = sb([P, CHUNK, PACK], BF16, "h_first")
+        h_fifth = sb([P, BLOCK, PACK], BF16, "h_fifth")
+        h_last = later.tile([P, CHUNK - BLOCK, PACK], BF16, name="h_last", align_bytes=64, offset=0)
         h_codes = [sb([P, CHUNK], U32, "h_codes%d" % c) for c in range(CHUNKS)]
-        h_planes = [sb([P, CHUNK], U8, "h_planes%d" % c) for c in range(CHUNKS)]
-        h_accs = [bank(b, [P, PACK, BLOCK]) for b in range(S // BLOCK)]
+        h_planes = [
+            sb([P, CHUNK], U8, "h_planes0"),
+            later.tile([P, CHUNK], U8, name="h_planes1", align_bytes=64, offset=2 * (CHUNK - BLOCK) * PACK),
+        ]
         per_chunk = CHUNK // BLOCK
+        h_accs = {}
 
-        def h_passes(a):
-            for b in range(S // BLOCK):
+        def h_passes(a, blocks):
+            for b in blocks:
+                if a == 0:
+                    h_accs[b] = bank(b % per_chunk, [P, PACK, BLOCK])
                 for t in range(PACK):
                     nc.tensor.matmul_mx(
                         h_accs[b][:, t, :],
@@ -197,7 +203,9 @@ def tile_list_tutor_progress_matching_kernel(
                     )
 
         def h_woven(c, lo, hi):
-            return h_bf[c][:, lo:hi, :]
+            if c == 0:
+                return h_first[:, lo:hi, :]
+            return h_fifth[:] if lo == 0 else h_last[:, lo - BLOCK : hi - BLOCK, :]
 
         def h_empty(blocks):
             for b in blocks:
@@ -281,20 +289,24 @@ def tile_list_tutor_progress_matching_kernel(
         def z_quantise(c, a, lo, hi):
             quantise(z_codes[c][a][:, lo:hi], z_planes[c][a][:, lo:hi], z_bf[c][a][:, lo:hi, :])
 
-        h_passes(0)
-        h_passes(1)
-        h_empty(range(per_chunk))
+        h_passes(0, range(per_chunk))
+        h_passes(1, range(per_chunk))
+        for b in range(per_chunk):
+            h_empty((b,))
+            h_passes(0, (per_chunk + b,))
+            h_passes(1, (per_chunk + b,))
+        h_empty((per_chunk,))
         h_quantise(0, 0, CHUNK)
         v2_gather(0)
         e_fills(0, 4)
         v2_gather(1)
-        nc.gpsimd.tensor_scalar(
-            mix_bf[1][:], mix_rows[1][:].rearrange("p t c -> p c t"), 1.0, 0.0, ALU.mult, ALU.add
-        )
-        h_empty(range(per_chunk, 2 * per_chunk))
+        rows = mix_rows[1][:, :, 0:MIX_POOL].rearrange("p t c -> p c t")
+        nc.gpsimd.tensor_scalar(mix_bf[1][:, 0:MIX_POOL, :], rows, 1.0, 0.0, ALU.mult, ALU.add)
+        h_empty(range(per_chunk + 1, 2 * per_chunk))
         e_fills(4, 8)
-        mix_quantise(0)
-        h_quantise(1, 0, CHUNK)
+        h_quantise(1, 0, BLOCK)
+        nc.vector.tensor_copy(*weave_views(mix_bf[1][:, MIX_POOL:N, :], mix_rows[1][:, :, MIX_POOL:N]))
+        h_quantise(1, BLOCK, CHUNK)
         e_fills(8, 16)
 
         def y_open(c, lo, hi, groups):
@@ -342,18 +354,19 @@ def tile_list_tutor_progress_matching_kernel(
                 queue = last_queue if tiles[-1] == N // P - 1 else nc.sync
                 queue.dma_start(out_view[:, tiles[0] : tiles[-1] + 1, c * CHUNK + lo : c * CHUNK + hi], res[:])
 
-        first = y_open(0, 0, CHUNK, ((3, (0,)), (4, (1,)), (5, (2,))))
-        second = y_open(1, 0, HALF, ((6, (0, 1)), (7, (2,))))
+        first = y_open(0, 0, CHUNK, ((0, (0,)), (1, (1,)), (2, (2,))))
+        second = y_open(1, 0, HALF, ((3, (0, 1)), (7, (2,))))
         z_weave(0, 0, 0, CHUNK)
-        mix_quantise(1)
+        mix_quantise(0)
         z_quantise(0, 0, 0, CHUNK)
         y_mix(first, 0)
         z_weave(0, 1, 0, CHUNK)
-        z_weave(1, 0, 0, HALF)
+        mix_quantise(1)
         z_quantise(0, 1, 0, CHUNK)
         y_mix(first, 1)
         y_out(first)
-        third = y_open(1, HALF, CHUNK, ((1, (0,)), (2, (1,)), (0, (2,))))
+        third = y_open(1, HALF, CHUNK, ((5, (0,)), (6, (1,)), (4, (2,))))
+        z_weave(1, 0, 0, HALF)
         z_weave(1, 1, 0, HALF)
         z_quantise(1, 0, 0, HALF)
         y_mix(second, 0)

@@ -82,9 +82,9 @@ def tile_list_tutor_progress_matching_kernel(
 
         nc.sync.dma_start(idx[:], offs)
         nc.sync.dma_start(v_scale_win[0:QUAD, :].bitcast(I32), tab_scales.rearrange("a q x -> q a x").bitcast(I32))
+        nc.sync.dma_start(v_word_win0[:], words_of(tab_words, 0))
         nc.sync.dma_start(idx2[:], offs2)
         nc.sync.dma_start(v2_scale_win[0:P:8, :].bitcast(I32), tab2_scales[0].bitcast(I32))
-        nc.sync.dma_start(v_word_win0[:], words_of(tab_words, 0))
         nc.sync.dma_start(wq_raw0[:], wq_view[0])
         vec_rows = sb([P, PACK * P], F32, "vec_rows")
         identity = sb([P, P], F32, "identity")
@@ -328,31 +328,29 @@ def tile_list_tutor_progress_matching_kernel(
                 accs.append((acc, tiles))
             return c, lo, hi, accs
 
-        def y_mix(piece, a, part=None):
-            c, base, end, accs = piece
-            lo, hi = part or (base, end)
+        def y_mix(piece, a):
+            c, lo, hi, accs = piece
             for acc, tiles in accs:
                 for place, n in enumerate(tiles):
                     ns = slice(a * N + n * P, a * N + (n + 1) * P)
                     nc.tensor.matmul_mx(
-                        acc[:, place, lo - base : hi - base],
+                        acc[:, place, :],
                         lhsT=mix_codes[:, ns].bitcast(FP8X4),
                         lhsT_scale=mix_planes[:, ns],
                         rhs=z_codes[c][a][:, lo:hi].bitcast(FP8X4),
                         rhs_scale=z_planes[c][a][:, lo:hi],
                         start=False,
-                        stop=(a == PASSES - 1 and place == len(tiles) - 1 and hi == end),
+                        stop=(a == PASSES - 1 and place == len(tiles) - 1),
                     )
 
         out_view = out.rearrange("(n p) j -> p n j", p=P)
 
-        def y_out(piece, last_queue=nc.sync):
+        def y_out(piece):
             c, lo, hi, accs = piece
             for acc, tiles in accs:
                 res = sb([P, len(tiles), hi - lo], F32, "res%d_%d_%d" % (c, lo, tiles[0]))
                 nc.scalar.activation(out=res[:], in_=acc[:], func=ACT.Tanh)
-                queue = last_queue if tiles[-1] == N // P - 1 else nc.sync
-                queue.dma_start(out_view[:, tiles[0] : tiles[-1] + 1, c * CHUNK + lo : c * CHUNK + hi], res[:])
+                nc.sync.dma_start(out_view[:, tiles[0] : tiles[-1] + 1, c * CHUNK + lo : c * CHUNK + hi], res[:])
 
         first = y_open(0, 0, CHUNK, ((0, (0,)), (1, (1,)), (2, (2,))))
         second = y_open(1, 0, HALF, ((3, (0, 1)), (7, (2,))))
@@ -365,7 +363,9 @@ def tile_list_tutor_progress_matching_kernel(
         z_quantise(0, 1, 0, CHUNK)
         y_mix(first, 1)
         y_out(first)
-        third = y_open(1, HALF, CHUNK, ((5, (0,)), (6, (1,)), (4, (2,))))
+        ends = ((HALF, HALF + BLOCK), (HALF + BLOCK, CHUNK))
+        tiles = tuple(range(N // P))
+        lasts = [y_open(1, lo, hi, ((number, tiles),)) for (lo, hi), number in zip(ends, (5, 6))]
         z_weave(1, 0, 0, HALF)
         z_weave(1, 1, 0, HALF)
         z_quantise(1, 0, 0, HALF)
@@ -374,12 +374,17 @@ def tile_list_tutor_progress_matching_kernel(
         z_quantise(1, 1, 0, HALF)
         y_mix(second, 1)
         y_out(second)
-        ends = ((HALF, HALF + BLOCK), (HALF + BLOCK, CHUNK))
         z_weave(1, 1, *ends[0])
         z_quantise(1, 0, HALF, CHUNK)
-        y_mix(third, 0)
+        for piece in lasts:
+            y_mix(piece, 0)
         z_weave(1, 1, *ends[1])
-        for part in ends:
+        for part, piece in zip(ends, lasts):
             z_quantise(1, 1, *part)
-            y_mix(third, 1, part)
-        y_out(third, nc.scalar)
+            y_mix(piece, 1)
+        res = sb([P, len(tiles), HALF], F32, "res_last")
+        nc.scalar.activation(out=res[:, :, 0:BLOCK], in_=lasts[0][3][0][0][:], func=ACT.Tanh)
+        for n in tiles:
+            nc.scalar.activation(out=res[:, n, BLOCK:HALF], in_=lasts[1][3][0][0][:, n, :], func=ACT.Tanh)
+            queue = nc.scalar if n == tiles[-1] else nc.sync
+            queue.dma_start(out_view[:, n, CHUNK + HALF : S], res[:, n, :])

@@ -42,7 +42,7 @@ def tile_list_tutor_progress_matching_kernel(
         held = ctx.enter_context(tc.tile_pool(name="held", bufs=1))
         first_tab = ctx.enter_context(tc.tile_pool(name="first_tab", bufs=1))
         later = ctx.enter_context(tc.tile_pool(name="later", bufs=1))
-        shared = ctx.enter_context(tc.tile_pool(name="shared", bufs=1))
+        second_wq = ctx.enter_context(tc.tile_pool(name="second_wq", bufs=1))
         psum = ctx.enter_context(tc.psum_pool(name="psum", bufs=1))
 
         def sb(shape, dtype, name, tag=None):
@@ -65,27 +65,26 @@ def tile_list_tutor_progress_matching_kernel(
 
         idx = held.tile([P, S // LIST_ROWS], U16, name="idx")
         idx2 = held.tile([P, S2 // LIST_ROWS], U16, name="idx2")
-        v_scale_win = sb([P, T], U8, "v_scale_win", tag="reuse_a")
+        v_scale_win = second_wq.tile([P, T], U8, name="v_scale_win", align_bytes=64, offset=0)
         v2_scale_win = sb([P, T2], U8, "v2_scale_win")
         v_word_win0 = first_tab.tile([P, T], I32, name="v_word_win0", align_bytes=64, offset=0)
         v_word_win1 = sb([P, T], I32, "v_word_win1")
-        wq_raw0 = later.tile([P, PACK, H], F32, name="wq_raw0", align_bytes=64, offset=0)
+        wq_raw0 = sb([P, PACK, H], F32, "wq_raw0")
         v_planes = sb([P, PASSES, S], U8, "v_planes")
 
+        nc.vector.memset(v_scale_win[:].bitcast(I32), 0)
         nc.vector.memset(v2_scale_win[:].bitcast(I32), 0)
-        nc.vector.memset(v_scale_win[QUAD : 2 * QUAD, :].bitcast(I32), 0)
-        nc.vector.memset(v_scale_win[2 * QUAD : P, :].bitcast(I32), 0)
         nc.vector.memset(v_planes[:].bitcast(I32), 0)
 
         wq_view = wq.rearrange("(a p i) r -> a p i r", a=PASSES, i=PACK)
         mix_view = mix.rearrange("(a p i) n -> a p i n", a=PASSES, i=PACK)
 
-        nc.sync.dma_start(idx[:], offs)
-        nc.sync.dma_start(v_scale_win[0:QUAD, :].bitcast(I32), tab_scales.rearrange("a q x -> q a x").bitcast(I32))
-        nc.sync.dma_start(v_word_win0[:], words_of(tab_words, 0))
-        nc.sync.dma_start(idx2[:], offs2)
-        nc.sync.dma_start(v2_scale_win[0:P:8, :].bitcast(I32), tab2_scales[0].bitcast(I32))
         nc.sync.dma_start(wq_raw0[:], wq_view[0])
+        nc.sync.dma_start(idx[:], offs)
+        nc.sync.dma_start(idx2[:], offs2)
+        nc.sync.dma_start(v_scale_win[0:P:4, :].bitcast(I32), tab_scales.rearrange("a q x -> q a x").bitcast(I32))
+        nc.sync.dma_start(v2_scale_win[0:P:8, :].bitcast(I32), tab2_scales[0].bitcast(I32))
+        nc.sync.dma_start(v_word_win0[:], words_of(tab_words, 0))
         vec_rows = sb([P, PACK * P], F32, "vec_rows")
         identity = sb([P, P], F32, "identity")
         nc.gpsimd.memset(vec_rows[:], 0.0)
@@ -94,14 +93,14 @@ def tile_list_tutor_progress_matching_kernel(
         nc.sync.dma_start(vec_rows[PASSES : PASSES + 1, :], bq.unsqueeze(0))
         nc.sync.dma_start(v_word_win1[:], words_of(tab_words, 1))
 
-        v_scale_rows = sb([P, S], U8, "v_scale_rows")
+        v_scale_rows = later.tile([P, S], U8, name="v_scale_rows", align_bytes=64, offset=0)
         nc.vector.tensor_copy(v_scale_rows[:], v_scale_win[:].indirect(idx[:]))
         for q in QUAD_ORDER:
             nc.sync.dma_start(
                 v_planes[QUAD * q : QUAD * q + 4, :, :].bitcast(I32),
-                v_scale_rows[8 * q : 8 * q + 8, :].bitcast(I32),
+                v_scale_rows[QUAD * q : QUAD * (q + 1) : 4, :].bitcast(I32),
             )
-        wq_raw1 = sb([P, PACK, H], F32, "wq_raw1", tag="reuse_a")
+        wq_raw1 = second_wq.tile([P, PACK, H], F32, name="wq_raw1", align_bytes=64, offset=0)
         nc.sync.dma_start(wq_raw1[:], wq_view[1])
 
         v2_scale_rows = sb([P, S2], U8, "v2_scale_rows")
@@ -137,7 +136,7 @@ def tile_list_tutor_progress_matching_kernel(
             )
 
         wq_bf = [
-            shared.tile([P, PACK, P, PACK], BF16, name="wq_bf0", align_bytes=64, offset=0),
+            sb([P, PACK, P, PACK], BF16, "wq_bf0"),
             sb([P, PACK, P, PACK], BF16, "wq_bf1"),
         ]
         wq_codes = sb([P, PASSES, H], U32, "wq_codes")
@@ -156,12 +155,18 @@ def tile_list_tutor_progress_matching_kernel(
             quantise(wq_codes[:, a, cols], wq_planes[:, a, cols], woven)
 
         nc.scalar.copy(*wq_views(0, wq_raw0[:], 0))
-        v2_word_win = later.tile([P, T2], I32, name="v2_word_win", align_bytes=64, offset=0)
-        nc.sync.dma_start(v2_word_win[:], words_of(tab2_words, 0))
         wq_quantise(0, 0, PACK)
 
-        wd_planes = shared.tile([P, PASSES, N], U8, name="wd_planes", align_bytes=64, offset=S2)
-        wd_codes = shared.tile([P, PASSES, 2 * N], U8, name="wd_codes", align_bytes=64, offset=2 * S2)
+        nc.vector.tensor_copy(v_words[1][:], v_word_win1[:].bitcast(U32).indirect(idx[:]))
+        v2_word_win = later.tile([P, T2], I32, name="v2_word_win", align_bytes=64, offset=0)
+        nc.sync.dma_start(v2_word_win[:], words_of(tab2_words, 0))
+        nc.scalar.copy(*wq_views(1, wq_raw1[:, :, 0 : PACK * WQ_SPLIT], 0))
+        nc.vector.tensor_copy(*wq_views(1, wq_raw1[:, :, PACK * WQ_SPLIT : H], WQ_SPLIT))
+        wq_quantise(1, 0, PACK // 2)
+        wq_quantise(1, PACK // 2, PACK)
+
+        wd_planes = second_wq.tile([P, PASSES, N], U8, name="wd_planes", align_bytes=64, offset=0)
+        wd_codes = second_wq.tile([P, PASSES, 2 * N], U8, name="wd_codes", align_bytes=64, offset=PASSES * N)
         nc.vector.memset(wd_planes[:].bitcast(I32), 0)
         nc.sync.dma_start(wd_codes[:].bitcast(I32), wd_words.rearrange("a p c -> p a c").bitcast(I32))
         for q in QUAD_ORDER:
@@ -169,12 +174,6 @@ def tile_list_tutor_progress_matching_kernel(
                 wd_planes[QUAD * q : QUAD * q + 4, :, :].bitcast(I32),
                 wd_scales[:, 4 * q : 4 * q + 4, :].rearrange("a r c -> r a c").bitcast(I32),
             )
-
-        nc.vector.tensor_copy(v_words[1][:], v_word_win1[:].bitcast(U32).indirect(idx[:]))
-        nc.scalar.copy(*wq_views(1, wq_raw1[:, :, 0 : PACK * WQ_SPLIT], 0))
-        nc.vector.tensor_copy(*wq_views(1, wq_raw1[:, :, PACK * WQ_SPLIT : H], WQ_SPLIT))
-        wq_quantise(1, 0, PACK // 2)
-        wq_quantise(1, PACK // 2, PACK)
 
         h_first = sb([P, CHUNK, PACK], BF16, "h_first")
         h_fifth = sb([P, BLOCK, PACK], BF16, "h_fifth")

@@ -57,6 +57,9 @@ def tile_list_tutor_progress_matching_kernel(
         def quantise(codes, plane, woven):
             nc.vector.quantize_mx(codes.bitcast(FP8X4), plane, woven.rearrange("p c t -> p (c t)"))
 
+        def weave(woven, slices):
+            nc.vector.tensor_copy(woven, slices.rearrange("p t c -> p c t"))
+
         def weave_views(woven, slices):
             return (
                 woven.rearrange("p (c i) t -> p c t i", i=4),
@@ -283,7 +286,7 @@ def tile_list_tutor_progress_matching_kernel(
                 e_bank(E_TURNS[turn], *fills[turn])
 
         def z_weave(c, a, lo, hi):
-            nc.vector.tensor_copy(*weave_views(z_bf[c][a][:, lo:hi, :], z_rows[c][a][:, :, lo:hi]))
+            weave(z_bf[c][a][:, lo:hi, :], z_rows[c][a][:, :, lo:hi])
 
         def z_quantise(c, a, lo, hi):
             quantise(z_codes[c][a][:, lo:hi], z_planes[c][a][:, lo:hi], z_bf[c][a][:, lo:hi, :])
@@ -304,7 +307,7 @@ def tile_list_tutor_progress_matching_kernel(
         h_empty(range(per_chunk + 1, 2 * per_chunk))
         e_fills(4, 8)
         h_quantise(1, 0, BLOCK)
-        nc.vector.tensor_copy(*weave_views(mix_bf[1][:, MIX_POOL:N, :], mix_rows[1][:, :, MIX_POOL:N]))
+        weave(mix_bf[1][:, MIX_POOL:N, :], mix_rows[1][:, :, MIX_POOL:N])
         h_quantise(1, BLOCK, CHUNK)
         e_fills(8, 16)
 

@@ -24,13 +24,14 @@ PASS = P * PACK
 QUADS = 4
 QUAD = P // QUADS
 QUAD_ORDER = (0, 2, 1, 3)
+V2_ROW = 8
 LIST_ROWS = 16
 CHUNK = 512
 CHUNKS = S // CHUNK
 HALF = CHUNK // 2
 BLOCK = 128
 MIX_POOL = 304
-WQ_SPLIT = 44
+WQ_SPLIT = 104
 E_TURNS = (4, 5, 6, 7) * 3 + (4, 5, 6, 4)
 
 
@@ -134,7 +135,7 @@ def tile_list_tutor_progress_matching_kernel(
         nc.vector.memset(v2_plane[:].bitcast(I32), 0)
         for q in QUAD_ORDER:
             nc.sync.dma_start(
-                v2_plane[QUAD * q : QUAD * q + 4, :].bitcast(I32),
+                v2_plane[QUAD * q + V2_ROW : QUAD * q + V2_ROW + 4, :].bitcast(I32),
                 v2_scale_rows[QUAD * q : QUAD * (q + 1) : 8, :].bitcast(I32),
             )
 
@@ -145,11 +146,11 @@ def tile_list_tutor_progress_matching_kernel(
         wq_codes = sb([P, PASSES, H], U32, "wq_codes")
         wq_planes = sb([P, PASSES, H], U8, "wq_planes")
 
-        def wq_views(a, raw, s0):
+        def wq_views(a, raw, s0, t0=0, t1=PACK):
             count = raw.shape[2] // PACK
             return (
-                wq_bf[a][:, :, s0 : s0 + count, :].rearrange("p t s i -> p s i t"),
-                raw.rearrange("p i (s t) -> p s i t", t=PACK),
+                wq_bf[a][:, t0:t1, s0 : s0 + count, :].rearrange("p t s i -> p s i t"),
+                raw.rearrange("p i (s t) -> p s i t", t=PACK)[:, :, :, t0:t1],
             )
 
         def wq_quantise(a, t0, t1):
@@ -163,8 +164,9 @@ def tile_list_tutor_progress_matching_kernel(
         nc.vector.tensor_copy(v_words[1][:], v_word_win1[:].bitcast(U32).indirect(idx[:]))
         v2_word_win = later.tile([P, T2], I32, name="v2_word_win", align_bytes=64, offset=0)
         nc.sync.dma_start(v2_word_win[:], words_of(tab2_words, 0))
-        nc.scalar.copy(*wq_views(1, wq_raw1[:, :, 0 : PACK * WQ_SPLIT], 0))
-        nc.vector.tensor_copy(*wq_views(1, wq_raw1[:, :, PACK * WQ_SPLIT : H], WQ_SPLIT))
+        nc.scalar.copy(*wq_views(1, wq_raw1[:, :, 0 : PACK * WQ_SPLIT], 0, PACK // 2, PACK))
+        nc.vector.tensor_copy(*wq_views(1, wq_raw1[:], 0, 0, PACK // 2))
+        nc.vector.tensor_copy(*wq_views(1, wq_raw1[:, :, PACK * WQ_SPLIT : H], WQ_SPLIT, PACK // 2, PACK))
         wq_quantise(1, 0, PACK // 2)
         wq_quantise(1, PACK // 2, PACK)
 
@@ -266,7 +268,7 @@ def tile_list_tutor_progress_matching_kernel(
                 nc.tensor.matmul_mx(
                     acc[:, place, :],
                     lhsT=v2_words[a][:, t * P : (t + 1) * P].bitcast(FP8X4),
-                    lhsT_scale=v2_plane[:, col * P : (col + 1) * P],
+                    lhsT_scale=v2_plane[V2_ROW:P, col * P : (col + 1) * P],
                     rhs=h_codes[c][:, lo:hi].bitcast(FP8X4),
                     rhs_scale=h_planes[c][:, lo:hi],
                     start=True,

@@ -31,6 +31,7 @@ CHUNKS = S // CHUNK
 HALF = CHUNK // 2
 BLOCK = 128
 MIX_POOL = 304
+MIX_AHEAD = 96
 WQ_SPLIT = 104
 E_TURNS = (4, 5, 6, 7) * 3 + (4, 5, 6, 4)
 
@@ -239,7 +240,7 @@ def tile_list_tutor_progress_matching_kernel(
                 nc.scalar.activation(
                     out=mix_rows[a][:, t, :], in_=mix_raw[:, a, t, :], func=ACT.Copy, scale=gain_sign[:, col : col + 1]
                 )
-        nc.scalar.copy(*weave_views(mix_bf[0][:], mix_rows[0][:]))
+        nc.scalar.copy(*weave_views(mix_bf[0][:, MIX_AHEAD:N, :], mix_rows[0][:, :, MIX_AHEAD:N]))
 
         def mix_quantise(a):
             quantise(mix_codes[:, a * N : (a + 1) * N], mix_planes[:, a * N : (a + 1) * N], mix_bf[a][:])
@@ -301,6 +302,7 @@ def tile_list_tutor_progress_matching_kernel(
             h_passes(1, (per_chunk + b,))
         h_empty((per_chunk,))
         h_quantise(0, 0, CHUNK)
+        weave(mix_bf[0][:, 0:MIX_AHEAD, :], mix_rows[0][:, :, 0:MIX_AHEAD])
         v2_gather(0)
         e_fills(0, 4)
         v2_gather(1)

@@ -30,10 +30,10 @@ CHUNK = 512
 CHUNKS = S // CHUNK
 HALF = CHUNK // 2
 BLOCK = 128
-MIX_POOL = 304
-MIX_AHEAD = 96
+MIX_AHEAD = 256
 WQ_SPLIT = 104
-E_TURNS = (4, 5, 6, 7) * 3 + (4, 5, 6, 4)
+E_TURNS = (0, 5, 6, 7) * 3 + (0, 5, 6, 0)
+H_BANKS = (0, 1, 2, 3, 4, 2, 3, 4)
 
 
 def tile_list_tutor_progress_matching_kernel(
@@ -195,7 +195,7 @@ def tile_list_tutor_progress_matching_kernel(
         def h_passes(a, blocks):
             for b in blocks:
                 if a == 0:
-                    h_accs[b] = bank(b % per_chunk, [P, PACK, BLOCK])
+                    h_accs[b] = bank(H_BANKS[b], [P, PACK, BLOCK])
                 for t in range(PACK):
                     nc.tensor.matmul_mx(
                         h_accs[b][:, t, :],
@@ -226,24 +226,32 @@ def tile_list_tutor_progress_matching_kernel(
             quantise(h_codes[c][:, lo:hi], h_planes[c][:, lo:hi], h_woven(c, lo, hi))
 
         mix_rows = [sb([P, PACK, N], BF16, "mix_rows%d" % a) for a in range(PASSES)]
-        mix_bf = [
-            sb([P, N, PACK], BF16, "mix_bf0"),
-            later.tile([P, N, PACK], BF16, name="mix_bf1", align_bytes=64, offset=2 * CHUNK * PACK),
-        ]
+        mix_ahead = sb([P, MIX_AHEAD, PACK], BF16, "mix_ahead")
+        ahead_codes = sb([P, MIX_AHEAD], U32, "ahead_codes")
         mix_codes = later.tile(
-            [P, PASSES * N], U32, name="mix_codes", align_bytes=64, offset=2 * (CHUNK + N) * PACK
+            [P, PASSES * N - MIX_AHEAD], U32, name="mix_codes", align_bytes=64, offset=2 * (CHUNK + N) * PACK
         )
         mix_planes = sb([P, PASSES * N], U8, "mix_planes")
-        for a in range(PASSES):
+
+        def mix_sign(a):
             for t in range(PACK):
                 col = a * PACK + t
                 nc.scalar.activation(
                     out=mix_rows[a][:, t, :], in_=mix_raw[:, a, t, :], func=ACT.Copy, scale=gain_sign[:, col : col + 1]
                 )
-        nc.scalar.copy(*weave_views(mix_bf[0][:, MIX_AHEAD:N, :], mix_rows[0][:, :, MIX_AHEAD:N]))
 
-        def mix_quantise(a):
-            quantise(mix_codes[:, a * N : (a + 1) * N], mix_planes[:, a * N : (a + 1) * N], mix_bf[a][:])
+        mix_sign(0)
+        nc.scalar.copy(*weave_views(mix_ahead[:], mix_rows[0][:, :, 0:MIX_AHEAD]))
+        mix_sign(1)
+
+        def mix_words(lo, hi):
+            return ahead_codes[:, lo:hi] if hi <= MIX_AHEAD else mix_codes[:, lo - MIX_AHEAD : hi - MIX_AHEAD]
+
+        def mix_quantise(lo, hi, woven):
+            quantise(mix_words(lo, hi), mix_planes[:, lo:hi], woven[:])
+
+        def pool_weave(woven, slices):
+            nc.gpsimd.tensor_scalar(woven, slices.rearrange("p t c -> p c t"), 1.0, 0.0, ALU.mult, ALU.add)
 
         v2_words = [sb([P, PASS], U32, "v2_words%d" % a) for a in range(PASSES)]
         list_cols = PASS // LIST_ROWS
@@ -294,25 +302,26 @@ def tile_list_tutor_progress_matching_kernel(
         def z_quantise(c, a, lo, hi):
             quantise(z_codes[c][a][:, lo:hi], z_planes[c][a][:, lo:hi], z_bf[c][a][:, lo:hi, :])
 
-        h_passes(0, range(per_chunk))
-        h_passes(1, range(per_chunk))
-        for b in range(per_chunk):
+        h_passes(0, range(per_chunk + 1))
+        h_passes(1, range(per_chunk + 1))
+        h_empty((0, 1))
+        for b in range(2, per_chunk + 1):
             h_empty((b,))
-            h_passes(0, (per_chunk + b,))
-            h_passes(1, (per_chunk + b,))
-        h_empty((per_chunk,))
+            h_passes(0, (per_chunk + b - 1,))
+            h_passes(1, (per_chunk + b - 1,))
         h_quantise(0, 0, CHUNK)
-        weave(mix_bf[0][:, 0:MIX_AHEAD, :], mix_rows[0][:, :, 0:MIX_AHEAD])
+        mix_quantise(0, MIX_AHEAD, mix_ahead)
+        mix_rest = sb([P, PASSES * N - MIX_AHEAD, PACK], BF16, "mix_rest", tag="mix_ahead")
+        pool_weave(mix_rest[:, 0 : N - MIX_AHEAD, :], mix_rows[0][:, :, MIX_AHEAD:N])
         v2_gather(0)
         e_fills(0, 4)
         v2_gather(1)
-        rows = mix_rows[1][:, :, 0:MIX_POOL].rearrange("p t c -> p c t")
-        nc.gpsimd.tensor_scalar(mix_bf[1][:, 0:MIX_POOL, :], rows, 1.0, 0.0, ALU.mult, ALU.add)
+        pool_weave(mix_rest[:, N - MIX_AHEAD :, :], mix_rows[1][:])
         h_empty(range(per_chunk + 1, 2 * per_chunk))
         e_fills(4, 8)
         h_quantise(1, 0, BLOCK)
-        weave(mix_bf[1][:, MIX_POOL:N, :], mix_rows[1][:, :, MIX_POOL:N])
-        h_quantise(1, BLOCK, CHUNK)
+        h_quantise(1, BLOCK, CHUNK - BLOCK)
+        h_quantise(1, CHUNK - BLOCK, CHUNK)
         e_fills(8, 16)
 
         def y_open(c, lo, hi, groups):
@@ -341,7 +350,7 @@ def tile_list_tutor_progress_matching_kernel(
                     ns = slice(a * N + n * P, a * N + (n + 1) * P)
                     nc.tensor.matmul_mx(
                         acc[:, place, :],
-                        lhsT=mix_codes[:, ns].bitcast(FP8X4),
+                        lhsT=mix_words(ns.start, ns.stop).bitcast(FP8X4),
                         lhsT_scale=mix_planes[:, ns],
                         rhs=z_codes[c][a][:, lo:hi].bitcast(FP8X4),
                         rhs_scale=z_planes[c][a][:, lo:hi],
@@ -358,14 +367,13 @@ def tile_list_tutor_progress_matching_kernel(
                 nc.scalar.activation(out=res[:], in_=acc[:], func=ACT.Tanh)
                 nc.sync.dma_start(out_view[:, tiles[0] : tiles[-1] + 1, c * CHUNK + lo : c * CHUNK + hi], res[:])
 
-        first = y_open(0, 0, CHUNK, ((0, (0,)), (1, (1,)), (2, (2,))))
-        second = y_open(1, 0, HALF, ((3, (0, 1)), (7, (2,))))
+        first = y_open(0, 0, CHUNK, ((2, (0,)), (3, (1,)), (4, (2,))))
+        second = y_open(1, 0, HALF, ((1, (0, 1)), (7, (2,))))
         z_weave(0, 0, 0, CHUNK)
-        mix_quantise(0)
+        mix_quantise(MIX_AHEAD, PASSES * N, mix_rest)
         z_quantise(0, 0, 0, CHUNK)
         y_mix(first, 0)
         z_weave(0, 1, 0, CHUNK)
-        mix_quantise(1)
         z_quantise(0, 1, 0, CHUNK)
         y_mix(first, 1)
         y_out(first)

@@ -30,10 +30,10 @@ CHUNK = 512
 CHUNKS = S // CHUNK
 HALF = CHUNK // 2
 BLOCK = 128
-MIX_AHEAD = 256
+MIX_POOL = 2
 WQ_SPLIT = 104
 E_TURNS = (0, 5, 6, 7) * 3 + (0, 5, 6, 0)
-H_BANKS = (0, 1, 2, 3, 4, 2, 3, 4)
+H_BANKS = (0, 1, 2, 3, 4, 1, 2, 3)
 
 
 def tile_list_tutor_progress_matching_kernel(
@@ -45,6 +45,7 @@ def tile_list_tutor_progress_matching_kernel(
         first_tab = ctx.enter_context(tc.tile_pool(name="first_tab", bufs=1))
         later = ctx.enter_context(tc.tile_pool(name="later", bufs=1))
         second_wq = ctx.enter_context(tc.tile_pool(name="second_wq", bufs=1))
+        signs = ctx.enter_context(tc.tile_pool(name="signs", bufs=1))
         psum = ctx.enter_context(tc.psum_pool(name="psum", bufs=1))
 
         def sb(shape, dtype, name, tag=None):
@@ -124,15 +125,18 @@ def tile_list_tutor_progress_matching_kernel(
 
         gain_sign0 = sb([P, PASSES * PACK], F32, "gain_sign0")
         gain_sign = sb([P, PASSES * PACK], F32, "gain_sign")
+        late_sign = signs.tile([P, PACK - MIX_POOL], F32, name="late_sign", align_bytes=64, offset=0)
         nc.scalar.activation(out=gain_sign0[:], in_=gain_sb, func=ACT.Sign)
         nc.scalar.activation(out=gain_sign[:], in_=gain_sign0[:], func=ACT.Sign, scale=2.0, bias=1.0)
+        nc.scalar.activation(
+            out=late_sign[:], in_=gain_sign0[:, PACK : 2 * PACK - MIX_POOL], func=ACT.Sign, scale=2.0, bias=1.0
+        )
 
         v_words = [sb([P, S], U32, "v_words%d" % a) for a in range(PASSES)]
         nc.vector.tensor_copy(v_words[0][:], v_word_win0[:].bitcast(U32).indirect(idx[:]))
-        mix_raw = first_tab.tile([P, PASSES, PACK, N], F32, name="mix_raw", align_bytes=64, offset=0)
-        v2_plane = first_tab.tile([P, S2], U8, name="v2_plane", align_bytes=64, offset=4 * PASSES * PACK * N)
-        for a in range(PASSES):
-            nc.sync.dma_start(mix_raw[:, a, :, :], mix_view[a])
+        mix_raw = [first_tab.tile([P, PACK, N], F32, name="mix_raw0", align_bytes=64, offset=0)]
+        v2_plane = first_tab.tile([P, S2], U8, name="v2_plane", align_bytes=64, offset=4 * PACK * N)
+        nc.sync.dma_start(mix_raw[0][:], mix_view[0])
         nc.vector.memset(v2_plane[:].bitcast(I32), 0)
         for q in QUAD_ORDER:
             nc.sync.dma_start(
@@ -165,6 +169,8 @@ def tile_list_tutor_progress_matching_kernel(
         nc.vector.tensor_copy(v_words[1][:], v_word_win1[:].bitcast(U32).indirect(idx[:]))
         v2_word_win = later.tile([P, T2], I32, name="v2_word_win", align_bytes=64, offset=0)
         nc.sync.dma_start(v2_word_win[:], words_of(tab2_words, 0))
+        mix_raw.append(sb([P, PACK, N], F32, "mix_raw1", tag="v_word_win1"))
+        nc.sync.dma_start(mix_raw[1][:], mix_view[1])
         nc.scalar.copy(*wq_views(1, wq_raw1[:, :, 0 : PACK * WQ_SPLIT], 0, PACK // 2, PACK))
         nc.vector.tensor_copy(*wq_views(1, wq_raw1[:], 0, 0, PACK // 2))
         nc.vector.tensor_copy(*wq_views(1, wq_raw1[:, :, PACK * WQ_SPLIT : H], WQ_SPLIT, PACK // 2, PACK))
@@ -182,12 +188,11 @@ def tile_list_tutor_progress_matching_kernel(
             )
 
         h_first = sb([P, CHUNK, PACK], BF16, "h_first")
-        h_fifth = sb([P, BLOCK, PACK], BF16, "h_fifth")
-        h_last = later.tile([P, CHUNK - BLOCK, PACK], BF16, name="h_last", align_bytes=64, offset=0)
+        h_last = later.tile([P, CHUNK, PACK], BF16, name="h_last", align_bytes=64, offset=0)
         h_codes = [sb([P, CHUNK], U32, "h_codes%d" % c) for c in range(CHUNKS)]
         h_planes = [
             sb([P, CHUNK], U8, "h_planes0"),
-            later.tile([P, CHUNK], U8, name="h_planes1", align_bytes=64, offset=2 * (CHUNK - BLOCK) * PACK),
+            later.tile([P, CHUNK], U8, name="h_planes1", align_bytes=64, offset=2 * CHUNK * PACK),
         ]
         per_chunk = CHUNK // BLOCK
         h_accs = {}
@@ -208,9 +213,7 @@ def tile_list_tutor_progress_matching_kernel(
                     )
 
         def h_woven(c, lo, hi):
-            if c == 0:
-                return h_first[:, lo:hi, :]
-            return h_fifth[:] if lo == 0 else h_last[:, lo - BLOCK : hi - BLOCK, :]
+            return (h_first, h_last)[c][:, lo:hi, :]
 
         def h_empty(blocks):
             for b in blocks:
@@ -226,32 +229,25 @@ def tile_list_tutor_progress_matching_kernel(
             quantise(h_codes[c][:, lo:hi], h_planes[c][:, lo:hi], h_woven(c, lo, hi))
 
         mix_rows = [sb([P, PACK, N], BF16, "mix_rows%d" % a) for a in range(PASSES)]
-        mix_ahead = sb([P, MIX_AHEAD, PACK], BF16, "mix_ahead")
-        ahead_codes = sb([P, MIX_AHEAD], U32, "ahead_codes")
-        mix_codes = later.tile(
-            [P, PASSES * N - MIX_AHEAD], U32, name="mix_codes", align_bytes=64, offset=2 * (CHUNK + N) * PACK
-        )
+        mix_bf = [sb([P, N, PACK], BF16, "mix_bf%d" % a) for a in range(PASSES)]
+        mix_codes = later.tile([P, PASSES * N], U32, name="mix_codes", align_bytes=64, offset=(2 * PACK + 1) * CHUNK)
         mix_planes = sb([P, PASSES * N], U8, "mix_planes")
 
-        def mix_sign(a):
-            for t in range(PACK):
-                col = a * PACK + t
-                nc.scalar.activation(
-                    out=mix_rows[a][:, t, :], in_=mix_raw[:, a, t, :], func=ACT.Copy, scale=gain_sign[:, col : col + 1]
-                )
+        def mix_sign(a, t, sign):
+            nc.scalar.activation(out=mix_rows[a][:, t, :], in_=mix_raw[a][:, t, :], func=ACT.Copy, scale=sign)
 
-        mix_sign(0)
-        nc.scalar.copy(*weave_views(mix_ahead[:], mix_rows[0][:, :, 0:MIX_AHEAD]))
-        mix_sign(1)
+        for t in range(PACK):
+            mix_sign(0, t, gain_sign[:, t : t + 1])
+        nc.scalar.copy(*weave_views(mix_bf[0][:], mix_rows[0][:]))
+        for t in range(PACK - MIX_POOL):
+            mix_sign(1, t, late_sign[:, t : t + 1])
+        for t in range(PACK - MIX_POOL, PACK):
+            sign = gain_sign[:, PACK + t : PACK + t + 1]
+            nc.gpsimd.tensor_scalar(mix_rows[1][:, t, :], mix_raw[1][:, t, :], sign, 0.0, ALU.mult, ALU.add)
+        nc.gpsimd.tensor_scalar(mix_bf[1][:], mix_rows[1][:].rearrange("p t c -> p c t"), 1.0, 0.0, ALU.mult, ALU.add)
 
-        def mix_words(lo, hi):
-            return ahead_codes[:, lo:hi] if hi <= MIX_AHEAD else mix_codes[:, lo - MIX_AHEAD : hi - MIX_AHEAD]
-
-        def mix_quantise(lo, hi, woven):
-            quantise(mix_words(lo, hi), mix_planes[:, lo:hi], woven[:])
-
-        def pool_weave(woven, slices):
-            nc.gpsimd.tensor_scalar(woven, slices.rearrange("p t c -> p c t"), 1.0, 0.0, ALU.mult, ALU.add)
+        def mix_quantise(a):
+            quantise(mix_codes[:, a * N : (a + 1) * N], mix_planes[:, a * N : (a + 1) * N], mix_bf[a][:])
 
         v2_words = [sb([P, PASS], U32, "v2_words%d" % a) for a in range(PASSES)]
         list_cols = PASS // LIST_ROWS
@@ -262,7 +258,11 @@ def tile_list_tutor_progress_matching_kernel(
                 v2_word_win[:].bitcast(U32).indirect(idx2[:, a * list_cols : (a + 1) * list_cols]),
             )
 
-        z_rows = [[sb([P, PACK, CHUNK], BF16, "z_rows%d%d" % (c, a)) for a in range(PASSES)] for c in range(CHUNKS)]
+        z_first = signs.tile([P, PACK, CHUNK], BF16, name="z_first", align_bytes=64, offset=0)
+        z_rows = [
+            [z_first if c + a == 0 else sb([P, PACK, CHUNK], BF16, "z_rows%d%d" % (c, a)) for a in range(PASSES)]
+            for c in range(CHUNKS)
+        ]
         z_bf = [[sb([P, CHUNK, PACK], BF16, "z_bf%d%d" % (c, a)) for a in range(PASSES)] for c in range(CHUNKS)]
         z_codes = [
             [sb([P, CHUNK], U32, "z_codes%d%d" % (c, a), tag="v2_words0" if c + a == 0 else None) for a in range(PASSES)]
@@ -304,23 +304,19 @@ def tile_list_tutor_progress_matching_kernel(
 
         h_passes(0, range(per_chunk + 1))
         h_passes(1, range(per_chunk + 1))
-        h_empty((0, 1))
-        for b in range(2, per_chunk + 1):
+        h_empty((0,))
+        for b in range(1, per_chunk):
             h_empty((b,))
-            h_passes(0, (per_chunk + b - 1,))
-            h_passes(1, (per_chunk + b - 1,))
-        h_quantise(0, 0, CHUNK)
-        mix_quantise(0, MIX_AHEAD, mix_ahead)
-        mix_rest = sb([P, PASSES * N - MIX_AHEAD, PACK], BF16, "mix_rest", tag="mix_ahead")
-        pool_weave(mix_rest[:, 0 : N - MIX_AHEAD, :], mix_rows[0][:, :, MIX_AHEAD:N])
+            h_passes(0, (per_chunk + b,))
+            h_passes(1, (per_chunk + b,))
+        h_quantise(0, 0, CHUNK - BLOCK)
+        h_quantise(0, CHUNK - BLOCK, CHUNK)
         v2_gather(0)
         e_fills(0, 4)
         v2_gather(1)
-        pool_weave(mix_rest[:, N - MIX_AHEAD :, :], mix_rows[1][:])
-        h_empty(range(per_chunk + 1, 2 * per_chunk))
+        h_empty(range(per_chunk, 2 * per_chunk))
         e_fills(4, 8)
-        h_quantise(1, 0, BLOCK)
-        h_quantise(1, BLOCK, CHUNK - BLOCK)
+        h_quantise(1, 0, CHUNK - BLOCK)
         h_quantise(1, CHUNK - BLOCK, CHUNK)
         e_fills(8, 16)
 
@@ -350,7 +346,7 @@ def tile_list_tutor_progress_matching_kernel(
                     ns = slice(a * N + n * P, a * N + (n + 1) * P)
                     nc.tensor.matmul_mx(
                         acc[:, place, :],
-                        lhsT=mix_words(ns.start, ns.stop).bitcast(FP8X4),
+                        lhsT=mix_codes[:, ns].bitcast(FP8X4),
                         lhsT_scale=mix_planes[:, ns],
                         rhs=z_codes[c][a][:, lo:hi].bitcast(FP8X4),
                         rhs_scale=z_planes[c][a][:, lo:hi],
@@ -367,13 +363,14 @@ def tile_list_tutor_progress_matching_kernel(
                 nc.scalar.activation(out=res[:], in_=acc[:], func=ACT.Tanh)
                 nc.sync.dma_start(out_view[:, tiles[0] : tiles[-1] + 1, c * CHUNK + lo : c * CHUNK + hi], res[:])
 
-        first = y_open(0, 0, CHUNK, ((2, (0,)), (3, (1,)), (4, (2,))))
-        second = y_open(1, 0, HALF, ((1, (0, 1)), (7, (2,))))
+        first = y_open(0, 0, CHUNK, ((4, (0,)), (1, (1,)), (2, (2,))))
+        second = y_open(1, 0, HALF, ((3, (0, 1)), (7, (2,))))
         z_weave(0, 0, 0, CHUNK)
-        mix_quantise(MIX_AHEAD, PASSES * N, mix_rest)
+        mix_quantise(0)
         z_quantise(0, 0, 0, CHUNK)
         y_mix(first, 0)
         z_weave(0, 1, 0, CHUNK)
+        mix_quantise(1)
         z_quantise(0, 1, 0, CHUNK)
         y_mix(first, 1)
         y_out(first)

@@ -33,7 +33,8 @@ BLOCK = 128
 MIX_POOL = 2
 WQ_SPLIT = 104
 E_TURNS = (0, 5, 6, 7) * 3 + (0, 5, 6, 0)
-H_BANKS = (0, 1, 2, 3, 4, 1, 2, 3)
+H_BANKS = (0, 1, 2, 3, 4, 1, 3, 2)
+MIX_REST = 128
 
 
 def tile_list_tutor_progress_matching_kernel(
@@ -229,25 +230,18 @@ def tile_list_tutor_progress_matching_kernel(
             quantise(h_codes[c][:, lo:hi], h_planes[c][:, lo:hi], h_woven(c, lo, hi))
 
         mix_rows = [sb([P, PACK, N], BF16, "mix_rows%d" % a) for a in range(PASSES)]
-        mix_bf = [sb([P, N, PACK], BF16, "mix_bf%d" % a) for a in range(PASSES)]
+        mix_head = sb([P, N - MIX_REST, PACK], BF16, "mix_head")
         mix_codes = later.tile([P, PASSES * N], U32, name="mix_codes", align_bytes=64, offset=(2 * PACK + 1) * CHUNK)
         mix_planes = sb([P, PASSES * N], U8, "mix_planes")
 
         def mix_sign(a, t, sign):
             nc.scalar.activation(out=mix_rows[a][:, t, :], in_=mix_raw[a][:, t, :], func=ACT.Copy, scale=sign)
 
-        for t in range(PACK):
-            mix_sign(0, t, gain_sign[:, t : t + 1])
-        nc.scalar.copy(*weave_views(mix_bf[0][:], mix_rows[0][:]))
-        for t in range(PACK - MIX_POOL):
-            mix_sign(1, t, late_sign[:, t : t + 1])
-        for t in range(PACK - MIX_POOL, PACK):
-            sign = gain_sign[:, PACK + t : PACK + t + 1]
-            nc.gpsimd.tensor_scalar(mix_rows[1][:, t, :], mix_raw[1][:, t, :], sign, 0.0, ALU.mult, ALU.add)
-        nc.gpsimd.tensor_scalar(mix_bf[1][:], mix_rows[1][:].rearrange("p t c -> p c t"), 1.0, 0.0, ALU.mult, ALU.add)
+        def pool_weave(woven, slices):
+            nc.gpsimd.tensor_scalar(woven, slices.rearrange("p t c -> p c t"), 1.0, 0.0, ALU.mult, ALU.add)
 
-        def mix_quantise(a):
-            quantise(mix_codes[:, a * N : (a + 1) * N], mix_planes[:, a * N : (a + 1) * N], mix_bf[a][:])
+        def mix_quantise(lo, hi, woven):
+            quantise(mix_codes[:, lo:hi], mix_planes[:, lo:hi], woven[:])
 
         v2_words = [sb([P, PASS], U32, "v2_words%d" % a) for a in range(PASSES)]
         list_cols = PASS // LIST_ROWS
@@ -303,14 +297,28 @@ def tile_list_tutor_progress_matching_kernel(
             quantise(z_codes[c][a][:, lo:hi], z_planes[c][a][:, lo:hi], z_bf[c][a][:, lo:hi, :])
 
         h_passes(0, range(per_chunk + 1))
-        h_passes(1, range(per_chunk + 1))
-        h_empty((0,))
-        for b in range(1, per_chunk):
-            h_empty((b,))
-            h_passes(0, (per_chunk + b,))
-            h_passes(1, (per_chunk + b,))
+        h_passes(1, (0, 3, 1, 2, 4))
+        h_rows = sb([P, PACK, BLOCK], BF16, "h_rows")
+        for t in range(PACK):
+            nc.scalar.activation(out=h_rows[:, t, :], in_=h_accs[3][:, t, :], func=ACT.Identity, bias=bq_sb[:, t : t + 1])
+        h_empty((0, 1, 2))
+        for b in range(per_chunk + 1, 2 * per_chunk):
+            h_passes(0, (b,))
+            h_passes(1, (b,))
+        weave(h_woven(0, CHUNK - BLOCK, CHUNK), h_rows[:])
         h_quantise(0, 0, CHUNK - BLOCK)
         h_quantise(0, CHUNK - BLOCK, CHUNK)
+        for t in range(PACK):
+            mix_sign(0, t, gain_sign[:, t : t + 1])
+        nc.scalar.copy(*weave_views(mix_head[:], mix_rows[0][:, :, 0 : N - MIX_REST]))
+        for t in range(PACK - MIX_POOL):
+            mix_sign(1, t, late_sign[:, t : t + 1])
+        mix_rest = sb([P, N + MIX_REST, PACK], BF16, "mix_rest", tag="h_first")
+        pool_weave(mix_rest[:, 0:MIX_REST, :], mix_rows[0][:, :, N - MIX_REST : N])
+        for t in range(PACK - MIX_POOL, PACK):
+            sign = gain_sign[:, PACK + t : PACK + t + 1]
+            nc.gpsimd.tensor_scalar(mix_rows[1][:, t, :], mix_raw[1][:, t, :], sign, 0.0, ALU.mult, ALU.add)
+        pool_weave(mix_rest[:, MIX_REST:, :], mix_rows[1][:])
         v2_gather(0)
         e_fills(0, 4)
         v2_gather(1)
@@ -363,14 +371,14 @@ def tile_list_tutor_progress_matching_kernel(
                 nc.scalar.activation(out=res[:], in_=acc[:], func=ACT.Tanh)
                 nc.sync.dma_start(out_view[:, tiles[0] : tiles[-1] + 1, c * CHUNK + lo : c * CHUNK + hi], res[:])
 
-        first = y_open(0, 0, CHUNK, ((4, (0,)), (1, (1,)), (2, (2,))))
-        second = y_open(1, 0, HALF, ((3, (0, 1)), (7, (2,))))
+        first = y_open(0, 0, CHUNK, ((4, (0,)), (1, (1,)), (3, (2,))))
+        second = y_open(1, 0, HALF, ((2, (0, 1)), (7, (2,))))
         z_weave(0, 0, 0, CHUNK)
-        mix_quantise(0)
+        mix_quantise(0, N - MIX_REST, mix_head)
+        mix_quantise(N - MIX_REST, PASSES * N, mix_rest)
         z_quantise(0, 0, 0, CHUNK)
         y_mix(first, 0)
         z_weave(0, 1, 0, CHUNK)
-        mix_quantise(1)
         z_quantise(0, 1, 0, CHUNK)
         y_mix(first, 1)
         y_out(first)

@@ -32,9 +32,9 @@ HALF = CHUNK // 2
 BLOCK = 128
 MIX_POOL = 2
 WQ_SPLIT = 104
-E_TURNS = (0, 5, 6, 7) * 3 + (0, 5, 6, 0)
+E_TURNS = (0, 5, 6, 7) * 4
 H_BANKS = (0, 1, 2, 3, 4, 1, 3, 2)
-MIX_REST = 128
+MIX_FIRST = 1
 
 
 def tile_list_tutor_progress_matching_kernel(
@@ -229,8 +229,8 @@ def tile_list_tutor_progress_matching_kernel(
         def h_quantise(c, lo, hi):
             quantise(h_codes[c][:, lo:hi], h_planes[c][:, lo:hi], h_woven(c, lo, hi))
 
-        mix_rows = [sb([P, PACK, N], BF16, "mix_rows%d" % a) for a in range(PASSES)]
-        mix_head = sb([P, N - MIX_REST, PACK], BF16, "mix_head")
+        mix_rows = [sb([P, PACK, N], BF16, "mix_rows0", tag="wq_bf1"), sb([P, PACK, N], BF16, "mix_rows1")]
+        mix_bf = [sb([P, N, PACK], BF16, "mix_bf%d" % a) for a in range(PASSES)]
         mix_codes = later.tile([P, PASSES * N], U32, name="mix_codes", align_bytes=64, offset=(2 * PACK + 1) * CHUNK)
         mix_planes = sb([P, PASSES * N], U8, "mix_planes")
 
@@ -240,8 +240,12 @@ def tile_list_tutor_progress_matching_kernel(
         def pool_weave(woven, slices):
             nc.gpsimd.tensor_scalar(woven, slices.rearrange("p t c -> p c t"), 1.0, 0.0, ALU.mult, ALU.add)
 
-        def mix_quantise(lo, hi, woven):
-            quantise(mix_codes[:, lo:hi], mix_planes[:, lo:hi], woven[:])
+        def pool_sign(a, t):
+            sign = gain_sign[:, a * PACK + t : a * PACK + t + 1]
+            nc.gpsimd.tensor_scalar(mix_rows[a][:, t, :], mix_raw[a][:, t, :], sign, 0.0, ALU.mult, ALU.add)
+
+        def mix_quantise(a):
+            quantise(mix_codes[:, a * N : (a + 1) * N], mix_planes[:, a * N : (a + 1) * N], mix_bf[a][:])
 
         v2_words = [sb([P, PASS], U32, "v2_words%d" % a) for a in range(PASSES)]
         list_cols = PASS // LIST_ROWS
@@ -298,33 +302,36 @@ def tile_list_tutor_progress_matching_kernel(
 
         h_passes(0, range(per_chunk + 1))
         h_passes(1, (0, 3, 1, 2, 4))
-        h_rows = sb([P, PACK, BLOCK], BF16, "h_rows")
-        for t in range(PACK):
-            nc.scalar.activation(out=h_rows[:, t, :], in_=h_accs[3][:, t, :], func=ACT.Identity, bias=bq_sb[:, t : t + 1])
+        h_rows = {b: sb([P, PACK, BLOCK], BF16, "h_rows%d" % b) for b in (3, 4)}
+        for t in range(MIX_FIRST):
+            mix_sign(0, t, gain_sign[:, t : t + 1])
+        for t in range(MIX_FIRST, PACK):
+            pool_sign(0, t)
+        for b, rows in h_rows.items():
+            for t in range(PACK):
+                nc.scalar.activation(out=rows[:, t, :], in_=h_accs[b][:, t, :], func=ACT.Identity, bias=bq_sb[:, t : t + 1])
         h_empty((0, 1, 2))
         for b in range(per_chunk + 1, 2 * per_chunk):
             h_passes(0, (b,))
             h_passes(1, (b,))
-        weave(h_woven(0, CHUNK - BLOCK, CHUNK), h_rows[:])
+        weave(h_woven(0, CHUNK - BLOCK, CHUNK), h_rows[3][:])
         h_quantise(0, 0, CHUNK - BLOCK)
         h_quantise(0, CHUNK - BLOCK, CHUNK)
-        for t in range(PACK):
-            mix_sign(0, t, gain_sign[:, t : t + 1])
-        nc.scalar.copy(*weave_views(mix_head[:], mix_rows[0][:, :, 0 : N - MIX_REST]))
+        nc.scalar.copy(*weave_views(mix_bf[0][:], mix_rows[0][:]))
         for t in range(PACK - MIX_POOL):
             mix_sign(1, t, late_sign[:, t : t + 1])
-        mix_rest = sb([P, N + MIX_REST, PACK], BF16, "mix_rest", tag="h_first")
-        pool_weave(mix_rest[:, 0:MIX_REST, :], mix_rows[0][:, :, N - MIX_REST : N])
+        h_fifth = sb([P, BLOCK, PACK], BF16, "h_fifth", tag="h_first")
+        pool_weave(h_fifth[:], h_rows[4][:])
         for t in range(PACK - MIX_POOL, PACK):
-            sign = gain_sign[:, PACK + t : PACK + t + 1]
-            nc.gpsimd.tensor_scalar(mix_rows[1][:, t, :], mix_raw[1][:, t, :], sign, 0.0, ALU.mult, ALU.add)
-        pool_weave(mix_rest[:, MIX_REST:, :], mix_rows[1][:])
+            pool_sign(1, t)
+        pool_weave(mix_bf[1][:], mix_rows[1][:])
         v2_gather(0)
         e_fills(0, 4)
         v2_gather(1)
-        h_empty(range(per_chunk, 2 * per_chunk))
+        h_empty(range(per_chunk + 1, 2 * per_chunk))
         e_fills(4, 8)
-        h_quantise(1, 0, CHUNK - BLOCK)
+        quantise(h_codes[1][:, 0:BLOCK], h_planes[1][:, 0:BLOCK], h_fifth[:])
+        h_quantise(1, BLOCK, CHUNK - BLOCK)
         h_quantise(1, CHUNK - BLOCK, CHUNK)
         e_fills(8, 16)
 
@@ -372,10 +379,10 @@ def tile_list_tutor_progress_matching_kernel(
                 nc.sync.dma_start(out_view[:, tiles[0] : tiles[-1] + 1, c * CHUNK + lo : c * CHUNK + hi], res[:])
 
         first = y_open(0, 0, CHUNK, ((4, (0,)), (1, (1,)), (3, (2,))))
-        second = y_open(1, 0, HALF, ((2, (0, 1)), (7, (2,))))
+        second = y_open(1, 0, HALF, ((2, (0, 1)), (6, (2,))))
         z_weave(0, 0, 0, CHUNK)
-        mix_quantise(0, N - MIX_REST, mix_head)
-        mix_quantise(N - MIX_REST, PASSES * N, mix_rest)
+        mix_quantise(0)
+        mix_quantise(1)
         z_quantise(0, 0, 0, CHUNK)
         y_mix(first, 0)
         z_weave(0, 1, 0, CHUNK)
@@ -384,7 +391,7 @@ def tile_list_tutor_progress_matching_kernel(
         y_out(first)
         ends = ((HALF, HALF + BLOCK), (HALF + BLOCK, CHUNK))
         tiles = tuple(range(N // P))
-        lasts = [y_open(1, lo, hi, ((number, tiles),)) for (lo, hi), number in zip(ends, (5, 6))]
+        lasts = [y_open(1, lo, hi, ((number, tiles),)) for (lo, hi), number in zip(ends, (0, 5))]
         z_weave(1, 0, 0, HALF)
         z_weave(1, 1, 0, HALF)
         z_quantise(1, 0, 0, HALF)

from contextlib import ExitStack

import concourse.mybir as mybir
from concourse.masks import make_identity

K, H, N, T, S, T2, S2 = 1024, 512, 384, 4096, 1024, 2048, 1024
FLOPS = 2 * S * (K * H + H * S2 + S2 * N + K * N)

F32 = mybir.dt.float32
BF16 = mybir.dt.bfloat16
I32 = mybir.dt.int32
U32 = mybir.dt.uint32
U16 = mybir.dt.uint16
U8 = mybir.dt.uint8
FP8X4 = mybir.dt.float8_e4m3fn_x4
FP4X4 = mybir.dt.float4_e2m1fn_x4
ALU = mybir.AluOpType
ACT = mybir.ActivationFunctionType

P = 128
PACK = 4
PASSES = 2
PASS = P * PACK
QUADS = 4
QUAD = P // QUADS
QUAD_ORDER = (0, 2, 1, 3)
V2_ROW = 8
LIST_ROWS = 16
CHUNK = 512
CHUNKS = S // CHUNK
HALF = CHUNK // 2
BLOCK = 128
MIX_POOL = 2
WQ_SPLIT = 104
E_TURNS = (0, 5, 6, 7) * 4
H_BANKS = (0, 1, 2, 3, 4, 1, 3, 2)
MIX_FIRST = 1


def tile_list_tutor_progress_matching_kernel(
    tc, tab_words, tab_scales, offs, tab2_words, tab2_scales, offs2, wq, bq, gain, mix, wd_words, wd_scales, out
):
    nc = tc.nc
    with ExitStack() as ctx:
        held = ctx.enter_context(tc.tile_pool(name="held", bufs=1))
        first_tab = ctx.enter_context(tc.tile_pool(name="first_tab", bufs=1))
        later = ctx.enter_context(tc.tile_pool(name="later", bufs=1))
        second_wq = ctx.enter_context(tc.tile_pool(name="second_wq", bufs=1))
        signs = ctx.enter_context(tc.tile_pool(name="signs", bufs=1))
        psum = ctx.enter_context(tc.psum_pool(name="psum", bufs=1))

        def sb(shape, dtype, name, tag=None):
            return held.tile(shape, dtype, name=name, tag=tag or name, align_bytes=64)

        def bank(number, shape):
            return psum.tile(shape, F32, name="bank%d" % number, tag="bank%d" % number)

        def words_of(table, a):
            return table[a].rearrange("p t i -> p (t i)").bitcast(I32)

        def quantise(codes, plane, woven):
            nc.vector.quantize_mx(codes.bitcast(FP8X4), plane, woven.rearrange("p c t -> p (c t)"))

        def weave(woven, slices):
            nc.vector.tensor_copy(woven, slices.rearrange("p t c -> p c t"))

        def weave_views(woven, slices):
            return (
                woven.rearrange("p (c i) t -> p c t i", i=4),
                slices.rearrange("p t (c i) -> p c t i", i=4),
            )

        idx = held.tile([P, S // LIST_ROWS], U16, name="idx")
        idx2 = held.tile([P, S2 // LIST_ROWS], U16, name="idx2")
        v_scale_win = second_wq.tile([P, T], U8, name="v_scale_win", align_bytes=64, offset=0)
        v2_scale_win = sb([P, T2], U8, "v2_scale_win")
        v_word_win0 = first_tab.tile([P, T], I32, name="v_word_win0", align_bytes=64, offset=0)
        v_word_win1 = sb([P, T], I32, "v_word_win1")
        wq_raw0 = sb([P, PACK, H], F32, "wq_raw0")
        v_planes = sb([P, PASSES, S], U8, "v_planes")

        nc.vector.memset(v_scale_win[:].bitcast(I32), 0)
        nc.vector.memset(v2_scale_win[:].bitcast(I32), 0)
        nc.vector.memset(v_planes[:].bitcast(I32), 0)

        wq_view = wq.rearrange("(a p i) r -> a p i r", a=PASSES, i=PACK)
        mix_view = mix.rearrange("(a p i) n -> a p i n", a=PASSES, i=PACK)

        nc.sync.dma_start(wq_raw0[:], wq_view[0])
        nc.sync.dma_start(idx[:], offs)
        nc.sync.dma_start(idx2[:], offs2)
        nc.sync.dma_start(v_scale_win[0:P:4, :].bitcast(I32), tab_scales.rearrange("a q x -> q a x").bitcast(I32))
        nc.sync.dma_start(v2_scale_win[0:P:8, :].bitcast(I32), tab2_scales[0].bitcast(I32))
        nc.sync.dma_start(v_word_win0[:], words_of(tab_words, 0))
        vec_rows = sb([P, PACK * P], F32, "vec_rows")
        identity = sb([P, P], F32, "identity")
        nc.gpsimd.memset(vec_rows[:], 0.0)
        make_identity(nc, identity[:])
        nc.sync.dma_start(vec_rows[0:PASSES, :], gain.rearrange("(a x) -> a x", a=PASSES))
        nc.sync.dma_start(vec_rows[PASSES : PASSES + 1, :], bq.unsqueeze(0))
        nc.sync.dma_start(v_word_win1[:], words_of(tab_words, 1))

        v_scale_rows = later.tile([P, S], U8, name="v_scale_rows", align_bytes=64, offset=0)
        nc.vector.tensor_copy(v_scale_rows[:], v_scale_win[:].indirect(idx[:]))
        for q in QUAD_ORDER:
            nc.sync.dma_start(
                v_planes[QUAD * q : QUAD * q + 4, :, :].bitcast(I32),
                v_scale_rows[QUAD * q : QUAD * (q + 1) : 4, :].bitcast(I32),
            )
        wq_raw1 = second_wq.tile([P, PACK, H], F32, name="wq_raw1", align_bytes=64, offset=0)
        nc.sync.dma_start(wq_raw1[:], wq_view[1])

        v2_scale_rows = sb([P, S2], U8, "v2_scale_rows")
        nc.vector.tensor_copy(
            v2_scale_rows[:].rearrange("p (a i s) -> p a s i", a=PASSES, i=PACK), v2_scale_win[:].indirect(idx2[:])
        )


        turned = bank(0, [P, PACK, P])
        for t in range(PACK):
            nc.tensor.transpose(turned[:, t, :], vec_rows[:, t : PACK * P : PACK], identity[:])
        vec_cols = sb([P, PASSES + 1, PACK], F32, "vec_cols")
        nc.scalar.copy(vec_cols[:], turned[:, :, 0 : PASSES + 1].rearrange("p t w -> p w t"))
        gain_sb = vec_cols[:, 0:PASSES, :].rearrange("p a t -> p (a t)")
        bq_sb = vec_cols[:, PASSES, :]

        gain_sign0 = sb([P, PASSES * PACK], F32, "gain_sign0")
        gain_sign = sb([P, PASSES * PACK], F32, "gain_sign")
        late_sign = signs.tile([P, PACK - MIX_POOL], F32, name="late_sign", align_bytes=64, offset=0)
        nc.scalar.activation(out=gain_sign0[:], in_=gain_sb, func=ACT.Sign)
        nc.scalar.activation(out=gain_sign[:], in_=gain_sign0[:], func=ACT.Sign, scale=2.0, bias=1.0)
        nc.scalar.activation(
            out=late_sign[:], in_=gain_sign0[:, PACK : 2 * PACK - MIX_POOL], func=ACT.Sign, scale=2.0, bias=1.0
        )

        v_words = [sb([P, S], U32, "v_words%d" % a) for a in range(PASSES)]
        nc.vector.tensor_copy(v_words[0][:], v_word_win0[:].bitcast(U32).indirect(idx[:]))
        mix_raw = [first_tab.tile([P, PACK, N], F32, name="mix_raw0", align_bytes=64, offset=0)]
        v2_plane = first_tab.tile([P, S2], U8, name="v2_plane", align_bytes=64, offset=4 * PACK * N)
        nc.sync.dma_start(mix_raw[0][:], mix_view[0])
        nc.vector.memset(v2_plane[:].bitcast(I32), 0)
        for q in QUAD_ORDER:
            nc.sync.dma_start(
                v2_plane[QUAD * q + V2_ROW : QUAD * q + V2_ROW + 4, :].bitcast(I32),
                v2_scale_rows[QUAD * q : QUAD * (q + 1) : 8, :].bitcast(I32),
            )

        wq_bf = [
            sb([P, PACK, P, PACK], BF16, "wq_bf0"),
            sb([P, PACK, P, PACK], BF16, "wq_bf1"),
        ]
        wq_codes = sb([P, PASSES, H], U32, "wq_codes")
        wq_planes = sb([P, PASSES, H], U8, "wq_planes")

        def wq_views(a, raw, s0, t0=0, t1=PACK):
            count = raw.shape[2] // PACK
            return (
                wq_bf[a][:, t0:t1, s0 : s0 + count, :].rearrange("p t s i -> p s i t"),
                raw.rearrange("p i (s t) -> p s i t", t=PACK)[:, :, :, t0:t1],
            )

        def wq_quantise(a, t0, t1):
            cols = slice(t0 * P, t1 * P)
            woven = wq_bf[a][:, t0:t1, :, :].rearrange("p t s i -> p (t s) i")
            quantise(wq_codes[:, a, cols], wq_planes[:, a, cols], woven)

        nc.scalar.copy(*wq_views(0, wq_raw0[:], 0))
        wq_quantise(0, 0, PACK)

        nc.vector.tensor_copy(v_words[1][:], v_word_win1[:].bitcast(U32).indirect(idx[:]))
        v2_word_win = later.tile([P, T2], I32, name="v2_word_win", align_bytes=64, offset=0)
        nc.sync.dma_start(v2_word_win[:], words_of(tab2_words, 0))
        mix_raw.append(sb([P, PACK, N], F32, "mix_raw1", tag="v_word_win1"))
        nc.sync.dma_start(mix_raw[1][:], mix_view[1])
        nc.scalar.copy(*wq_views(1, wq_raw1[:, :, 0 : PACK * WQ_SPLIT], 0, PACK // 2, PACK))
        nc.vector.tensor_copy(*wq_views(1, wq_raw1[:], 0, 0, PACK // 2))
        nc.vector.tensor_copy(*wq_views(1, wq_raw1[:, :, PACK * WQ_SPLIT : H], WQ_SPLIT, PACK // 2, PACK))
        wq_quantise(1, 0, PACK // 2)
        wq_quantise(1, PACK // 2, PACK)

        wd_planes = second_wq.tile([P, PASSES, N], U8, name="wd_planes", align_bytes=64, offset=0)
        wd_codes = second_wq.tile([P, PASSES, 2 * N], U8, name="wd_codes", align_bytes=64, offset=PASSES * N)
        nc.vector.memset(wd_planes[:].bitcast(I32), 0)
        nc.sync.dma_start(wd_codes[:].bitcast(I32), wd_words.rearrange("a p c -> p a c").bitcast(I32))
        for q in QUAD_ORDER:
            nc.sync.dma_start(
                wd_planes[QUAD * q : QUAD * q + 4, :, :].bitcast(I32),
                wd_scales[:, 4 * q : 4 * q + 4, :].rearrange("a r c -> r a c").bitcast(I32),
            )

        h_first = sb([P, CHUNK, PACK], BF16, "h_first")
        h_last = later.tile([P, CHUNK, PACK], BF16, name="h_last", align_bytes=64, offset=0)
        h_codes = [sb([P, CHUNK], U32, "h_codes%d" % c) for c in range(CHUNKS)]
        h_planes = [
            sb([P, CHUNK], U8, "h_planes0"),
            later.tile([P, CHUNK], U8, name="h_planes1", align_bytes=64, offset=2 * CHUNK * PACK),
        ]
        per_chunk = CHUNK // BLOCK
        h_accs = {}

        def h_passes(a, blocks):
            for b in blocks:
                if a == 0:
                    h_accs[b] = bank(H_BANKS[b], [P, PACK, BLOCK])
                for t in range(PACK):
                    nc.tensor.matmul_mx(
                        h_accs[b][:, t, :],
                        lhsT=wq_codes[:, a, t * P : (t + 1) * P].bitcast(FP8X4),
                        lhsT_scale=wq_planes[:, a, t * P : (t + 1) * P],
                        rhs=v_words[a][:, b * BLOCK : (b + 1) * BLOCK].bitcast(FP8X4),
                        rhs_scale=v_planes[:, a, b * BLOCK : (b + 1) * BLOCK],
                        start=(a == 0 and t == 0),
                        stop=(a == PASSES - 1 and t == PACK - 1),
                    )

        def h_woven(c, lo, hi):
            return (h_first, h_last)[c][:, lo:hi, :]

        def h_empty(blocks):
            for b in blocks:
                c, lo = b // per_chunk, (b % per_chunk) * BLOCK
                nc.vector.tensor_tensor(
                    h_woven(c, lo, lo + BLOCK).rearrange("p (j i) t -> p j t i", i=2),
                    h_accs[b][:].rearrange("p t (j i) -> p j t i", i=2),
                    bq_sb.unsqueeze(1).unsqueeze(3).to_broadcast([P, BLOCK // 2, PACK, 2]),
                    ALU.add,
                )

        def h_quantise(c, lo, hi):
            quantise(h_codes[c][:, lo:hi], h_planes[c][:, lo:hi], h_woven(c, lo, hi))

        mix_rows = [sb([P, PACK, N], BF16, "mix_rows0", tag="wq_bf1"), sb([P, PACK, N], BF16, "mix_rows1")]
        mix_bf = [sb([P, N, PACK], BF16, "mix_bf%d" % a) for a in range(PASSES)]
        mix_codes = later.tile([P, PASSES * N], U32, name="mix_codes", align_bytes=64, offset=(2 * PACK + 1) * CHUNK)
        mix_planes = sb([P, PASSES * N], U8, "mix_planes")

        def mix_sign(a, t, sign):
            nc.scalar.activation(out=mix_rows[a][:, t, :], in_=mix_raw[a][:, t, :], func=ACT.Copy, scale=sign)

        def pool_weave(woven, slices):
            nc.gpsimd.tensor_scalar(woven, slices.rearrange("p t c -> p c t"), 1.0, 0.0, ALU.mult, ALU.add)

        def pool_sign(a, t):
            sign = gain_sign[:, a * PACK + t : a * PACK + t + 1]
            nc.gpsimd.tensor_scalar(mix_rows[a][:, t, :], mix_raw[a][:, t, :], sign, 0.0, ALU.mult, ALU.add)

        def mix_quantise(a):
            quantise(mix_codes[:, a * N : (a + 1) * N], mix_planes[:, a * N : (a + 1) * N], mix_bf[a][:])

        v2_words = [sb([P, PASS], U32, "v2_words%d" % a) for a in range(PASSES)]
        list_cols = PASS // LIST_ROWS

        def v2_gather(a):
            nc.vector.tensor_copy(
                v2_words[a][:].rearrange("p (i s) -> p s i", i=PACK),
                v2_word_win[:].bitcast(U32).indirect(idx2[:, a * list_cols : (a + 1) * list_cols]),
            )

        z_first = signs.tile([P, PACK, CHUNK], BF16, name="z_first", align_bytes=64, offset=0)
        z_rows = [
            [z_first if c + a == 0 else sb([P, PACK, CHUNK], BF16, "z_rows%d%d" % (c, a)) for a in range(PASSES)]
            for c in range(CHUNKS)
        ]
        z_bf = [[sb([P, CHUNK, PACK], BF16, "z_bf%d%d" % (c, a)) for a in range(PASSES)] for c in range(CHUNKS)]
        z_codes = [
            [sb([P, CHUNK], U32, "z_codes%d%d" % (c, a), tag="v2_words0" if c + a == 0 else None) for a in range(PASSES)]
            for c in range(CHUNKS)
        ]
        z_planes = [[sb([P, CHUNK], U8, "z_planes%d%d" % (c, a)) for a in range(PASSES)] for c in range(CHUNKS)]

        def e_bank(number, c, a, slices, lo, hi):
            acc = bank(number, [P, len(slices), hi - lo])
            for place, t in enumerate(slices):
                col = a * PACK + t
                nc.tensor.matmul_mx(
                    acc[:, place, :],
                    lhsT=v2_words[a][:, t * P : (t + 1) * P].bitcast(FP8X4),
                    lhsT_scale=v2_plane[V2_ROW:P, col * P : (col + 1) * P],
                    rhs=h_codes[c][:, lo:hi].bitcast(FP8X4),
                    rhs_scale=h_planes[c][:, lo:hi],
                    start=True,
                    stop=True,
                )
            for place, t in enumerate(slices):
                col = a * PACK + t
                nc.scalar.activation(
                    out=z_rows[c][a][:, t, lo:hi], in_=acc[:, place, :], func=ACT.Abs, scale=gain_sb[:, col : col + 1]
                )

        fills = [(c, a, (t,), 0, CHUNK) for c, a in ((0, 0), (0, 1), (1, 0)) for t in range(PACK)]
        fills.extend((1, 1, pair, lo, lo + HALF) for lo in (0, HALF) for pair in ((0, 1), (2, 3)))

        def e_fills(first, last):
            for turn in range(first, last):
                e_bank(E_TURNS[turn], *fills[turn])

        def z_weave(c, a, lo, hi):
            weave(z_bf[c][a][:, lo:hi, :], z_rows[c][a][:, :, lo:hi])

        def z_quantise(c, a, lo, hi):
            quantise(z_codes[c][a][:, lo:hi], z_planes[c][a][:, lo:hi], z_bf[c][a][:, lo:hi, :])

        h_passes(0, range(per_chunk + 1))
        h_passes(1, (0, 3, 1, 2, 4))
        h_rows = {b: sb([P, PACK, BLOCK], BF16, "h_rows%d" % b) for b in (3, 4)}
        for t in range(MIX_FIRST):
            mix_sign(0, t, gain_sign[:, t : t + 1])
        for t in range(MIX_FIRST, PACK):
            pool_sign(0, t)
        for b, rows in h_rows.items():
            for t in range(PACK):
                nc.scalar.activation(out=rows[:, t, :], in_=h_accs[b][:, t, :], func=ACT.Identity, bias=bq_sb[:, t : t + 1])
        h_empty((0, 1, 2))
        for b in range(per_chunk + 1, 2 * per_chunk):
            h_passes(0, (b,))
            h_passes(1, (b,))
        weave(h_woven(0, CHUNK - BLOCK, CHUNK), h_rows[3][:])
        h_quantise(0, 0, CHUNK - BLOCK)
        h_quantise(0, CHUNK - BLOCK, CHUNK)
        nc.scalar.copy(*weave_views(mix_bf[0][:], mix_rows[0][:]))
        for t in range(PACK - MIX_POOL):
            mix_sign(1, t, late_sign[:, t : t + 1])
        h_fifth = sb([P, BLOCK, PACK], BF16, "h_fifth", tag="h_first")
        pool_weave(h_fifth[:], h_rows[4][:])
        for t in range(PACK - MIX_POOL, PACK):
            pool_sign(1, t)
        pool_weave(mix_bf[1][:], mix_rows[1][:])
        v2_gather(0)
        e_fills(0, 4)
        v2_gather(1)
        h_empty(range(per_chunk + 1, 2 * per_chunk))
        e_fills(4, 8)
        quantise(h_codes[1][:, 0:BLOCK], h_planes[1][:, 0:BLOCK], h_fifth[:])
        h_quantise(1, BLOCK, CHUNK - BLOCK)
        h_quantise(1, CHUNK - BLOCK, CHUNK)
        e_fills(8, 16)

        def y_open(c, lo, hi, groups):
            js = slice(c * CHUNK + lo, c * CHUNK + hi)
            accs = []
            for number, tiles in groups:
                acc = bank(number, [P, len(tiles), hi - lo])
                for place, n in enumerate(tiles):
                    for a in range(PASSES):
                        nc.tensor.matmul_mx(
                            acc[:, place, :],
                            lhsT=wd_codes[:, a, 2 * n * P : 2 * (n + 1) * P].bitcast(FP4X4),
                            lhsT_scale=wd_planes[:, a, n * P : (n + 1) * P],
                            rhs=v_words[a][:, js].bitcast(FP8X4),
                            rhs_scale=v_planes[:, a, js],
                            start=(place == 0 and a == 0),
                            stop=False,
                        )
                accs.append((acc, tiles))
            return c, lo, hi, accs

        def y_mix(piece, a):
            c, lo, hi, accs = piece
            for acc, tiles in accs:
                for place, n in enumerate(tiles):
                    ns = slice(a * N + n * P, a * N + (n + 1) * P)
                    nc.tensor.matmul_mx(
                        acc[:, place, :],
                        lhsT=mix_codes[:, ns].bitcast(FP8X4),
                        lhsT_scale=mix_planes[:, ns],
                        rhs=z_codes[c][a][:, lo:hi].bitcast(FP8X4),
                        rhs_scale=z_planes[c][a][:, lo:hi],
                        start=False,
                        stop=(a == PASSES - 1 and place == len(tiles) - 1),
                    )

        out_view = out.rearrange("(n p) j -> p n j", p=P)

        def y_out(piece):
            c, lo, hi, accs = piece
            for acc, tiles in accs:
                res = sb([P, len(tiles), hi - lo], F32, "res%d_%d_%d" % (c, lo, tiles[0]))
                nc.scalar.activation(out=res[:], in_=acc[:], func=ACT.Tanh)
                nc.sync.dma_start(out_view[:, tiles[0] : tiles[-1] + 1, c * CHUNK + lo : c * CHUNK + hi], res[:])

        first = y_open(0, 0, CHUNK, ((4, (0,)), (1, (1,)), (3, (2,))))
        second = y_open(1, 0, HALF, ((2, (0, 1)), (6, (2,))))
        z_weave(0, 0, 0, CHUNK)
        mix_quantise(0)
        mix_quantise(1)
        z_quantise(0, 0, 0, CHUNK)
        y_mix(first, 0)
        z_weave(0, 1, 0, CHUNK)
        z_quantise(0, 1, 0, CHUNK)
        y_mix(first, 1)
        y_out(first)
        ends = ((HALF, HALF + BLOCK), (HALF + BLOCK, CHUNK))
        tiles = tuple(range(N // P))
        lasts = [y_open(1, lo, hi, ((number, tiles),)) for (lo, hi), number in zip(ends, (0, 5))]
        z_weave(1, 0, 0, HALF)
        z_weave(1, 1, 0, HALF)
        z_quantise(1, 0, 0, HALF)
        y_mix(second, 0)
        z_weave(1, 0, HALF, CHUNK)
        z_quantise(1, 1, 0, HALF)
        y_mix(second, 1)
        y_out(second)
        z_weave(1, 1, *ends[0])
        z_quantise(1, 0, HALF, CHUNK)
        for piece in lasts:
            y_mix(piece, 0)
        z_weave(1, 1, *ends[1])
        for part, piece in zip(ends, lasts):
            z_quantise(1, 1, *part)
            y_mix(piece, 1)
        res = sb([P, len(tiles), HALF], F32, "res_last")
        nc.scalar.activation(out=res[:, :, 0:BLOCK], in_=lasts[0][3][0][0][:], func=ACT.Tanh)
        for n in tiles:
            nc.scalar.activation(out=res[:, n, BLOCK:HALF], in_=lasts[1][3][0][0][:, n, :], func=ACT.Tanh)
            queue = nc.scalar if n == tiles[-1] else nc.sync
            queue.dma_start(out_view[:, n, CHUNK + HALF : S], res[:, n, :])
